import numpy as np
import ml_dtypes


def mxq(x, axis, fmt="e4m3"):
    dtype, down = {"e4m3": (ml_dtypes.float8_e4m3fn, 7), "e5m2": (ml_dtypes.float8_e5m2, 14)}[fmt]
    v = np.moveaxis(np.asarray(x, np.float32).astype(ml_dtypes.bfloat16).astype(np.float64), axis, -1)
    blocks = v.reshape(v.shape[:-1] + (-1, 32))
    amax = np.abs(blocks).max(-1, keepdims=True)
    byte = np.maximum(np.where(amax > 0, np.frexp(amax)[1] - 1 + 127, 0) - down, 1)
    scale = np.exp2(byte - 127.0)
    codes = (blocks / scale).astype(np.float32).astype(dtype).astype(np.float64)
    return np.moveaxis((codes * scale).reshape(v.shape), -1, axis)


WIDE = False


def mx_kscale(k):
    if not WIDE:
        return np.ones(k)
    levels = np.array([10, -10, 5, -5, 0])
    if k % 512:
        return np.exp2(np.random.permutation(np.resize(levels, k // 32))).repeat(32)
    a = np.empty((k // 512, 16))
    for p in range(k // 512):
        a[p, :8] = np.random.permutation(np.resize(levels, 8))
        for g in range(8):
            far = levels[np.abs(levels - a[p, g]) >= 10]
            a[p, g + 8] = far[np.random.randint(len(far))]
    return np.exp2(a.ravel()).repeat(32)


def f64(x):
    return np.asarray(x).astype(np.float64)


def striped(idx):
    return np.tile(idx.reshape(-1, 16).T, (8, 1)).astype(np.uint16)


def unstriped(offs):
    return offs[:16].T.reshape(-1).astype(np.int64)


E2M1 = np.array([0.0, 0.5, 1.0, 1.5, 2.0, 3.0, 4.0, 6.0, -0.0, -0.5, -1.0, -1.5, -2.0, -3.0, -4.0, -6.0])


def pack_weight(w, fmt):
    k, n = w.shape
    w = f64(np.asarray(w, np.float32).astype(ml_dtypes.bfloat16)).reshape(k // 32, 32, n)
    amax = np.abs(w).max(1)
    if fmt == "e4m3":
        byte = np.frexp(amax)[1] - 1 + 127 - 7
    else:
        mant, ex = np.frexp(amax / 6.0)
        byte = np.where(mant > 0.5, ex, ex - 1) + 127
    byte = np.clip(np.where(amax > 0, byte, 1), 1, 254)
    scaled = (w * np.exp2(127.0 - byte)[:, None, :]).reshape(k, n).astype(np.float32)
    by_word = np.ascontiguousarray(scaled.reshape(k // 512, 128, 4, n).transpose(0, 1, 3, 2))
    if fmt == "e4m3":
        words = by_word.astype(ml_dtypes.float8_e4m3fn).view(np.uint8)
    else:
        c = by_word.astype(ml_dtypes.float4_e2m1fn).view(np.uint8) & 0xF
        words = (c[..., 0::2] | (c[..., 1::2] << 4)).reshape(k // 512, 128, 2 * n)
    return np.ascontiguousarray(words), np.ascontiguousarray(byte.astype(np.uint8).reshape(k // 512, 16, n))


def unpack_weight(words, scales, fmt):
    g, _, n = scales.shape
    words = np.ascontiguousarray(words).reshape(g, 128, n, -1)
    if fmt == "e4m3":
        vals = words.view(ml_dtypes.float8_e4m3fn).astype(np.float64)
    else:
        nib = np.empty((g, 128, n, 4), np.uint8)
        nib[..., 0::2] = words & 0xF
        nib[..., 1::2] = words >> 4
        vals = E2M1[nib]
    vals = vals * np.repeat(np.exp2(scales.astype(np.float64) - 127.0), 8, axis=1)[..., None]
    return vals.transpose(0, 1, 3, 2).reshape(g * 512, n)


def gelu(v):
    return 0.5 * v * (1.0 + np.tanh(np.sqrt(2.0 / np.pi) * (v + 0.044715 * v**3)))


K, T, S, H, T2, N = 1024, 4096, 1024, 512, 2048, 512

def setup_inputs():
    n = np.random.standard_normal
    s = mx_kscale(K)[:, None]
    u = mx_kscale(H)[:, None]
    tab_words, tab_scales = pack_weight(n((K, T)) * s, "e4m3")
    wout_words, wout_scales = pack_weight(n((K, H)) / np.sqrt(K) / s * u.T, "e2m1")
    wjam_words, wjam_scales = pack_weight(n((H, N)) / np.sqrt(H) / u, "e2m1")
    return {
        "tab_words": tab_words, "tab_scales": tab_scales,
        "offs": striped(np.random.permutation(T)[:S]),
        "offs2": striped(np.random.permutation(T2)[:S]),
        "win": (n((K, H)) / np.sqrt(K) / s * u.T).astype(np.float32),
        "wout_words": wout_words, "wout_scales": wout_scales,
        "wgs": np.exp(0.3 * n((128, S))).astype(np.float32),
        "old": (n((H, T2)) * u).astype(np.float32),
        "wfree": (n((H, N)) / np.sqrt(H) / u).astype(np.float32),
        "wjam_words": wjam_words, "wjam_scales": wjam_scales,
    }

def reference(tab_words, tab_scales, offs, offs2, win, wout_words, wout_scales, wgs, old, wfree, wjam_words, wjam_scales):
    v = unpack_weight(tab_words, tab_scales, "e4m3")[:, unstriped(offs)]
    wout = unpack_weight(wout_words, wout_scales, "e2m1")
    wjam = unpack_weight(wjam_words, wjam_scales, "e2m1")
    a = mxq(f64(win), 0, "e4m3").T @ v
    b = wout.T @ v
    h = np.maximum(a, 0.0) - np.maximum(b, 0.0)
    page = np.zeros((H, T2))
    page[:, unstriped(offs2)] = np.tile(f64(wgs), (H // 128, 1)) * h
    z = mxq(page + f64(old), 0, "e4m3")
    yf = mxq(f64(wfree), 0, "e4m3").T @ z
    yj = wjam.T @ z
    return np.maximum(yf, yj)

@@ -1,0 +1,273 @@
+from contextlib import ExitStack
+
+import concourse.mybir as mybir
+from concourse.masks import make_identity
+
+K, T, S, H, T2, N = 1024, 4096, 1024, 512, 2048, 512
+FLOPS = 2 * (2 * K * H * S + 2 * H * N * T2)
+
+F32 = mybir.dt.float32
+BF16 = mybir.dt.bfloat16
+I32 = mybir.dt.int32
+U32 = mybir.dt.uint32
+U16 = mybir.dt.uint16
+U8 = mybir.dt.uint8
+FP8X4 = mybir.dt.float8_e4m3fn_x4
+FP4X4 = mybir.dt.float4_e2m1fn_x4
+ALU = mybir.AluOpType
+ACT = mybir.ActivationFunctionType
+
+P = 128
+PACK = 4
+K_PASS = P * PACK
+PASSES = K // K_PASS
+BANK = 512
+HALVES = S // BANK
+LIST_COLS = BANK // 16
+ROW_TILES = H // P
+CHUNKS = T2 // BANK
+BLOCKS = BANK // P
+OUT_TILES = N // P
+
+
+def tile_list_junction_flow_forecast_kernel(
+    tc, tab_words, tab_scales, offs, offs2, win, wout_words, wout_scales, wgs, old, wfree, wjam_words, wjam_scales, out
+):
+    nc = tc.nc
+    with ExitStack() as ctx:
+        lists = ctx.enter_context(tc.tile_pool(name="lists", bufs=1))
+        keep = ctx.enter_context(tc.tile_pool(name="keep", bufs=1))
+        ring2 = ctx.enter_context(tc.tile_pool(name="ring2", bufs=2))
+        ring4 = ctx.enter_context(tc.tile_pool(name="ring4", bufs=4))
+        psum = ctx.enter_context(tc.psum_pool(name="psum", bufs=8))
+
+        def load_scale_rows(queue, plane, dram):
+            rows = dram.bitcast(I32).rearrange("a (q r) w -> r q a w", r=4)
+            for r in range(4):
+                queue.dma_start(out=plane[r:P:32, :, :], in_=rows[r])
+
+        pick = lists.tile([P, S // 16], U16, name="pick")
+        place = lists.tile([P, S // 16], U16, name="place")
+
+        tab_w = [keep.tile([P, T], I32, name=f"tab_w{a}") for a in range(PASSES)]
+        tab_s = keep.tile([P, PASSES, T // 4], I32, name="tab_s")
+        wout_w = keep.tile([P, PASSES, H // 2], I32, name="wout_w", align_bytes=64)
+        wout_s = keep.tile([P, PASSES, H // 4], I32, name="wout_s", align_bytes=64)
+        wjam_w = keep.tile([P, 1, N // 2], I32, name="wjam_w", align_bytes=64)
+        wjam_s = keep.tile([P, 1, N // 4], I32, name="wjam_s", align_bytes=64)
+        win_first = keep.tile([P, PASSES, PACK, P], F32, name="win_first")
+        win_rest = keep.tile([P, PASSES, PACK, H - P], F32, name="win_rest")
+        wgs_sb = keep.tile([P, S], F32, name="wgs_sb")
+        old_sb = [keep.tile([P, T2], F32, name=f"old{m}") for m in range(ROW_TILES)]
+        wfree_raw = keep.tile([P, PACK, N], F32, name="wfree_raw")
+        pages = [keep.tile([P, T2], F32, name=f"page{b}") for b in range(2)]
+        ident = keep.tile([P, P], F32, name="ident")
+        perm = keep.tile([P, P], F32, name="perm")
+
+        nc.vector.memset(wout_s[:], 0)
+        nc.vector.memset(tab_s[:], 0)
+        nc.vector.memset(wjam_s[:], 0)
+        for page in pages:
+            nc.vector.memset(page[:], 0.0)
+
+        words = tab_words.rearrange("a p t i -> a p (t i)").bitcast(I32)
+        win_rows = win.rearrange("(a p i) c -> a p i c", a=PASSES, i=PACK)
+        nc.sync.dma_start(pick[:], offs)
+        nc.sync.dma_start(out=tab_w[0][:], in_=words[0])
+        load_scale_rows(nc.scalar, wout_s, wout_scales)
+        load_scale_rows(nc.sync, tab_s, tab_scales)
+        nc.sync.dma_start(out=wout_w[:], in_=wout_words.bitcast(I32).rearrange("a p w -> p a w"))
+        nc.sync.dma_start(out=tab_w[1][:], in_=words[1])
+        for a in range(PASSES):
+            nc.sync.dma_start(out=win_first[:, a], in_=win_rows[a, :, :, 0:P])
+        nc.sync.dma_start(out=wgs_sb[:], in_=wgs)
+        nc.sync.dma_start(place[:], offs2)
+        for a in range(PASSES):
+            nc.sync.dma_start(out=win_rest[:, a], in_=win_rows[a, :, :, P:H])
+        for m in range(ROW_TILES):
+            nc.sync.dma_start(out=old_sb[m][:], in_=old[m * P : (m + 1) * P, :])
+        nc.sync.dma_start(out=wfree_raw[:], in_=wfree.rearrange("(p i) n -> p i n", i=PACK))
+        nc.sync.dma_start(out=wjam_w[:], in_=wjam_words.bitcast(I32).rearrange("a p w -> p a w"))
+        load_scale_rows(nc.sync, wjam_s, wjam_scales)
+
+        make_identity(nc, ident[:])
+        nc.gpsimd.tensor_copy(
+            out=perm[:].rearrange("k (u q e) -> k u q e", u=2, e=2),
+            in_=ident[:].rearrange("k (q u e) -> k u q e", u=2, e=2),
+        )
+
+        v_w = keep.tile([P, PASSES, S], U32, name="v_w", align_bytes=64)
+        v_s = keep.tile([P, PASSES, S], U8, name="v_s", align_bytes=64)
+        win_w = keep.tile([P, ROW_TILES, PASSES * P], U32, name="win_w", align_bytes=64)
+        win_s = keep.tile([P, ROW_TILES, PASSES * P], U8, name="win_s", align_bytes=64)
+        wfree_w = keep.tile([P, N], U32, name="wfree_w", align_bytes=64)
+        wfree_s = keep.tile([P, N], U8, name="wfree_s", align_bytes=64)
+        z_t = [keep.tile([P, BLOCKS, H], BF16, name=f"z_t{c}") for c in range(CHUNKS)]
+
+        def quantize_win(m, passes):
+            raw = win_first[:] if m == 0 else win_rest[:, :, :, (m - 1) * P : m * P]
+            count = passes.stop - passes.start
+            cols = slice(passes.start * P, passes.stop * P)
+            grouped = ring2.tile([P, count, P, PACK], BF16, name="win_grouped", align_bytes=64)
+            nc.scalar.copy(out=grouped[:], in_=raw[:, passes].rearrange("p a i c -> p a c i"))
+            nc.vector.quantize_mx(
+                out=win_w[:, m, cols].bitcast(FP8X4),
+                scales=win_s[:, m, cols],
+                in_=grouped[:].rearrange("p a c i -> p (a c i)"),
+            )
+
+        def quantize_wfree():
+            grouped = keep.tile([P, N, PACK], BF16, name="wfree_grouped", align_bytes=64)
+            nc.scalar.copy(out=grouped[:], in_=wfree_raw[:].rearrange("p i n -> p n i"))
+            nc.vector.quantize_mx(
+                out=wfree_w[:].bitcast(FP8X4), scales=wfree_s[:], in_=grouped[:].rearrange("p n i -> p (n i)")
+            )
+
+        nc.vector.tensor_copy(out=v_w[:, 0, :], in_=tab_w[0][:].bitcast(U32).indirect(pick[:]))
+        for a in range(PASSES):
+            nc.vector.tensor_copy(out=v_s[:, a, :], in_=tab_s[:, a, :].bitcast(U8).indirect(pick[:]))
+        for g in range(HALVES):
+            nc.vector.tensor_copy(
+                out=v_w[:, 1, g * BANK : (g + 1) * BANK],
+                in_=tab_w[1][:].bitcast(U32).indirect(pick[:, g * LIST_COLS : (g + 1) * LIST_COLS]),
+            )
+        for a in range(PASSES):
+            quantize_win(0, slice(a, a + 1))
+
+        def net_inflow(m):
+            h = ring2.tile([P, S], F32, name="h")
+            for g in range(HALVES):
+                cols = slice(g * BANK, (g + 1) * BANK)
+                outflow = psum.tile([P, BANK], F32, name="outflow", tag="bank")
+                inflow = psum.tile([P, BANK], F32, name="inflow", tag="bank")
+                for a in range(PASSES):
+                    nc.tensor.matmul_mx(
+                        out=outflow[:],
+                        lhsT=wout_w[:, a, m * P // 2 : (m + 1) * P // 2].bitcast(U8).bitcast(FP4X4),
+                        lhsT_scale=wout_s[:, a, m * P // 4 : (m + 1) * P // 4].bitcast(U8),
+                        rhs=v_w[:, a, cols].bitcast(FP8X4),
+                        rhs_scale=v_s[:, a, cols],
+                        start=(a == 0),
+                        stop=(a == PASSES - 1),
+                    )
+                for a in range(PASSES):
+                    nc.tensor.matmul_mx(
+                        out=inflow[:],
+                        lhsT=win_w[:, m, a * P : (a + 1) * P].bitcast(FP8X4),
+                        lhsT_scale=win_s[:, m, a * P : (a + 1) * P],
+                        rhs=v_w[:, a, cols].bitcast(FP8X4),
+                        rhs_scale=v_s[:, a, cols],
+                        start=(a == 0),
+                        stop=(a == PASSES - 1),
+                    )
+                out_relu = ring2.tile([P, BANK], F32, name="out_relu")
+                nc.scalar.activation(out=out_relu[:], in_=outflow[:], func=ACT.Relu)
+                nc.vector.scalar_tensor_tensor(
+                    out=h[:, cols], in0=inflow[:], scalar=0.0, in1=out_relu[:], op0=ALU.max, op1=ALU.subtract
+                )
+            return h
+
+        def scatter(m, h, pieces):
+            page = pages[m % 2]
+            hw = ring2.tile([P, S], F32, name="hw")
+            width = S // pieces
+            for g in range(pieces):
+                cols = slice(g * width, (g + 1) * width)
+                nc.vector.tensor_tensor(out=hw[:, cols], in0=h[:, cols], in1=wgs_sb[:, cols], op=ALU.mult)
+                nc.vector.tensor_copy(
+                    out=page[:].indirect(place[:, g * width // 16 : (g + 1) * width // 16]), in_=hw[:, cols]
+                )
+
+        def turn(bank, source, c, opens):
+            for q in range(BLOCKS):
+                cols = slice(c * BANK + q * P, c * BANK + (q + 1) * P)
+                nc.tensor.matmul(
+                    bank[:, q, :],
+                    source[:, cols],
+                    perm[:],
+                    start=(opens and q == 0),
+                    stop=(not opens and q == BLOCKS - 1),
+                    is_transpose=True,
+                )
+
+        def turn_old(m, c):
+            bank = psum.tile([P, BLOCKS, P], F32, name="z_bank", tag="bank")
+            turn(bank, old_sb[m], c, True)
+            return bank
+
+        def add_page(m, c, bank):
+            turn(bank, pages[m % 2], c, False)
+            half = P // 2
+            nc.scalar.copy(
+                out=z_t[c][:].rearrange("t q (u m x) -> t (q u) m x", u=2, x=half)[:, :, m, :],
+                in_=bank[:].rearrange("t q (u x) -> t (q u) x", u=2),
+            )
+
+        def turn_back_and_quantize(c):
+            pairs = z_t[c][:].rearrange("t q r -> t (q r)").bitcast(F32)
+            grouped = ring2.tile([P, BANK * PACK], BF16, name="z_grouped", align_bytes=64)
+            grouped_pairs = grouped[:].bitcast(F32)
+            for b in range(2):
+                bank = psum.tile([P, 2, 2, P], F32, name="pair_bank", tag="bank")
+                for q in range(2):
+                    for u in range(2):
+                        first = ((2 * b + q) * 2 + u) * P
+                        nc.tensor.transpose(bank[:, q, u, :], pairs[:, first : first + P], ident[:])
+                dst = grouped_pairs[:, b * BANK : (b + 1) * BANK].rearrange("p (q t u) -> p q t u", q=2, u=2)
+                src = bank[:].rearrange("p q u t -> p q t u")
+                if c >= CHUNKS // 2:
+                    nc.scalar.copy(out=dst, in_=src)
+                else:
+                    nc.vector.tensor_copy(out=dst, in_=src)
+            z_w = ring2.tile([P, BANK], U32, name="z_w", align_bytes=64)
+            z_s = ring2.tile([P, BANK], U8, name="z_s", align_bytes=64)
+            nc.vector.quantize_mx(out=z_w[:].bitcast(FP8X4), scales=z_s[:], in_=grouped[:])
+            return z_w, z_s
+
+        def forecast(c, z_w, z_s):
+            for n in range(OUT_TILES):
+                free = psum.tile([P, BANK], F32, name="free", tag="bank")
+                jam = psum.tile([P, BANK], F32, name="jam", tag="bank")
+                nc.tensor.matmul_mx(
+                    out=free[:],
+                    lhsT=wfree_w[:, n * P : (n + 1) * P].bitcast(FP8X4),
+                    lhsT_scale=wfree_s[:, n * P : (n + 1) * P],
+                    rhs=z_w[:].bitcast(FP8X4),
+                    rhs_scale=z_s[:],
+                    start=True,
+                    stop=True,
+                )
+                nc.tensor.matmul_mx(
+                    out=jam[:],
+                    lhsT=wjam_w[:, 0, n * P // 2 : (n + 1) * P // 2].bitcast(U8).bitcast(FP4X4),
+                    lhsT_scale=wjam_s[:, 0, n * P // 4 : (n + 1) * P // 4].bitcast(U8),
+                    rhs=z_w[:].bitcast(FP8X4),
+                    rhs_scale=z_s[:],
+                    start=True,
+                    stop=True,
+                )
+                free_sb = ring4.tile([P, BANK], F32, name="free_sb")
+                nc.scalar.copy(out=free_sb[:], in_=free[:])
+                result = ring4.tile([P, BANK], F32, name="result")
+                nc.vector.tensor_tensor(out=result[:], in0=jam[:], in1=free_sb[:], op=ALU.max)
+                nc.sync.dma_start(out=out[n * P : (n + 1) * P, c * BANK : (c + 1) * BANK], in_=result[:])
+
+        last = ROW_TILES - 1
+        h = net_inflow(0)
+        for m in range(last):
+            quantize_win(m + 1, slice(0, PASSES))
+            scatter(m, h, HALVES if m == 0 else 1)
+            h = net_inflow(m + 1)
+            for c in range(CHUNKS):
+                add_page(m, c, turn_old(m, c))
+        banks = [turn_old(last, c) for c in range(CHUNKS)]
+        scatter(last, h, 1)
+        quantize_wfree()
+        for c in range(CHUNKS):
+            add_page(last, c, banks[c])
+        quantized = turn_back_and_quantize(0)
+        for c in range(CHUNKS):
+            current = quantized
+            if c + 1 < CHUNKS:
+                quantized = turn_back_and_quantize(c + 1)
+            forecast(c, *current)

@@ -38,8 +38,11 @@ def tile_list_junction_flow_forecast_kernel(
         lists = ctx.enter_context(tc.tile_pool(name="lists", bufs=1))
         keep = ctx.enter_context(tc.tile_pool(name="keep", bufs=1))
         ring2 = ctx.enter_context(tc.tile_pool(name="ring2", bufs=2))
+        ring3 = ctx.enter_context(tc.tile_pool(name="ring3", bufs=3))
         ring4 = ctx.enter_context(tc.tile_pool(name="ring4", bufs=4))
-        psum = ctx.enter_context(tc.psum_pool(name="psum", bufs=8))
+        ring8 = ctx.enter_context(tc.tile_pool(name="ring8", bufs=8))
+        psum_mx = ctx.enter_context(tc.psum_pool(name="psum_mx", bufs=2))
+        psum_turn = ctx.enter_context(tc.psum_pool(name="psum_turn", bufs=4))
 
         def load_scale_rows(queue, plane, dram):
             rows = dram.bitcast(I32).rearrange("a (q r) w -> r q a w", r=4)
@@ -55,8 +58,7 @@ def tile_list_junction_flow_forecast_kernel(
         wout_s = keep.tile([P, PASSES, H // 4], I32, name="wout_s", align_bytes=64)
         wjam_w = keep.tile([P, 1, N // 2], I32, name="wjam_w", align_bytes=64)
         wjam_s = keep.tile([P, 1, N // 4], I32, name="wjam_s", align_bytes=64)
-        win_first = keep.tile([P, PASSES, PACK, P], F32, name="win_first")
-        win_rest = keep.tile([P, PASSES, PACK, H - P], F32, name="win_rest")
+        win_raw = keep.tile([P, PASSES, PACK, H], F32, name="win_raw")
         wgs_sb = keep.tile([P, S], F32, name="wgs_sb")
         old_sb = [keep.tile([P, T2], F32, name=f"old{m}") for m in range(ROW_TILES)]
         wfree_raw = keep.tile([P, PACK, N], F32, name="wfree_raw")
@@ -79,11 +81,12 @@ def tile_list_junction_flow_forecast_kernel(
         nc.sync.dma_start(out=wout_w[:], in_=wout_words.bitcast(I32).rearrange("a p w -> p a w"))
         nc.sync.dma_start(out=tab_w[1][:], in_=words[1])
         for a in range(PASSES):
-            nc.sync.dma_start(out=win_first[:, a], in_=win_rows[a, :, :, 0:P])
+            nc.sync.dma_start(out=win_raw[:, a, :, 0:P], in_=win_rows[a, :, :, 0:P])
         nc.sync.dma_start(out=wgs_sb[:], in_=wgs)
         nc.sync.dma_start(place[:], offs2)
-        for a in range(PASSES):
-            nc.sync.dma_start(out=win_rest[:, a], in_=win_rows[a, :, :, P:H])
+        for cols in (slice(P, 2 * P), slice(2 * P, H)):
+            for a in range(PASSES):
+                nc.sync.dma_start(out=win_raw[:, a, :, cols], in_=win_rows[a, :, :, cols])
         for m in range(ROW_TILES):
             nc.sync.dma_start(out=old_sb[m][:], in_=old[m * P : (m + 1) * P, :])
         nc.sync.dma_start(out=wfree_raw[:], in_=wfree.rearrange("(p i) n -> p i n", i=PACK))
@@ -105,7 +108,7 @@ def tile_list_junction_flow_forecast_kernel(
         z_t = [keep.tile([P, BLOCKS, H], BF16, name=f"z_t{c}") for c in range(CHUNKS)]
 
         def quantize_win(m, passes):
-            raw = win_first[:] if m == 0 else win_rest[:, :, :, (m - 1) * P : m * P]
+            raw = win_raw[:, :, :, m * P : (m + 1) * P]
             count = passes.stop - passes.start
             cols = slice(passes.start * P, passes.stop * P)
             grouped = ring2.tile([P, count, P, PACK], BF16, name="win_grouped", align_bytes=64)
@@ -135,11 +138,11 @@ def tile_list_junction_flow_forecast_kernel(
             quantize_win(0, slice(a, a + 1))
 
         def net_inflow(m):
-            h = ring2.tile([P, S], F32, name="h")
+            h = ring3.tile([P, S], F32, name="h")
             for g in range(HALVES):
                 cols = slice(g * BANK, (g + 1) * BANK)
-                outflow = psum.tile([P, BANK], F32, name="outflow", tag="bank")
-                inflow = psum.tile([P, BANK], F32, name="inflow", tag="bank")
+                outflow = psum_mx.tile([P, BANK], F32, name="outflow", tag="scalar_reads")
+                inflow = psum_mx.tile([P, BANK], F32, name="inflow", tag="vector_reads")
                 for a in range(PASSES):
                     nc.tensor.matmul_mx(
                         out=outflow[:],
@@ -162,24 +165,34 @@ def tile_list_junction_flow_forecast_kernel(
                     )
                 out_relu = ring2.tile([P, BANK], F32, name="out_relu")
                 nc.scalar.activation(out=out_relu[:], in_=outflow[:], func=ACT.Relu)
-                nc.vector.scalar_tensor_tensor(
-                    out=h[:, cols], in0=inflow[:], scalar=0.0, in1=out_relu[:], op0=ALU.max, op1=ALU.subtract
-                )
+                if m == 0:
+                    nc.vector.scalar_tensor_tensor(
+                        out=h[:, cols], in0=inflow[:], scalar=0.0, in1=out_relu[:], op0=ALU.max, op1=ALU.subtract
+                    )
+                    if g > 0:
+                        nc.vector.tensor_tensor(out=h[:, cols], in0=h[:, cols], in1=wgs_sb[:, cols], op=ALU.mult)
+                else:
+                    in_relu = ring2.tile([P, BANK], F32, name="in_relu")
+                    nc.scalar.activation(out=in_relu[:], in_=inflow[:], func=ACT.Relu)
+                    net = ring2.tile([P, BANK], F32, name="net")
+                    nc.gpsimd.tensor_tensor(out=net[:], in0=in_relu[:], in1=out_relu[:], op=ALU.subtract)
+                    nc.gpsimd.tensor_tensor(out=h[:, cols], in0=net[:], in1=wgs_sb[:, cols], op=ALU.mult)
             return h
 
-        def scatter(m, h, pieces):
+        def scatter(m, h, widths):
             page = pages[m % 2]
-            hw = ring2.tile([P, S], F32, name="hw")
-            width = S // pieces
-            for g in range(pieces):
-                cols = slice(g * width, (g + 1) * width)
-                nc.vector.tensor_tensor(out=hw[:, cols], in0=h[:, cols], in1=wgs_sb[:, cols], op=ALU.mult)
-                nc.vector.tensor_copy(
-                    out=page[:].indirect(place[:, g * width // 16 : (g + 1) * width // 16]), in_=hw[:, cols]
-                )
+            first = 0
+            for width in widths:
+                cols = slice(first, first + width)
+                window = page[:].indirect(place[:, first // 16 : (first + width) // 16])
+                if m == 0 and first < BANK:
+                    nc.vector.tensor_tensor(out=window, in0=h[:, cols], in1=wgs_sb[:, cols], op=ALU.mult)
+                else:
+                    nc.vector.tensor_copy(out=window, in_=h[:, cols])
+                first += width
 
-        def turn(bank, source, c, opens):
-            for q in range(BLOCKS):
+        def turn(bank, source, c, blocks, opens):
+            for q in blocks:
                 cols = slice(c * BANK + q * P, c * BANK + (q + 1) * P)
                 nc.tensor.matmul(
                     bank[:, q, :],
@@ -191,83 +204,98 @@ def tile_list_junction_flow_forecast_kernel(
                 )
 
         def turn_old(m, c):
-            bank = psum.tile([P, BLOCKS, P], F32, name="z_bank", tag="bank")
-            turn(bank, old_sb[m], c, True)
+            bank = psum_turn.tile([P, BLOCKS, P], F32, name="z_bank", tag="bank")
+            turn(bank, old_sb[m], c, range(BLOCKS), True)
             return bank
 
         def add_page(m, c, bank):
-            turn(bank, pages[m % 2], c, False)
+            turn(bank, pages[m % 2], c, range(BLOCKS), False)
             half = P // 2
             nc.scalar.copy(
                 out=z_t[c][:].rearrange("t q (u m x) -> t (q u) m x", u=2, x=half)[:, :, m, :],
                 in_=bank[:].rearrange("t q (u x) -> t (q u) x", u=2),
             )
 
-        def turn_back_and_quantize(c):
+        def turn_back_and_quantize(first, width):
+            c, q0 = first // BANK, first % BANK // P
             pairs = z_t[c][:].rearrange("t q r -> t (q r)").bitcast(F32)
-            grouped = ring2.tile([P, BANK * PACK], BF16, name="z_grouped", align_bytes=64)
+            grouped = ring2.tile([P, width * PACK], BF16, name="z_grouped", align_bytes=64)
             grouped_pairs = grouped[:].bitcast(F32)
-            for b in range(2):
-                bank = psum.tile([P, 2, 2, P], F32, name="pair_bank", tag="bank")
+            for b in range(width // (2 * P)):
+                bank = psum_turn.tile([P, 2, 2, P], F32, name="pair_bank", tag="bank")
                 for q in range(2):
                     for u in range(2):
-                        first = ((2 * b + q) * 2 + u) * P
-                        nc.tensor.transpose(bank[:, q, u, :], pairs[:, first : first + P], ident[:])
+                        word = ((q0 + 2 * b + q) * 2 + u) * P
+                        nc.tensor.transpose(bank[:, q, u, :], pairs[:, word : word + P], ident[:])
                 dst = grouped_pairs[:, b * BANK : (b + 1) * BANK].rearrange("p (q t u) -> p q t u", q=2, u=2)
                 src = bank[:].rearrange("p q u t -> p q t u")
-                if c >= CHUNKS // 2:
+                if first >= T2 // 2:
                     nc.scalar.copy(out=dst, in_=src)
                 else:
                     nc.vector.tensor_copy(out=dst, in_=src)
-            z_w = ring2.tile([P, BANK], U32, name="z_w", align_bytes=64)
-            z_s = ring2.tile([P, BANK], U8, name="z_s", align_bytes=64)
+            z_w = ring2.tile([P, width], U32, name="z_w", align_bytes=64)
+            z_s = ring2.tile([P, width], U8, name="z_s", align_bytes=64)
             nc.vector.quantize_mx(out=z_w[:].bitcast(FP8X4), scales=z_s[:], in_=grouped[:])
             return z_w, z_s
 
-        def forecast(c, z_w, z_s):
-            for n in range(OUT_TILES):
-                free = psum.tile([P, BANK], F32, name="free", tag="bank")
-                jam = psum.tile([P, BANK], F32, name="jam", tag="bank")
-                nc.tensor.matmul_mx(
-                    out=free[:],
-                    lhsT=wfree_w[:, n * P : (n + 1) * P].bitcast(FP8X4),
-                    lhsT_scale=wfree_s[:, n * P : (n + 1) * P],
-                    rhs=z_w[:].bitcast(FP8X4),
-                    rhs_scale=z_s[:],
-                    start=True,
-                    stop=True,
-                )
-                nc.tensor.matmul_mx(
-                    out=jam[:],
-                    lhsT=wjam_w[:, 0, n * P // 2 : (n + 1) * P // 2].bitcast(U8).bitcast(FP4X4),
-                    lhsT_scale=wjam_s[:, 0, n * P // 4 : (n + 1) * P // 4].bitcast(U8),
-                    rhs=z_w[:].bitcast(FP8X4),
-                    rhs_scale=z_s[:],
-                    start=True,
-                    stop=True,
-                )
-                free_sb = ring4.tile([P, BANK], F32, name="free_sb")
+        def forecast(first, width, z_w, z_s):
+            group = BANK // width
+            for g in range(OUT_TILES // group):
+                free = psum_mx.tile([P, group, width], F32, name="free", tag="scalar_reads")
+                if g % 2 == 0:
+                    jam = psum_mx.tile([P, group, width], F32, name="jam", tag="vector_reads")
+                else:
+                    jam = psum_turn.tile([P, group, width], F32, name="jam", tag="bank")
+                for i in range(group):
+                    n = g * group + i
+                    nc.tensor.matmul_mx(
+                        out=free[:, i, :],
+                        lhsT=wfree_w[:, n * P : (n + 1) * P].bitcast(FP8X4),
+                        lhsT_scale=wfree_s[:, n * P : (n + 1) * P],
+                        rhs=z_w[:].bitcast(FP8X4),
+                        rhs_scale=z_s[:],
+                        start=True,
+                        stop=True,
+                    )
+                for i in range(group):
+                    n = g * group + i
+                    nc.tensor.matmul_mx(
+                        out=jam[:, i, :],
+                        lhsT=wjam_w[:, 0, n * P // 2 : (n + 1) * P // 2].bitcast(U8).bitcast(FP4X4),
+                        lhsT_scale=wjam_s[:, 0, n * P // 4 : (n + 1) * P // 4].bitcast(U8),
+                        rhs=z_w[:].bitcast(FP8X4),
+                        rhs_scale=z_s[:],
+                        start=True,
+                        stop=True,
+                    )
+                free_sb = ring4.tile([P, group, width], F32, name="free_sb")
                 nc.scalar.copy(out=free_sb[:], in_=free[:])
-                result = ring4.tile([P, BANK], F32, name="result")
+                result = ring8.tile([P, group, width], F32, name="result")
                 nc.vector.tensor_tensor(out=result[:], in0=jam[:], in1=free_sb[:], op=ALU.max)
-                nc.sync.dma_start(out=out[n * P : (n + 1) * P, c * BANK : (c + 1) * BANK], in_=result[:])
+                rows = out[g * group * P : (g + 1) * group * P, first : first + width]
+                nc.sync.dma_start(out=rows.rearrange("(i p) t -> p i t", p=P), in_=result[:])
 
         last = ROW_TILES - 1
         h = net_inflow(0)
-        for m in range(last):
-            quantize_win(m + 1, slice(0, PASSES))
-            scatter(m, h, HALVES if m == 0 else 1)
-            h = net_inflow(m + 1)
-            for c in range(CHUNKS):
-                add_page(m, c, turn_old(m, c))
+        for m in range(ROW_TILES):
+            if m == 0:
+                for later in range(1, ROW_TILES):
+                    quantize_win(later, slice(0, PASSES))
+            scatter(m, h, ([256, 256, 512], [512, 512], [S], [S])[m])
+            if m < last:
+                h = net_inflow(m + 1)
+            if m > 0:
+                for c in range(CHUNKS):
+                    add_page(m - 1, c, turn_old(m - 1, c))
         banks = [turn_old(last, c) for c in range(CHUNKS)]
-        scatter(last, h, 1)
         quantize_wfree()
         for c in range(CHUNKS):
             add_page(last, c, banks[c])
-        quantized = turn_back_and_quantize(0)
-        for c in range(CHUNKS):
+        widths = [256, 256, 512, 512, 512]
+        firsts = [sum(widths[:i]) for i in range(len(widths))]
+        quantized = turn_back_and_quantize(firsts[0], widths[0])
+        for i in range(len(widths)):
             current = quantized
-            if c + 1 < CHUNKS:
-                quantized = turn_back_and_quantize(c + 1)
-            forecast(c, *current)
+            if i + 1 < len(widths):
+                quantized = turn_back_and_quantize(firsts[i + 1], widths[i + 1])
+            forecast(firsts[i], widths[i], *current)

@@ -41,14 +41,14 @@ def tile_list_junction_flow_forecast_kernel(
         ring3 = ctx.enter_context(tc.tile_pool(name="ring3", bufs=3))
         ring4 = ctx.enter_context(tc.tile_pool(name="ring4", bufs=4))
         ring8 = ctx.enter_context(tc.tile_pool(name="ring8", bufs=8))
-        psum_mx = ctx.enter_context(tc.psum_pool(name="psum_mx", bufs=2))
-        psum_turn = ctx.enter_context(tc.psum_pool(name="psum_turn", bufs=4))
+        psum = ctx.enter_context(tc.psum_pool(name="psum", bufs=1))
 
         def load_scale_rows(queue, plane, dram):
             rows = dram.bitcast(I32).rearrange("a (q r) w -> r q a w", r=4)
             for r in range(4):
                 queue.dma_start(out=plane[r:P:32, :, :], in_=rows[r])
 
+        last = ROW_TILES - 1
         pick = lists.tile([P, S // 16], U16, name="pick")
         place = lists.tile([P, S // 16], U16, name="place")
 
@@ -127,7 +127,7 @@ def tile_list_junction_flow_forecast_kernel(
             )
 
         nc.vector.tensor_copy(out=v_w[:, 0, :], in_=tab_w[0][:].bitcast(U32).indirect(pick[:]))
-        for a in range(PASSES):
+        for a in reversed(range(PASSES)):
             nc.vector.tensor_copy(out=v_s[:, a, :], in_=tab_s[:, a, :].bitcast(U8).indirect(pick[:]))
         for g in range(HALVES):
             nc.vector.tensor_copy(
@@ -141,8 +141,8 @@ def tile_list_junction_flow_forecast_kernel(
             h = ring3.tile([P, S], F32, name="h")
             for g in range(HALVES):
                 cols = slice(g * BANK, (g + 1) * BANK)
-                outflow = psum_mx.tile([P, BANK], F32, name="outflow", tag="scalar_reads")
-                inflow = psum_mx.tile([P, BANK], F32, name="inflow", tag="vector_reads")
+                outflow = psum.tile([P, BANK], F32, name="outflow", tag=f"bank{HALVES + g}")
+                inflow = psum.tile([P, BANK], F32, name="inflow", tag=f"bank{g}")
                 for a in range(PASSES):
                     nc.tensor.matmul_mx(
                         out=outflow[:],
@@ -179,9 +179,8 @@ def tile_list_junction_flow_forecast_kernel(
                     nc.gpsimd.tensor_tensor(out=h[:, cols], in0=net[:], in1=wgs_sb[:, cols], op=ALU.mult)
             return h
 
-        def scatter(m, h, widths):
+        def scatter(m, h, first, widths):
             page = pages[m % 2]
-            first = 0
             for width in widths:
                 cols = slice(first, first + width)
                 window = page[:].indirect(place[:, first // 16 : (first + width) // 16])
@@ -190,6 +189,19 @@ def tile_list_junction_flow_forecast_kernel(
                 else:
                     nc.vector.tensor_copy(out=window, in_=h[:, cols])
                 first += width
+
+        def warm_up():
+            bank = psum.tile([P, BANK], F32, name="warm_bank", tag="bank7")
+            for n in range(3):
+                nc.tensor.matmul_mx(
+                    out=bank[:],
+                    lhsT=wfree_w[:, n * P : (n + 1) * P].bitcast(FP8X4),
+                    lhsT_scale=wfree_s[:, n * P : (n + 1) * P],
+                    rhs=v_w[:, 0, 0:BANK].bitcast(FP8X4),
+                    rhs_scale=v_s[:, 0, 0:BANK],
+                    start=True,
+                    stop=True,
+                )
 
         def turn(bank, source, c, blocks, opens):
             for q in blocks:
@@ -204,7 +216,7 @@ def tile_list_junction_flow_forecast_kernel(
                 )
 
         def turn_old(m, c):
-            bank = psum_turn.tile([P, BLOCKS, P], F32, name="z_bank", tag="bank")
+            bank = psum.tile([P, BLOCKS, P], F32, name="z_bank", tag=f"bank{c if m == last else CHUNKS + c}")
             turn(bank, old_sb[m], c, range(BLOCKS), True)
             return bank
 
@@ -222,14 +234,14 @@ def tile_list_junction_flow_forecast_kernel(
             grouped = ring2.tile([P, width * PACK], BF16, name="z_grouped", align_bytes=64)
             grouped_pairs = grouped[:].bitcast(F32)
             for b in range(width // (2 * P)):
-                bank = psum_turn.tile([P, 2, 2, P], F32, name="pair_bank", tag="bank")
+                bank = psum.tile([P, 2, 2, P], F32, name="pair_bank", tag=f"bank{4 + (first // (2 * P) + b) % 2}")
                 for q in range(2):
                     for u in range(2):
                         word = ((q0 + 2 * b + q) * 2 + u) * P
                         nc.tensor.transpose(bank[:, q, u, :], pairs[:, word : word + P], ident[:])
                 dst = grouped_pairs[:, b * BANK : (b + 1) * BANK].rearrange("p (q t u) -> p q t u", q=2, u=2)
                 src = bank[:].rearrange("p q u t -> p q t u")
-                if first >= T2 // 2:
+                if first // (2 * P) + b >= 3:
                     nc.scalar.copy(out=dst, in_=src)
                 else:
                     nc.vector.tensor_copy(out=dst, in_=src)
@@ -241,11 +253,9 @@ def tile_list_junction_flow_forecast_kernel(
         def forecast(first, width, z_w, z_s):
             group = BANK // width
             for g in range(OUT_TILES // group):
-                free = psum_mx.tile([P, group, width], F32, name="free", tag="scalar_reads")
-                if g % 2 == 0:
-                    jam = psum_mx.tile([P, group, width], F32, name="jam", tag="vector_reads")
-                else:
-                    jam = psum_turn.tile([P, group, width], F32, name="jam", tag="bank")
+                step = first * OUT_TILES // BANK + g
+                free = psum.tile([P, group, width], F32, name="free", tag=f"bank{step % 2}")
+                jam = psum.tile([P, group, width], F32, name="jam", tag=f"bank{(2, 3, 6, 7)[step % 4]}")
                 for i in range(group):
                     n = g * group + i
                     nc.tensor.matmul_mx(
@@ -275,20 +285,21 @@ def tile_list_junction_flow_forecast_kernel(
                 rows = out[g * group * P : (g + 1) * group * P, first : first + width]
                 nc.sync.dma_start(out=rows.rearrange("(i p) t -> p i t", p=P), in_=result[:])
 
-        last = ROW_TILES - 1
         h = net_inflow(0)
-        for m in range(ROW_TILES):
-            if m == 0:
-                for later in range(1, ROW_TILES):
-                    quantize_win(later, slice(0, PASSES))
-            scatter(m, h, ([256, 256, 512], [512, 512], [S], [S])[m])
-            if m < last:
-                h = net_inflow(m + 1)
+        for m in range(last):
+            quantize_win(m + 1, slice(0, PASSES))
+            scatter(m, h, 0, [256, 256, 512] if m == 0 else [512, 512])
+            h = net_inflow(m + 1)
             if m > 0:
                 for c in range(CHUNKS):
                     add_page(m - 1, c, turn_old(m - 1, c))
+        scatter(last, h, 0, [512, 256])
+        for c in range(CHUNKS):
+            add_page(last - 1, c, turn_old(last - 1, c))
         banks = [turn_old(last, c) for c in range(CHUNKS)]
         quantize_wfree()
+        warm_up()
+        scatter(last, h, 768, [256])
         for c in range(CHUNKS):
             add_page(last, c, banks[c])
         widths = [256, 256, 512, 512, 512]

@@ -28,6 +28,7 @@ ROW_TILES = H // P
 CHUNKS = T2 // BANK
 BLOCKS = BANK // P
 OUT_TILES = N // P
+STEPS = OUT_TILES * CHUNKS
 
 
 def tile_list_junction_flow_forecast_kernel(
@@ -38,7 +39,6 @@ def tile_list_junction_flow_forecast_kernel(
         lists = ctx.enter_context(tc.tile_pool(name="lists", bufs=1))
         keep = ctx.enter_context(tc.tile_pool(name="keep", bufs=1))
         ring2 = ctx.enter_context(tc.tile_pool(name="ring2", bufs=2))
-        ring3 = ctx.enter_context(tc.tile_pool(name="ring3", bufs=3))
         ring4 = ctx.enter_context(tc.tile_pool(name="ring4", bufs=4))
         ring8 = ctx.enter_context(tc.tile_pool(name="ring8", bufs=8))
         psum = ctx.enter_context(tc.psum_pool(name="psum", bufs=1))
@@ -79,22 +79,23 @@ def tile_list_junction_flow_forecast_kernel(
         load_scale_rows(nc.scalar, wout_s, wout_scales)
         load_scale_rows(nc.sync, tab_s, tab_scales)
         nc.sync.dma_start(out=wout_w[:], in_=wout_words.bitcast(I32).rearrange("a p w -> p a w"))
-        nc.sync.dma_start(out=tab_w[1][:], in_=words[1])
-        for a in range(PASSES):
-            nc.sync.dma_start(out=win_raw[:, a, :, 0:P], in_=win_rows[a, :, :, 0:P])
-        nc.sync.dma_start(out=wgs_sb[:], in_=wgs)
         nc.sync.dma_start(place[:], offs2)
+        nc.sync.dma_start(out=win_raw[:, 0, :, 0:P], in_=win_rows[0, :, :, 0:P])
+        nc.sync.dma_start(out=tab_w[1][:], in_=words[1])
+        nc.sync.dma_start(out=win_raw[:, 1, :, 0:P], in_=win_rows[1, :, :, 0:P])
+        nc.sync.dma_start(out=wgs_sb[:], in_=wgs)
         for cols in (slice(P, 2 * P), slice(2 * P, H)):
             for a in range(PASSES):
                 nc.sync.dma_start(out=win_raw[:, a, :, cols], in_=win_rows[a, :, :, cols])
         for m in range(ROW_TILES):
             nc.sync.dma_start(out=old_sb[m][:], in_=old[m * P : (m + 1) * P, :])
-        nc.sync.dma_start(out=wfree_raw[:], in_=wfree.rearrange("(p i) n -> p i n", i=PACK))
+            if m == 1:
+                nc.sync.dma_start(out=wfree_raw[:], in_=wfree.rearrange("(p i) n -> p i n", i=PACK))
         nc.sync.dma_start(out=wjam_w[:], in_=wjam_words.bitcast(I32).rearrange("a p w -> p a w"))
         load_scale_rows(nc.sync, wjam_s, wjam_scales)
 
         make_identity(nc, ident[:])
-        nc.gpsimd.tensor_copy(
+        nc.scalar.copy(
             out=perm[:].rearrange("k (u q e) -> k u q e", u=2, e=2),
             in_=ident[:].rearrange("k (q u e) -> k u q e", u=2, e=2),
         )
@@ -103,7 +104,6 @@ def tile_list_junction_flow_forecast_kernel(
         v_s = keep.tile([P, PASSES, S], U8, name="v_s", align_bytes=64)
         win_w = keep.tile([P, ROW_TILES, PASSES * P], U32, name="win_w", align_bytes=64)
         win_s = keep.tile([P, ROW_TILES, PASSES * P], U8, name="win_s", align_bytes=64)
-        wfree_w = keep.tile([P, N], U32, name="wfree_w", align_bytes=64)
         wfree_s = keep.tile([P, N], U8, name="wfree_s", align_bytes=64)
         z_t = [keep.tile([P, BLOCKS, H], BF16, name=f"z_t{c}") for c in range(CHUNKS)]
 
@@ -111,7 +111,8 @@ def tile_list_junction_flow_forecast_kernel(
             raw = win_raw[:, :, :, m * P : (m + 1) * P]
             count = passes.stop - passes.start
             cols = slice(passes.start * P, passes.stop * P)
-            grouped = ring2.tile([P, count, P, PACK], BF16, name="win_grouped", align_bytes=64)
+            slot = f"first_grouped{passes.start}" if m == 0 else h_slot(m - 1, 1)
+            grouped = keep.tile([P, count, P, PACK], BF16, name="win_grouped", tag=slot, align_bytes=64)
             nc.scalar.copy(out=grouped[:], in_=raw[:, passes].rearrange("p a i c -> p a c i"))
             nc.vector.quantize_mx(
                 out=win_w[:, m, cols].bitcast(FP8X4),
@@ -119,28 +120,34 @@ def tile_list_junction_flow_forecast_kernel(
                 in_=grouped[:].rearrange("p a c i -> p (a c i)"),
             )
 
+        def h_slot(m, g):
+            return f"h{g * (1 + m % 2)}"
+
         def quantize_wfree():
             grouped = keep.tile([P, N, PACK], BF16, name="wfree_grouped", align_bytes=64)
             nc.scalar.copy(out=grouped[:], in_=wfree_raw[:].rearrange("p i n -> p n i"))
+            codes = keep.tile([P, N], U32, name="wfree_w", tag=h_slot(last, 0), align_bytes=64)
             nc.vector.quantize_mx(
-                out=wfree_w[:].bitcast(FP8X4), scales=wfree_s[:], in_=grouped[:].rearrange("p n i -> p (n i)")
+                out=codes[:].bitcast(FP8X4), scales=wfree_s[:], in_=grouped[:].rearrange("p n i -> p (n i)")
             )
+            return codes
 
         nc.vector.tensor_copy(out=v_w[:, 0, :], in_=tab_w[0][:].bitcast(U32).indirect(pick[:]))
         for a in reversed(range(PASSES)):
             nc.vector.tensor_copy(out=v_s[:, a, :], in_=tab_s[:, a, :].bitcast(U8).indirect(pick[:]))
         for g in range(HALVES):
+            quantize_win(0, slice(g, g + 1))
             nc.vector.tensor_copy(
                 out=v_w[:, 1, g * BANK : (g + 1) * BANK],
                 in_=tab_w[1][:].bitcast(U32).indirect(pick[:, g * LIST_COLS : (g + 1) * LIST_COLS]),
             )
-        for a in range(PASSES):
-            quantize_win(0, slice(a, a + 1))
 
         def net_inflow(m):
-            h = ring3.tile([P, S], F32, name="h")
+            halves = []
             for g in range(HALVES):
                 cols = slice(g * BANK, (g + 1) * BANK)
+                h = keep.tile([P, BANK], F32, name="h", tag=h_slot(m, g), align_bytes=64)
+                halves.append(h)
                 outflow = psum.tile([P, BANK], F32, name="outflow", tag=f"bank{HALVES + g}")
                 inflow = psum.tile([P, BANK], F32, name="inflow", tag=f"bank{g}")
                 for a in range(PASSES):
@@ -163,36 +170,25 @@ def tile_list_junction_flow_forecast_kernel(
                         start=(a == 0),
                         stop=(a == PASSES - 1),
                     )
-                out_relu = ring2.tile([P, BANK], F32, name="out_relu")
+                out_relu = keep.tile([P, BANK], F32, name="out_relu", tag=f"out_relu{g}", align_bytes=64)
                 nc.scalar.activation(out=out_relu[:], in_=outflow[:], func=ACT.Relu)
-                if m == 0:
-                    nc.vector.scalar_tensor_tensor(
-                        out=h[:, cols], in0=inflow[:], scalar=0.0, in1=out_relu[:], op0=ALU.max, op1=ALU.subtract
-                    )
-                    if g > 0:
-                        nc.vector.tensor_tensor(out=h[:, cols], in0=h[:, cols], in1=wgs_sb[:, cols], op=ALU.mult)
-                else:
-                    in_relu = ring2.tile([P, BANK], F32, name="in_relu")
-                    nc.scalar.activation(out=in_relu[:], in_=inflow[:], func=ACT.Relu)
-                    net = ring2.tile([P, BANK], F32, name="net")
-                    nc.gpsimd.tensor_tensor(out=net[:], in0=in_relu[:], in1=out_relu[:], op=ALU.subtract)
-                    nc.gpsimd.tensor_tensor(out=h[:, cols], in0=net[:], in1=wgs_sb[:, cols], op=ALU.mult)
-            return h
+                nc.vector.scalar_tensor_tensor(
+                    out=h[:], in0=inflow[:], scalar=0.0, in1=out_relu[:], op0=ALU.max, op1=ALU.subtract
+                )
+            return halves
 
-        def scatter(m, h, first, widths):
+        def scatter(m, halves, first, widths):
             page = pages[m % 2]
             for width in widths:
                 cols = slice(first, first + width)
                 window = page[:].indirect(place[:, first // 16 : (first + width) // 16])
-                if m == 0 and first < BANK:
-                    nc.vector.tensor_tensor(out=window, in0=h[:, cols], in1=wgs_sb[:, cols], op=ALU.mult)
-                else:
-                    nc.vector.tensor_copy(out=window, in_=h[:, cols])
+                values = halves[first // BANK][:, first % BANK : first % BANK + width]
+                nc.vector.tensor_tensor(out=window, in0=values, in1=wgs_sb[:, cols], op=ALU.mult)
                 first += width
 
         def warm_up():
             bank = psum.tile([P, BANK], F32, name="warm_bank", tag="bank7")
-            for n in range(3):
+            for n in range(OUT_TILES):
                 nc.tensor.matmul_mx(
                     out=bank[:],
                     lhsT=wfree_w[:, n * P : (n + 1) * P].bitcast(FP8X4),
@@ -203,30 +199,33 @@ def tile_list_junction_flow_forecast_kernel(
                     stop=True,
                 )
 
-        def turn(bank, source, c, blocks, opens):
-            for q in blocks:
-                cols = slice(c * BANK + q * P, c * BANK + (q + 1) * P)
+        def turn(bank, source, first, opens):
+            blocks = bank.shape[1]
+            for q in range(blocks):
                 nc.tensor.matmul(
                     bank[:, q, :],
-                    source[:, cols],
+                    source[:, first + q * P : first + (q + 1) * P],
                     perm[:],
                     start=(opens and q == 0),
-                    stop=(not opens and q == BLOCKS - 1),
+                    stop=(not opens and q == blocks - 1),
                     is_transpose=True,
                 )
 
-        def turn_old(m, c):
-            bank = psum.tile([P, BLOCKS, P], F32, name="z_bank", tag=f"bank{c if m == last else CHUNKS + c}")
-            turn(bank, old_sb[m], c, range(BLOCKS), True)
+        def turn_old(m, first, width, bank_number):
+            bank = psum.tile([P, width // P, P], F32, name="z_bank", tag=f"bank{bank_number}")
+            turn(bank, old_sb[m], first, True)
             return bank
 
-        def add_page(m, c, bank):
-            turn(bank, pages[m % 2], c, range(BLOCKS), False)
-            half = P // 2
-            nc.scalar.copy(
-                out=z_t[c][:].rearrange("t q (u m x) -> t (q u) m x", u=2, x=half)[:, :, m, :],
-                in_=bank[:].rearrange("t q (u x) -> t (q u) x", u=2),
-            )
+        def add_page(m, first, bank, on_vector):
+            turn(bank, pages[m % 2], first, False)
+            q0 = first % BANK // P
+            rows = z_t[first // BANK][:, q0 : q0 + bank.shape[1], :]
+            dst = rows.rearrange("t q (u m x) -> t (q u) m x", u=2, x=P // 2)[:, :, m, :]
+            src = bank[:].rearrange("t q (u x) -> t (q u) x", u=2)
+            if on_vector:
+                nc.vector.tensor_copy(out=dst, in_=src)
+            else:
+                nc.scalar.copy(out=dst, in_=src)
 
         def turn_back_and_quantize(first, width):
             c, q0 = first // BANK, first % BANK // P
@@ -241,7 +240,7 @@ def tile_list_junction_flow_forecast_kernel(
                         nc.tensor.transpose(bank[:, q, u, :], pairs[:, word : word + P], ident[:])
                 dst = grouped_pairs[:, b * BANK : (b + 1) * BANK].rearrange("p (q t u) -> p q t u", q=2, u=2)
                 src = bank[:].rearrange("p q u t -> p q t u")
-                if first // (2 * P) + b >= 3:
+                if first // (2 * P) + b >= 2:
                     nc.scalar.copy(out=dst, in_=src)
                 else:
                     nc.vector.tensor_copy(out=dst, in_=src)
@@ -279,31 +278,39 @@ def tile_list_junction_flow_forecast_kernel(
                         stop=True,
                     )
                 free_sb = ring4.tile([P, group, width], F32, name="free_sb")
-                nc.scalar.copy(out=free_sb[:], in_=free[:])
                 result = ring8.tile([P, group, width], F32, name="result")
-                nc.vector.tensor_tensor(out=result[:], in0=jam[:], in1=free_sb[:], op=ALU.max)
-                rows = out[g * group * P : (g + 1) * group * P, first : first + width]
-                nc.sync.dma_start(out=rows.rearrange("(i p) t -> p i t", p=P), in_=result[:])
+                rows = out[g * group * P : (g + 1) * group * P, first : first + width].rearrange("(i p) t -> p i t", p=P)
+                piece = width // 2 if step == STEPS - 1 else width
+                for start in range(0, width, piece):
+                    cols = slice(start, start + piece)
+                    nc.scalar.copy(out=free_sb[:, :, cols], in_=free[:, :, cols])
+                    nc.vector.tensor_tensor(out=result[:, :, cols], in0=jam[:, :, cols], in1=free_sb[:, :, cols], op=ALU.max)
+                    nc.sync.dma_start(out=rows[:, :, cols], in_=result[:, :, cols])
 
+        def add_old_and_page(m):
+            banks = [turn_old(m, c * BANK, BANK, CHUNKS + c) for c in range(CHUNKS)]
+            for c in range(CHUNKS):
+                add_page(m, c * BANK, banks[c], False)
+
+        quantize_win(1, slice(0, PASSES))
         h = net_inflow(0)
         for m in range(last):
-            quantize_win(m + 1, slice(0, PASSES))
-            scatter(m, h, 0, [256, 256, 512] if m == 0 else [512, 512])
+            scatter(m, h, 0, [BANK, BANK])
+            if m + 2 < ROW_TILES:
+                quantize_win(m + 2, slice(0, PASSES))
             h = net_inflow(m + 1)
             if m > 0:
-                for c in range(CHUNKS):
-                    add_page(m - 1, c, turn_old(m - 1, c))
-        scatter(last, h, 0, [512, 256])
-        for c in range(CHUNKS):
-            add_page(last - 1, c, turn_old(last - 1, c))
-        banks = [turn_old(last, c) for c in range(CHUNKS)]
-        quantize_wfree()
-        warm_up()
-        scatter(last, h, 768, [256])
-        for c in range(CHUNKS):
-            add_page(last, c, banks[c])
+                add_old_and_page(m - 1)
+        scatter(last, h, 0, [BANK])
+        add_old_and_page(last - 1)
         widths = [256, 256, 512, 512, 512]
         firsts = [sum(widths[:i]) for i in range(len(widths))]
+        banks = [turn_old(last, firsts[i], widths[i], (0, 6, 1, 2, 3)[i]) for i in range(len(widths))]
+        wfree_w = quantize_wfree()
+        warm_up()
+        scatter(last, h, BANK, [BANK // 2, BANK // 2])
+        for i in range(len(widths)):
+            add_page(last, firsts[i], banks[i], i in (1, 2))
         quantized = turn_back_and_quantize(firsts[0], widths[0])
         for i in range(len(widths)):
             current = quantized

@@ -29,6 +29,7 @@ CHUNKS = T2 // BANK
 BLOCKS = BANK // P
 OUT_TILES = N // P
 STEPS = OUT_TILES * CHUNKS
+WARM_PASSES = 4
 
 
 def tile_list_junction_flow_forecast_kernel(
@@ -38,282 +39,268 @@ def tile_list_junction_flow_forecast_kernel(
     with ExitStack() as ctx:
         lists = ctx.enter_context(tc.tile_pool(name="lists", bufs=1))
         keep = ctx.enter_context(tc.tile_pool(name="keep", bufs=1))
-        ring2 = ctx.enter_context(tc.tile_pool(name="ring2", bufs=2))
         ring4 = ctx.enter_context(tc.tile_pool(name="ring4", bufs=4))
         ring8 = ctx.enter_context(tc.tile_pool(name="ring8", bufs=8))
         psum = ctx.enter_context(tc.psum_pool(name="psum", bufs=1))
 
-        def load_scale_rows(queue, plane, dram):
+        def load_scale_rows(plane, dram):
             rows = dram.bitcast(I32).rearrange("a (q r) w -> r q a w", r=4)
             for r in range(4):
-                queue.dma_start(out=plane[r:P:32, :, :], in_=rows[r])
+                nc.gpsimd.dma_start(out=plane[r:P:32, :, :], in_=rows[r])
 
         last = ROW_TILES - 1
         pick = lists.tile([P, S // 16], U16, name="pick")
         place = lists.tile([P, S // 16], U16, name="place")
 
-        tab_w = [keep.tile([P, T], I32, name=f"tab_w{a}") for a in range(PASSES)]
-        tab_s = keep.tile([P, PASSES, T // 4], I32, name="tab_s")
+        tab_s = keep.tile([P, T // 4], I32, name="tab_s", tag="tab_s", align_bytes=64)
+        tab_w = [keep.tile([P, T], I32, name=f"tab_w{a}", tag=("page1", "tab_w1")[a]) for a in range(PASSES)]
         wout_w = keep.tile([P, PASSES, H // 2], I32, name="wout_w", align_bytes=64)
         wout_s = keep.tile([P, PASSES, H // 4], I32, name="wout_s", align_bytes=64)
         wjam_w = keep.tile([P, 1, N // 2], I32, name="wjam_w", align_bytes=64)
         wjam_s = keep.tile([P, 1, N // 4], I32, name="wjam_s", align_bytes=64)
-        win_raw = keep.tile([P, PASSES, PACK, H], F32, name="win_raw")
+        win_first = [keep.tile([P, 1, PACK, P], F32, name=f"win_first{a}") for a in range(PASSES)]
+        win_second = keep.tile([P, PASSES, PACK, P], F32, name="win_second")
+        win_rest = keep.tile([P, PASSES, PACK, 2 * P], F32, name="win_rest")
         wgs_sb = keep.tile([P, S], F32, name="wgs_sb")
-        old_sb = [keep.tile([P, T2], F32, name=f"old{m}") for m in range(ROW_TILES)]
+        old_sb = [
+            keep.tile([P, T2], F32, name=f"old{m}", tag="second2" if m == 0 else f"old{m}", align_bytes=64)
+            for m in range(ROW_TILES)
+        ]
         wfree_raw = keep.tile([P, PACK, N], F32, name="wfree_raw")
-        pages = [keep.tile([P, T2], F32, name=f"page{b}") for b in range(2)]
         ident = keep.tile([P, P], F32, name="ident")
-        perm = keep.tile([P, P], F32, name="perm")
+        v_w = [keep.tile([P, S], U32, name=f"v_w{a}", align_bytes=64) for a in range(PASSES)]
+        picked_s = keep.tile([P, S], U8, name="picked_s")
+        v_s = keep.tile([P, PASSES, S // 4], I32, name="v_s", align_bytes=64)
 
-        nc.vector.memset(wout_s[:], 0)
-        nc.vector.memset(tab_s[:], 0)
-        nc.vector.memset(wjam_s[:], 0)
-        for page in pages:
-            nc.vector.memset(page[:], 0.0)
+        pages = [keep.tile([P, T2], F32, name="page0")]
+        nc.vector.memset(pages[0][:], 0.0)
+        nc.gpsimd.memset(tab_s[:], 0)
+        nc.gpsimd.memset(v_s[:], 0)
+        nc.gpsimd.memset(wout_s[:], 0)
+        load_scale_rows(wout_s, wout_scales)
+        nc.gpsimd.memset(wjam_s[:], 0)
+        load_scale_rows(wjam_s, wjam_scales)
+        make_identity(nc, ident[:])
 
         words = tab_words.rearrange("a p t i -> a p (t i)").bitcast(I32)
         win_rows = win.rearrange("(a p i) c -> a p i c", a=PASSES, i=PACK)
         nc.sync.dma_start(pick[:], offs)
+        for a in range(PASSES):
+            nc.sync.dma_start(out=win_first[a][:, 0], in_=win_rows[a, :, :, 0:P])
+        nc.sync.dma_start(out=tab_s[0:P:4, :], in_=tab_scales.bitcast(I32).rearrange("a q w -> (a q) w"))
         nc.sync.dma_start(out=tab_w[0][:], in_=words[0])
-        load_scale_rows(nc.scalar, wout_s, wout_scales)
-        load_scale_rows(nc.sync, tab_s, tab_scales)
         nc.sync.dma_start(out=wout_w[:], in_=wout_words.bitcast(I32).rearrange("a p w -> p a w"))
-        nc.sync.dma_start(place[:], offs2)
-        nc.sync.dma_start(out=win_raw[:, 0, :, 0:P], in_=win_rows[0, :, :, 0:P])
-        nc.sync.dma_start(out=tab_w[1][:], in_=words[1])
-        nc.sync.dma_start(out=win_raw[:, 1, :, 0:P], in_=win_rows[1, :, :, 0:P])
+        nc.vector.tensor_copy(out=picked_s[:], in_=tab_s[:].bitcast(U8).indirect(pick[:]))
+        for a in range(PASSES):
+            for r in range(4):
+                row = 64 * a + 4 * r
+                nc.sync.dma_start(out=v_s[r:P:32, a, :], in_=picked_s[:].bitcast(I32)[row : 64 * a + 64 : 16, :])
+            cols = slice(a * T // 2, (a + 1) * T // 2)
+            nc.sync.dma_start(out=tab_w[1][:, cols], in_=words[1][:, cols])
+        for a in range(PASSES):
+            nc.sync.dma_start(out=win_second[:, a], in_=win_rows[a, :, :, P : 2 * P])
         nc.sync.dma_start(out=wgs_sb[:], in_=wgs)
-        for cols in (slice(P, 2 * P), slice(2 * P, H)):
-            for a in range(PASSES):
-                nc.sync.dma_start(out=win_raw[:, a, :, cols], in_=win_rows[a, :, :, cols])
+        nc.sync.dma_start(place[:], offs2)
+        for a in range(PASSES):
+            nc.sync.dma_start(out=win_rest[:, a], in_=win_rows[a, :, :, 2 * P : H])
         for m in range(ROW_TILES):
             nc.sync.dma_start(out=old_sb[m][:], in_=old[m * P : (m + 1) * P, :])
-            if m == 1:
+            if m == 0:
                 nc.sync.dma_start(out=wfree_raw[:], in_=wfree.rearrange("(p i) n -> p i n", i=PACK))
         nc.sync.dma_start(out=wjam_w[:], in_=wjam_words.bitcast(I32).rearrange("a p w -> p a w"))
-        load_scale_rows(nc.sync, wjam_s, wjam_scales)
 
-        make_identity(nc, ident[:])
-        nc.scalar.copy(
-            out=perm[:].rearrange("k (u q e) -> k u q e", u=2, e=2),
-            in_=ident[:].rearrange("k (q u e) -> k u q e", u=2, e=2),
-        )
-
-        v_w = keep.tile([P, PASSES, S], U32, name="v_w", align_bytes=64)
-        v_s = keep.tile([P, PASSES, S], U8, name="v_s", align_bytes=64)
-        win_w = keep.tile([P, ROW_TILES, PASSES * P], U32, name="win_w", align_bytes=64)
-        win_s = keep.tile([P, ROW_TILES, PASSES * P], U8, name="win_s", align_bytes=64)
+        win_s = [keep.tile([P, PASSES * P], U8, name=f"win_s{m}", align_bytes=64) for m in range(ROW_TILES)]
         wfree_s = keep.tile([P, N], U8, name="wfree_s", align_bytes=64)
         z_t = [keep.tile([P, BLOCKS, H], BF16, name=f"z_t{c}") for c in range(CHUNKS)]
 
-        def quantize_win(m, passes):
-            raw = win_raw[:, :, :, m * P : (m + 1) * P]
-            count = passes.stop - passes.start
-            cols = slice(passes.start * P, passes.stop * P)
-            slot = f"first_grouped{passes.start}" if m == 0 else h_slot(m - 1, 1)
-            grouped = keep.tile([P, count, P, PACK], BF16, name="win_grouped", tag=slot, align_bytes=64)
-            nc.scalar.copy(out=grouped[:], in_=raw[:, passes].rearrange("p a i c -> p a c i"))
-            nc.vector.quantize_mx(
-                out=win_w[:, m, cols].bitcast(FP8X4),
-                scales=win_s[:, m, cols],
-                in_=grouped[:].rearrange("p a c i -> p (a c i)"),
-            )
-
-        def h_slot(m, g):
-            return f"h{g * (1 + m % 2)}"
-
-        def quantize_wfree():
-            grouped = keep.tile([P, N, PACK], BF16, name="wfree_grouped", align_bytes=64)
-            nc.scalar.copy(out=grouped[:], in_=wfree_raw[:].rearrange("p i n -> p n i"))
-            codes = keep.tile([P, N], U32, name="wfree_w", tag=h_slot(last, 0), align_bytes=64)
-            nc.vector.quantize_mx(
-                out=codes[:].bitcast(FP8X4), scales=wfree_s[:], in_=grouped[:].rearrange("p n i -> p (n i)")
-            )
-            return codes
-
-        nc.vector.tensor_copy(out=v_w[:, 0, :], in_=tab_w[0][:].bitcast(U32).indirect(pick[:]))
-        for a in reversed(range(PASSES)):
-            nc.vector.tensor_copy(out=v_s[:, a, :], in_=tab_s[:, a, :].bitcast(U8).indirect(pick[:]))
+        first_codes = keep.tile([P, PASSES * P], U32, name="first_codes", align_bytes=64)
+        first_grouped = keep.tile([P, PASSES, P, PACK], BF16, name="first_grouped", tag="tab_s", align_bytes=64)
+        for a in range(PASSES):
+            nc.vector.tensor_copy(out=first_grouped[:, a], in_=win_first[a][:, 0].rearrange("p i c -> p c i"))
+        nc.vector.quantize_mx(
+            out=first_codes[:].bitcast(FP8X4), scales=win_s[0][:], in_=first_grouped[:].rearrange("p a c i -> p (a c i)")
+        )
+        nc.vector.tensor_copy(out=v_w[0][:], in_=tab_w[0][:].bitcast(U32).indirect(pick[:]))
+        pages.append(keep.tile([P, T2], F32, name="page1", tag="page1"))
+        nc.vector.memset(pages[1][:], 0.0)
         for g in range(HALVES):
-            quantize_win(0, slice(g, g + 1))
             nc.vector.tensor_copy(
-                out=v_w[:, 1, g * BANK : (g + 1) * BANK],
+                out=v_w[1][:, g * BANK : (g + 1) * BANK],
                 in_=tab_w[1][:].bitcast(U32).indirect(pick[:, g * LIST_COLS : (g + 1) * LIST_COLS]),
             )
 
-        def net_inflow(m):
-            halves = []
-            for g in range(HALVES):
-                cols = slice(g * BANK, (g + 1) * BANK)
-                h = keep.tile([P, BANK], F32, name="h", tag=h_slot(m, g), align_bytes=64)
-                halves.append(h)
-                outflow = psum.tile([P, BANK], F32, name="outflow", tag=f"bank{HALVES + g}")
-                inflow = psum.tile([P, BANK], F32, name="inflow", tag=f"bank{g}")
-                for a in range(PASSES):
-                    nc.tensor.matmul_mx(
-                        out=outflow[:],
-                        lhsT=wout_w[:, a, m * P // 2 : (m + 1) * P // 2].bitcast(U8).bitcast(FP4X4),
-                        lhsT_scale=wout_s[:, a, m * P // 4 : (m + 1) * P // 4].bitcast(U8),
-                        rhs=v_w[:, a, cols].bitcast(FP8X4),
-                        rhs_scale=v_s[:, a, cols],
-                        start=(a == 0),
-                        stop=(a == PASSES - 1),
-                    )
-                for a in range(PASSES):
-                    nc.tensor.matmul_mx(
-                        out=inflow[:],
-                        lhsT=win_w[:, m, a * P : (a + 1) * P].bitcast(FP8X4),
-                        lhsT_scale=win_s[:, m, a * P : (a + 1) * P],
-                        rhs=v_w[:, a, cols].bitcast(FP8X4),
-                        rhs_scale=v_s[:, a, cols],
-                        start=(a == 0),
-                        stop=(a == PASSES - 1),
-                    )
-                out_relu = keep.tile([P, BANK], F32, name="out_relu", tag=f"out_relu{g}", align_bytes=64)
-                nc.scalar.activation(out=out_relu[:], in_=outflow[:], func=ACT.Relu)
-                nc.vector.scalar_tensor_tensor(
-                    out=h[:], in0=inflow[:], scalar=0.0, in1=out_relu[:], op0=ALU.max, op1=ALU.subtract
+        def quantize_weight(raw, scales, grouped_slot, codes_slot):
+            count, width = raw.shape[1], raw.shape[3]
+            grouped = keep.tile([P, count, width, PACK], BF16, name="grouped", tag=grouped_slot, align_bytes=64)
+            nc.scalar.copy(out=grouped[:], in_=raw.rearrange("p a i c -> p a c i"))
+            codes = keep.tile([P, count * width], U32, name="codes", tag=codes_slot, align_bytes=64)
+            nc.vector.quantize_mx(
+                out=codes[:].bitcast(FP8X4), scales=scales[:], in_=grouped[:].rearrange("p a c i -> p (a c i)")
+            )
+            return codes
+
+        def quantize_win(m):
+            raw = win_second[:] if m == 1 else win_rest[:, :, :, (m - 2) * P : (m - 1) * P]
+            return quantize_weight(raw, win_s[m], f"second{m - 1}", f"first{m - 2}")
+
+        def flows(m, g, win_w):
+            cols = slice(g * BANK, (g + 1) * BANK)
+            scale_cols = slice(g * BANK // 4, (g + 1) * BANK // 4)
+            outflow = psum.tile([P, BANK], F32, name="outflow", tag=f"bank{HALVES + g}")
+            inflow = psum.tile([P, BANK], F32, name="inflow", tag=f"bank{g}")
+            for a in range(PASSES):
+                nc.tensor.matmul_mx(
+                    out=outflow[:],
+                    lhsT=wout_w[:, a, m * P // 2 : (m + 1) * P // 2].bitcast(U8).bitcast(FP4X4),
+                    lhsT_scale=wout_s[:, a, m * P // 4 : (m + 1) * P // 4].bitcast(U8),
+                    rhs=v_w[a][:, cols].bitcast(FP8X4),
+                    rhs_scale=v_s[:, a, scale_cols].bitcast(U8),
+                    start=(a == 0),
+                    stop=(a == PASSES - 1),
                 )
-            return halves
+            for a in range(PASSES):
+                nc.tensor.matmul_mx(
+                    out=inflow[:],
+                    lhsT=win_w[:, a * P : (a + 1) * P].bitcast(FP8X4),
+                    lhsT_scale=win_s[m][:, a * P : (a + 1) * P],
+                    rhs=v_w[a][:, cols].bitcast(FP8X4),
+                    rhs_scale=v_s[:, a, scale_cols].bitcast(U8),
+                    start=(a == 0),
+                    stop=(a == PASSES - 1),
+                )
+            out_relu = keep.tile([P, BANK], F32, name="out_relu", tag=f"out_relu{g}")
+            nc.scalar.activation(out=out_relu[:], in_=outflow[:], func=ACT.Relu)
+            return inflow, out_relu
 
-        def scatter(m, halves, first, widths):
-            page = pages[m % 2]
-            for width in widths:
-                cols = slice(first, first + width)
-                window = page[:].indirect(place[:, first // 16 : (first + width) // 16])
-                values = halves[first // BANK][:, first % BANK : first % BANK + width]
-                nc.vector.tensor_tensor(out=window, in0=values, in1=wgs_sb[:, cols], op=ALU.mult)
-                first += width
+        def net_inflow(m, g, inflow, out_relu):
+            h = keep.tile([P, BANK], F32, name="h", tag=f"{('first', 'second')[g]}{m}", align_bytes=64)
+            nc.vector.scalar_tensor_tensor(
+                out=h[:], in0=inflow[:], scalar=0.0, in1=out_relu[:], op0=ALU.max, op1=ALU.subtract
+            )
+            return h
 
-        def warm_up():
-            bank = psum.tile([P, BANK], F32, name="warm_bank", tag="bank7")
-            for n in range(OUT_TILES):
+        def scatter(m, g, h):
+            window = pages[m % 2][:].indirect(place[:, g * LIST_COLS : (g + 1) * LIST_COLS])
+            nc.vector.tensor_tensor(out=window, in0=h[:], in1=wgs_sb[:, g * BANK : (g + 1) * BANK], op=ALU.mult)
+
+        def warm_up(wfree_w):
+            bank = psum.tile([P, BANK], F32, name="warm_bank", tag="bank1")
+            for n in range(WARM_PASSES):
+                cols = slice(n % OUT_TILES * P, (n % OUT_TILES + 1) * P)
                 nc.tensor.matmul_mx(
                     out=bank[:],
-                    lhsT=wfree_w[:, n * P : (n + 1) * P].bitcast(FP8X4),
-                    lhsT_scale=wfree_s[:, n * P : (n + 1) * P],
-                    rhs=v_w[:, 0, 0:BANK].bitcast(FP8X4),
-                    rhs_scale=v_s[:, 0, 0:BANK],
+                    lhsT=wfree_w[:, cols].bitcast(FP8X4),
+                    lhsT_scale=wfree_s[:, cols],
+                    rhs=v_w[0][:, 0:BANK].bitcast(FP8X4),
+                    rhs_scale=v_s[:, 0, 0 : BANK // 4].bitcast(U8),
                     start=True,
                     stop=True,
                 )
 
-        def turn(bank, source, first, opens):
-            blocks = bank.shape[1]
-            for q in range(blocks):
+        def turn(bank, source, c, opens):
+            for q in range(BLOCKS):
                 nc.tensor.matmul(
                     bank[:, q, :],
-                    source[:, first + q * P : first + (q + 1) * P],
-                    perm[:],
+                    source[:, c * BANK + q * P : c * BANK + (q + 1) * P],
+                    ident[:],
                     start=(opens and q == 0),
-                    stop=(not opens and q == blocks - 1),
+                    stop=(not opens and q == BLOCKS - 1),
                     is_transpose=True,
                 )
 
-        def turn_old(m, first, width, bank_number):
-            bank = psum.tile([P, width // P, P], F32, name="z_bank", tag=f"bank{bank_number}")
-            turn(bank, old_sb[m], first, True)
-            return bank
+        def turn_old(m):
+            banks = []
+            for c in range(CHUNKS):
+                bank = psum.tile([P, BLOCKS, P], F32, name="z_bank", tag=f"bank{4 + c}")
+                turn(bank, old_sb[m], c, True)
+                banks.append(bank)
+            return banks
 
-        def add_page(m, first, bank, on_vector):
-            turn(bank, pages[m % 2], first, False)
-            q0 = first % BANK // P
-            rows = z_t[first // BANK][:, q0 : q0 + bank.shape[1], :]
-            dst = rows.rearrange("t q (u m x) -> t (q u) m x", u=2, x=P // 2)[:, :, m, :]
-            src = bank[:].rearrange("t q (u x) -> t (q u) x", u=2)
+        def copy_out(on_vector, dst, src):
             if on_vector:
                 nc.vector.tensor_copy(out=dst, in_=src)
             else:
                 nc.scalar.copy(out=dst, in_=src)
 
-        def turn_back_and_quantize(first, width):
-            c, q0 = first // BANK, first % BANK // P
+        def add_page(m, banks):
+            for c in range(CHUNKS):
+                turn(banks[c], pages[m % 2], c, False)
+                dst = z_t[c][:].rearrange("t q (u m j e) -> t q u m j e", u=2, m=ROW_TILES, e=2)[:, :, :, m, :, :]
+                src = banks[c][:].rearrange("t q (j u e) -> t q u j e", u=2, e=2)
+                copy_out(m == last and c % 2 == 0, dst, src)
+
+        bank_pairs = ((0, 2), (3, 1), (4, 5), (6, 7))
+
+        def turn_back_and_quantize(c):
             pairs = z_t[c][:].rearrange("t q r -> t (q r)").bitcast(F32)
-            grouped = ring2.tile([P, width * PACK], BF16, name="z_grouped", align_bytes=64)
+            grouped = ring4.tile([P, BANK * PACK], BF16, name="z_grouped", align_bytes=64)
             grouped_pairs = grouped[:].bitcast(F32)
-            for b in range(width // (2 * P)):
-                bank = psum.tile([P, 2, 2, P], F32, name="pair_bank", tag=f"bank{4 + (first // (2 * P) + b) % 2}")
+            for b in range(2):
+                bank = psum.tile([P, 2, 2, P], F32, name="pair_bank", tag=f"bank{bank_pairs[c][b]}")
                 for q in range(2):
                     for u in range(2):
-                        word = ((q0 + 2 * b + q) * 2 + u) * P
+                        word = ((2 * b + q) * 2 + u) * P
                         nc.tensor.transpose(bank[:, q, u, :], pairs[:, word : word + P], ident[:])
                 dst = grouped_pairs[:, b * BANK : (b + 1) * BANK].rearrange("p (q t u) -> p q t u", q=2, u=2)
                 src = bank[:].rearrange("p q u t -> p q t u")
-                if first // (2 * P) + b >= 2:
-                    nc.scalar.copy(out=dst, in_=src)
-                else:
-                    nc.vector.tensor_copy(out=dst, in_=src)
-            z_w = ring2.tile([P, width], U32, name="z_w", align_bytes=64)
-            z_s = ring2.tile([P, width], U8, name="z_s", align_bytes=64)
+                copy_out(c < 2 and b == c, dst, src)
+            z_w = ring4.tile([P, BANK], U32, name="z_w", align_bytes=64)
+            z_s = ring4.tile([P, BANK], U8, name="z_s", align_bytes=64)
             nc.vector.quantize_mx(out=z_w[:].bitcast(FP8X4), scales=z_s[:], in_=grouped[:])
             return z_w, z_s
 
-        def forecast(first, width, z_w, z_s):
-            group = BANK // width
-            for g in range(OUT_TILES // group):
-                step = first * OUT_TILES // BANK + g
-                free = psum.tile([P, group, width], F32, name="free", tag=f"bank{step % 2}")
-                jam = psum.tile([P, group, width], F32, name="jam", tag=f"bank{(2, 3, 6, 7)[step % 4]}")
-                for i in range(group):
-                    n = g * group + i
-                    nc.tensor.matmul_mx(
-                        out=free[:, i, :],
-                        lhsT=wfree_w[:, n * P : (n + 1) * P].bitcast(FP8X4),
-                        lhsT_scale=wfree_s[:, n * P : (n + 1) * P],
-                        rhs=z_w[:].bitcast(FP8X4),
-                        rhs_scale=z_s[:],
-                        start=True,
-                        stop=True,
-                    )
-                for i in range(group):
-                    n = g * group + i
-                    nc.tensor.matmul_mx(
-                        out=jam[:, i, :],
-                        lhsT=wjam_w[:, 0, n * P // 2 : (n + 1) * P // 2].bitcast(U8).bitcast(FP4X4),
-                        lhsT_scale=wjam_s[:, 0, n * P // 4 : (n + 1) * P // 4].bitcast(U8),
-                        rhs=z_w[:].bitcast(FP8X4),
-                        rhs_scale=z_s[:],
-                        start=True,
-                        stop=True,
-                    )
-                free_sb = ring4.tile([P, group, width], F32, name="free_sb")
-                result = ring8.tile([P, group, width], F32, name="result")
-                rows = out[g * group * P : (g + 1) * group * P, first : first + width].rearrange("(i p) t -> p i t", p=P)
-                piece = width // 2 if step == STEPS - 1 else width
-                for start in range(0, width, piece):
+        def forecast(c, wfree_w, z_w, z_s):
+            for n in range(OUT_TILES):
+                free = psum.tile([P, BANK], F32, name="free", tag=f"bank{bank_pairs[n][0]}")
+                jam = psum.tile([P, BANK], F32, name="jam", tag=f"bank{bank_pairs[n][1]}")
+                nc.tensor.matmul_mx(
+                    out=free[:],
+                    lhsT=wfree_w[:, n * P : (n + 1) * P].bitcast(FP8X4),
+                    lhsT_scale=wfree_s[:, n * P : (n + 1) * P],
+                    rhs=z_w[:].bitcast(FP8X4),
+                    rhs_scale=z_s[:],
+                    start=True,
+                    stop=True,
+                )
+                nc.tensor.matmul_mx(
+                    out=jam[:],
+                    lhsT=wjam_w[:, 0, n * P // 2 : (n + 1) * P // 2].bitcast(U8).bitcast(FP4X4),
+                    lhsT_scale=wjam_s[:, 0, n * P // 4 : (n + 1) * P // 4].bitcast(U8),
+                    rhs=z_w[:].bitcast(FP8X4),
+                    rhs_scale=z_s[:],
+                    start=True,
+                    stop=True,
+                )
+                free_sb = ring4.tile([P, BANK], F32, name="free_sb")
+                result = ring8.tile([P, BANK], F32, name="result")
+                rows = out[n * P : (n + 1) * P, c * BANK : (c + 1) * BANK]
+                piece = BANK // 2 if c * OUT_TILES + n == STEPS - 1 else BANK
+                for start in range(0, BANK, piece):
                     cols = slice(start, start + piece)
-                    nc.scalar.copy(out=free_sb[:, :, cols], in_=free[:, :, cols])
-                    nc.vector.tensor_tensor(out=result[:, :, cols], in0=jam[:, :, cols], in1=free_sb[:, :, cols], op=ALU.max)
-                    nc.sync.dma_start(out=rows[:, :, cols], in_=result[:, :, cols])
+                    nc.scalar.copy(out=free_sb[:, cols], in_=free[:, cols])
+                    nc.vector.tensor_tensor(out=result[:, cols], in0=jam[:, cols], in1=free_sb[:, cols], op=ALU.max)
+                    nc.sync.dma_start(out=rows[:, cols], in_=result[:, cols])
 
-        def add_old_and_page(m):
-            banks = [turn_old(m, c * BANK, BANK, CHUNKS + c) for c in range(CHUNKS)]
-            for c in range(CHUNKS):
-                add_page(m, c * BANK, banks[c], False)
-
-        quantize_win(1, slice(0, PASSES))
-        h = net_inflow(0)
-        for m in range(last):
-            scatter(m, h, 0, [BANK, BANK])
-            if m + 2 < ROW_TILES:
-                quantize_win(m + 2, slice(0, PASSES))
-            h = net_inflow(m + 1)
+        codes = first_codes
+        banks = None
+        for m in range(ROW_TILES):
+            sums = [flows(m, g, codes) for g in range(HALVES)]
             if m > 0:
-                add_old_and_page(m - 1)
-        scatter(last, h, 0, [BANK])
-        add_old_and_page(last - 1)
-        widths = [256, 256, 512, 512, 512]
-        firsts = [sum(widths[:i]) for i in range(len(widths))]
-        banks = [turn_old(last, firsts[i], widths[i], (0, 6, 1, 2, 3)[i]) for i in range(len(widths))]
-        wfree_w = quantize_wfree()
-        warm_up()
-        scatter(last, h, BANK, [BANK // 2, BANK // 2])
-        for i in range(len(widths)):
-            add_page(last, firsts[i], banks[i], i in (1, 2))
-        quantized = turn_back_and_quantize(firsts[0], widths[0])
-        for i in range(len(widths)):
-            current = quantized
-            if i + 1 < len(widths):
-                quantized = turn_back_and_quantize(firsts[i + 1], widths[i + 1])
-            forecast(firsts[i], widths[i], *current)
+                banks = turn_old(m - 1)
+            if m < last:
+                codes = quantize_win(m + 1)
+            h = [net_inflow(m, g, *sums[g]) for g in range(HALVES)]
+            if m > 0:
+                add_page(m - 1, banks)
+            scatter(m, 0, h[0])
+            if m == last:
+                banks = turn_old(last)
+                codes = quantize_weight(wfree_raw[:].rearrange("p i (a c) -> p a i c", a=1), wfree_s, "wfree", f"first{m}")
+                warm_up(codes)
+            scatter(m, 1, h[1])
+        add_page(last, banks)
+        quantized = [turn_back_and_quantize(c) for c in range(CHUNKS - 1)]
+        forecast(0, codes, *quantized[0])
+        quantized.append(turn_back_and_quantize(CHUNKS - 1))
+        for c in range(1, CHUNKS):
+            forecast(c, codes, *quantized[c])

@@ -43,10 +43,10 @@ def tile_list_junction_flow_forecast_kernel(
         ring8 = ctx.enter_context(tc.tile_pool(name="ring8", bufs=8))
         psum = ctx.enter_context(tc.psum_pool(name="psum", bufs=1))
 
-        def load_scale_rows(plane, dram):
+        def load_scale_rows(queue, plane, dram):
             rows = dram.bitcast(I32).rearrange("a (q r) w -> r q a w", r=4)
             for r in range(4):
-                nc.gpsimd.dma_start(out=plane[r:P:32, :, :], in_=rows[r])
+                queue.dma_start(out=plane[r:P:32, :, :], in_=rows[r])
 
         last = ROW_TILES - 1
         pick = lists.tile([P, S // 16], U16, name="pick")
@@ -58,8 +58,7 @@ def tile_list_junction_flow_forecast_kernel(
         wout_s = keep.tile([P, PASSES, H // 4], I32, name="wout_s", align_bytes=64)
         wjam_w = keep.tile([P, 1, N // 2], I32, name="wjam_w", align_bytes=64)
         wjam_s = keep.tile([P, 1, N // 4], I32, name="wjam_s", align_bytes=64)
-        win_first = [keep.tile([P, 1, PACK, P], F32, name=f"win_first{a}") for a in range(PASSES)]
-        win_second = keep.tile([P, PASSES, PACK, P], F32, name="win_second")
+        win_first = [keep.tile([P, PACK, 2 * P], F32, name=f"win_first{a}") for a in range(PASSES)]
         win_rest = keep.tile([P, PASSES, PACK, 2 * P], F32, name="win_rest")
         wgs_sb = keep.tile([P, S], F32, name="wgs_sb")
         old_sb = [
@@ -72,33 +71,27 @@ def tile_list_junction_flow_forecast_kernel(
         picked_s = keep.tile([P, S], U8, name="picked_s")
         v_s = keep.tile([P, PASSES, S // 4], I32, name="v_s", align_bytes=64)
 
-        pages = [keep.tile([P, T2], F32, name="page0")]
-        nc.vector.memset(pages[0][:], 0.0)
         nc.gpsimd.memset(tab_s[:], 0)
         nc.gpsimd.memset(v_s[:], 0)
         nc.gpsimd.memset(wout_s[:], 0)
-        load_scale_rows(wout_s, wout_scales)
         nc.gpsimd.memset(wjam_s[:], 0)
-        load_scale_rows(wjam_s, wjam_scales)
+        load_scale_rows(nc.gpsimd, wout_s, wout_scales)
         make_identity(nc, ident[:])
 
         words = tab_words.rearrange("a p t i -> a p (t i)").bitcast(I32)
         win_rows = win.rearrange("(a p i) c -> a p i c", a=PASSES, i=PACK)
         nc.sync.dma_start(pick[:], offs)
-        for a in range(PASSES):
-            nc.sync.dma_start(out=win_first[a][:, 0], in_=win_rows[a, :, :, 0:P])
-        nc.sync.dma_start(out=tab_s[0:P:4, :], in_=tab_scales.bitcast(I32).rearrange("a q w -> (a q) w"))
         nc.sync.dma_start(out=tab_w[0][:], in_=words[0])
-        nc.sync.dma_start(out=wout_w[:], in_=wout_words.bitcast(I32).rearrange("a p w -> p a w"))
+        nc.scalar.dma_start(out=tab_s[0:P:4, :], in_=tab_scales.bitcast(I32).rearrange("a q w -> (a q) w"))
         nc.vector.tensor_copy(out=picked_s[:], in_=tab_s[:].bitcast(U8).indirect(pick[:]))
         for a in range(PASSES):
             for r in range(4):
                 row = 64 * a + 4 * r
-                nc.sync.dma_start(out=v_s[r:P:32, a, :], in_=picked_s[:].bitcast(I32)[row : 64 * a + 64 : 16, :])
-            cols = slice(a * T // 2, (a + 1) * T // 2)
-            nc.sync.dma_start(out=tab_w[1][:, cols], in_=words[1][:, cols])
+                nc.scalar.dma_start(out=v_s[r:P:32, a, :], in_=picked_s[:].bitcast(I32)[row : 64 * a + 64 : 16, :])
         for a in range(PASSES):
-            nc.sync.dma_start(out=win_second[:, a], in_=win_rows[a, :, :, P : 2 * P])
+            nc.sync.dma_start(out=win_first[a][:], in_=win_rows[a, :, :, 0 : 2 * P])
+        nc.sync.dma_start(out=wout_w[:], in_=wout_words.bitcast(I32).rearrange("a p w -> p a w"))
+        nc.sync.dma_start(out=tab_w[1][:], in_=words[1])
         nc.sync.dma_start(out=wgs_sb[:], in_=wgs)
         nc.sync.dma_start(place[:], offs2)
         for a in range(PASSES):
@@ -108,19 +101,25 @@ def tile_list_junction_flow_forecast_kernel(
             if m == 0:
                 nc.sync.dma_start(out=wfree_raw[:], in_=wfree.rearrange("(p i) n -> p i n", i=PACK))
         nc.sync.dma_start(out=wjam_w[:], in_=wjam_words.bitcast(I32).rearrange("a p w -> p a w"))
+        load_scale_rows(nc.sync, wjam_s, wjam_scales)
 
-        win_s = [keep.tile([P, PASSES * P], U8, name=f"win_s{m}", align_bytes=64) for m in range(ROW_TILES)]
-        wfree_s = keep.tile([P, N], U8, name="wfree_s", align_bytes=64)
         z_t = [keep.tile([P, BLOCKS, H], BF16, name=f"z_t{c}") for c in range(CHUNKS)]
 
-        first_codes = keep.tile([P, PASSES * P], U32, name="first_codes", align_bytes=64)
-        first_grouped = keep.tile([P, PASSES, P, PACK], BF16, name="first_grouped", tag="tab_s", align_bytes=64)
-        for a in range(PASSES):
-            nc.vector.tensor_copy(out=first_grouped[:, a], in_=win_first[a][:, 0].rearrange("p i c -> p c i"))
-        nc.vector.quantize_mx(
-            out=first_codes[:].bitcast(FP8X4), scales=win_s[0][:], in_=first_grouped[:].rearrange("p a c i -> p (a c i)")
-        )
+        pages = [keep.tile([P, T2], F32, name="page0", tag="tab_s", align_bytes=64)]
+        nc.vector.memset(pages[0][:], 0.0)
         nc.vector.tensor_copy(out=v_w[0][:], in_=tab_w[0][:].bitcast(U32).indirect(pick[:]))
+        first_codes = keep.tile([P, 2, PASSES * P], U32, name="first_codes", align_bytes=64)
+        first_scales = keep.tile([P, 2, PASSES * P], U8, name="first_scales", align_bytes=64)
+        first_grouped = keep.tile([P, 2, PASSES, P, PACK], BF16, name="first_grouped", align_bytes=64)
+        for a in range(PASSES):
+            nc.vector.tensor_copy(
+                out=first_grouped[:, :, a], in_=win_first[a][:].rearrange("p i (m c) -> p m c i", m=2)
+            )
+        nc.vector.quantize_mx(
+            out=first_codes[:].rearrange("p m c -> p (m c)").bitcast(FP8X4),
+            scales=first_scales[:].rearrange("p m c -> p (m c)"),
+            in_=first_grouped[:].rearrange("p m a c i -> p (m a c i)"),
+        )
         pages.append(keep.tile([P, T2], F32, name="page1", tag="page1"))
         nc.vector.memset(pages[1][:], 0.0)
         for g in range(HALVES):
@@ -129,21 +128,23 @@ def tile_list_junction_flow_forecast_kernel(
                 in_=tab_w[1][:].bitcast(U32).indirect(pick[:, g * LIST_COLS : (g + 1) * LIST_COLS]),
             )
 
-        def quantize_weight(raw, scales, grouped_slot, codes_slot):
+        def quantize_weight(raw, grouped_slot, codes_slot):
             count, width = raw.shape[1], raw.shape[3]
+            scales = keep.tile([P, count * width], U8, name="scales", tag=f"scales_{codes_slot}", align_bytes=64)
             grouped = keep.tile([P, count, width, PACK], BF16, name="grouped", tag=grouped_slot, align_bytes=64)
             nc.scalar.copy(out=grouped[:], in_=raw.rearrange("p a i c -> p a c i"))
             codes = keep.tile([P, count * width], U32, name="codes", tag=codes_slot, align_bytes=64)
             nc.vector.quantize_mx(
                 out=codes[:].bitcast(FP8X4), scales=scales[:], in_=grouped[:].rearrange("p a c i -> p (a c i)")
             )
-            return codes
+            return codes[:], scales[:]
 
         def quantize_win(m):
-            raw = win_second[:] if m == 1 else win_rest[:, :, :, (m - 2) * P : (m - 1) * P]
-            return quantize_weight(raw, win_s[m], f"second{m - 1}", f"first{m - 2}")
+            if m < 2:
+                return first_codes[:, m], first_scales[:, m]
+            return quantize_weight(win_rest[:, :, :, (m - 2) * P : (m - 1) * P], f"second{m - 1}", f"first{m - 2}")
 
-        def flows(m, g, win_w):
+        def flows(m, g, win_w, win_s):
             cols = slice(g * BANK, (g + 1) * BANK)
             scale_cols = slice(g * BANK // 4, (g + 1) * BANK // 4)
             outflow = psum.tile([P, BANK], F32, name="outflow", tag=f"bank{HALVES + g}")
@@ -162,7 +163,7 @@ def tile_list_junction_flow_forecast_kernel(
                 nc.tensor.matmul_mx(
                     out=inflow[:],
                     lhsT=win_w[:, a * P : (a + 1) * P].bitcast(FP8X4),
-                    lhsT_scale=win_s[m][:, a * P : (a + 1) * P],
+                    lhsT_scale=win_s[:, a * P : (a + 1) * P],
                     rhs=v_w[a][:, cols].bitcast(FP8X4),
                     rhs_scale=v_s[:, a, scale_cols].bitcast(U8),
                     start=(a == 0),
@@ -183,7 +184,7 @@ def tile_list_junction_flow_forecast_kernel(
             window = pages[m % 2][:].indirect(place[:, g * LIST_COLS : (g + 1) * LIST_COLS])
             nc.vector.tensor_tensor(out=window, in0=h[:], in1=wgs_sb[:, g * BANK : (g + 1) * BANK], op=ALU.mult)
 
-        def warm_up(wfree_w):
+        def warm_up(wfree_w, wfree_s):
             bank = psum.tile([P, BANK], F32, name="warm_bank", tag="bank1")
             for n in range(WARM_PASSES):
                 cols = slice(n % OUT_TILES * P, (n % OUT_TILES + 1) * P)
@@ -249,7 +250,7 @@ def tile_list_junction_flow_forecast_kernel(
             nc.vector.quantize_mx(out=z_w[:].bitcast(FP8X4), scales=z_s[:], in_=grouped[:])
             return z_w, z_s
 
-        def forecast(c, wfree_w, z_w, z_s):
+        def forecast(c, wfree_w, wfree_s, z_w, z_s):
             for n in range(OUT_TILES):
                 free = psum.tile([P, BANK], F32, name="free", tag=f"bank{bank_pairs[n][0]}")
                 jam = psum.tile([P, BANK], F32, name="jam", tag=f"bank{bank_pairs[n][1]}")
@@ -281,10 +282,10 @@ def tile_list_junction_flow_forecast_kernel(
                     nc.vector.tensor_tensor(out=result[:, cols], in0=jam[:, cols], in1=free_sb[:, cols], op=ALU.max)
                     nc.sync.dma_start(out=rows[:, cols], in_=result[:, cols])
 
-        codes = first_codes
+        codes = quantize_win(0)
         banks = None
         for m in range(ROW_TILES):
-            sums = [flows(m, g, codes) for g in range(HALVES)]
+            sums = [flows(m, g, *codes) for g in range(HALVES)]
             if m > 0:
                 banks = turn_old(m - 1)
             if m < last:
@@ -295,12 +296,12 @@ def tile_list_junction_flow_forecast_kernel(
             scatter(m, 0, h[0])
             if m == last:
                 banks = turn_old(last)
-                codes = quantize_weight(wfree_raw[:].rearrange("p i (a c) -> p a i c", a=1), wfree_s, "wfree", f"first{m}")
-                warm_up(codes)
+                codes = quantize_weight(wfree_raw[:].rearrange("p i (a c) -> p a i c", a=1), "wfree", f"first{m}")
+                warm_up(*codes)
             scatter(m, 1, h[1])
         add_page(last, banks)
         quantized = [turn_back_and_quantize(c) for c in range(CHUNKS - 1)]
-        forecast(0, codes, *quantized[0])
+        forecast(0, *codes, *quantized[0])
         quantized.append(turn_back_and_quantize(CHUNKS - 1))
         for c in range(1, CHUNKS):
-            forecast(c, codes, *quantized[c])
+            forecast(c, *codes, *quantized[c])

@@ -52,7 +52,7 @@ def tile_list_junction_flow_forecast_kernel(
         pick = lists.tile([P, S // 16], U16, name="pick")
         place = lists.tile([P, S // 16], U16, name="place")
 
-        tab_s = keep.tile([P, T // 4], I32, name="tab_s", tag="tab_s", align_bytes=64)
+        tab_s = keep.tile([P, T // 4], I32, name="tab_s")
         tab_w = [keep.tile([P, T], I32, name=f"tab_w{a}", tag=("page1", "tab_w1")[a]) for a in range(PASSES)]
         wout_w = keep.tile([P, PASSES, H // 2], I32, name="wout_w", align_bytes=64)
         wout_s = keep.tile([P, PASSES, H // 4], I32, name="wout_s", align_bytes=64)
@@ -71,7 +71,9 @@ def tile_list_junction_flow_forecast_kernel(
         picked_s = keep.tile([P, S], U8, name="picked_s")
         v_s = keep.tile([P, PASSES, S // 4], I32, name="v_s", align_bytes=64)
 
-        nc.gpsimd.memset(tab_s[:], 0)
+        pages = [keep.tile([P, T2], F32, name="page0")]
+        nc.vector.memset(tab_s[:], 0)
+        nc.vector.memset(pages[0][:], 0.0)
         nc.gpsimd.memset(v_s[:], 0)
         nc.gpsimd.memset(wout_s[:], 0)
         nc.gpsimd.memset(wjam_s[:], 0)
@@ -81,17 +83,17 @@ def tile_list_junction_flow_forecast_kernel(
         words = tab_words.rearrange("a p t i -> a p (t i)").bitcast(I32)
         win_rows = win.rearrange("(a p i) c -> a p i c", a=PASSES, i=PACK)
         nc.sync.dma_start(pick[:], offs)
-        nc.sync.dma_start(out=tab_w[0][:], in_=words[0])
-        nc.scalar.dma_start(out=tab_s[0:P:4, :], in_=tab_scales.bitcast(I32).rearrange("a q w -> (a q) w"))
+        for a in range(PASSES):
+            nc.sync.dma_start(out=win_first[a][:], in_=win_rows[a, :, :, 0 : 2 * P])
+        nc.sync.dma_start(out=wout_w[:], in_=wout_words.bitcast(I32).rearrange("a p w -> p a w"))
+        nc.sync.dma_start(out=tab_s[0:P:4, :], in_=tab_scales.bitcast(I32).rearrange("a q w -> (a q) w"))
+        for a in range(PASSES):
+            nc.sync.dma_start(out=tab_w[a][:], in_=words[a])
         nc.vector.tensor_copy(out=picked_s[:], in_=tab_s[:].bitcast(U8).indirect(pick[:]))
         for a in range(PASSES):
             for r in range(4):
                 row = 64 * a + 4 * r
                 nc.scalar.dma_start(out=v_s[r:P:32, a, :], in_=picked_s[:].bitcast(I32)[row : 64 * a + 64 : 16, :])
-        for a in range(PASSES):
-            nc.sync.dma_start(out=win_first[a][:], in_=win_rows[a, :, :, 0 : 2 * P])
-        nc.sync.dma_start(out=wout_w[:], in_=wout_words.bitcast(I32).rearrange("a p w -> p a w"))
-        nc.sync.dma_start(out=tab_w[1][:], in_=words[1])
         nc.sync.dma_start(out=wgs_sb[:], in_=wgs)
         nc.sync.dma_start(place[:], offs2)
         for a in range(PASSES):
@@ -105,8 +107,6 @@ def tile_list_junction_flow_forecast_kernel(
 
         z_t = [keep.tile([P, BLOCKS, H], BF16, name=f"z_t{c}") for c in range(CHUNKS)]
 
-        pages = [keep.tile([P, T2], F32, name="page0", tag="tab_s", align_bytes=64)]
-        nc.vector.memset(pages[0][:], 0.0)
         nc.vector.tensor_copy(out=v_w[0][:], in_=tab_w[0][:].bitcast(U32).indirect(pick[:]))
         first_codes = keep.tile([P, 2, PASSES * P], U32, name="first_codes", align_bytes=64)
         first_scales = keep.tile([P, 2, PASSES * P], U8, name="first_scales", align_bytes=64)

@@ -85,7 +85,6 @@ def tile_list_junction_flow_forecast_kernel(
         nc.sync.dma_start(pick[:], offs)
         for a in range(PASSES):
             nc.sync.dma_start(out=win_first[a][:], in_=win_rows[a, :, :, 0 : 2 * P])
-        nc.sync.dma_start(out=wout_w[:], in_=wout_words.bitcast(I32).rearrange("a p w -> p a w"))
         nc.sync.dma_start(out=tab_s[0:P:4, :], in_=tab_scales.bitcast(I32).rearrange("a q w -> (a q) w"))
         for a in range(PASSES):
             nc.sync.dma_start(out=tab_w[a][:], in_=words[a])
@@ -94,6 +93,7 @@ def tile_list_junction_flow_forecast_kernel(
             for r in range(4):
                 row = 64 * a + 4 * r
                 nc.scalar.dma_start(out=v_s[r:P:32, a, :], in_=picked_s[:].bitcast(I32)[row : 64 * a + 64 : 16, :])
+        nc.sync.dma_start(out=wout_w[:], in_=wout_words.bitcast(I32).rearrange("a p w -> p a w"))
         nc.sync.dma_start(out=wgs_sb[:], in_=wgs)
         nc.sync.dma_start(place[:], offs2)
         for a in range(PASSES):

@@ -72,12 +72,10 @@ def tile_list_junction_flow_forecast_kernel(
         v_s = keep.tile([P, PASSES, S // 4], I32, name="v_s", align_bytes=64)
 
         pages = [keep.tile([P, T2], F32, name="page0")]
-        nc.vector.memset(tab_s[:], 0)
+        for plane in (wout_s, tab_s, v_s, wjam_s):
+            nc.vector.memset(plane[:], 0)
         nc.vector.memset(pages[0][:], 0.0)
-        nc.gpsimd.memset(v_s[:], 0)
-        nc.gpsimd.memset(wout_s[:], 0)
-        nc.gpsimd.memset(wjam_s[:], 0)
-        load_scale_rows(nc.gpsimd, wout_s, wout_scales)
+        load_scale_rows(nc.scalar, wout_s, wout_scales)
         make_identity(nc, ident[:])
 
         words = tab_words.rearrange("a p t i -> a p (t i)").bitcast(I32)

@@ -61,10 +61,7 @@ def tile_list_junction_flow_forecast_kernel(
         win_first = [keep.tile([P, PACK, 2 * P], F32, name=f"win_first{a}") for a in range(PASSES)]
         win_rest = keep.tile([P, PASSES, PACK, 2 * P], F32, name="win_rest")
         wgs_sb = keep.tile([P, S], F32, name="wgs_sb")
-        old_sb = [
-            keep.tile([P, T2], F32, name=f"old{m}", tag="second2" if m == 0 else f"old{m}", align_bytes=64)
-            for m in range(ROW_TILES)
-        ]
+        old_sb = [keep.tile([P, T2], F32, name=f"old{m}") for m in range(ROW_TILES)]
         wfree_raw = keep.tile([P, PACK, N], F32, name="wfree_raw")
         ident = keep.tile([P, P], F32, name="ident")
         v_w = [keep.tile([P, S], U32, name=f"v_w{a}", align_bytes=64) for a in range(PASSES)]
@@ -75,6 +72,8 @@ def tile_list_junction_flow_forecast_kernel(
         for plane in (wout_s, tab_s, v_s, wjam_s):
             nc.vector.memset(plane[:], 0)
         nc.vector.memset(pages[0][:], 0.0)
+        third_page = keep.tile([P, T2], F32, name="page2")
+        nc.vector.memset(third_page[:], 0.0)
         load_scale_rows(nc.scalar, wout_s, wout_scales)
         make_identity(nc, ident[:])
 
@@ -120,33 +119,36 @@ def tile_list_junction_flow_forecast_kernel(
         )
         pages.append(keep.tile([P, T2], F32, name="page1", tag="page1"))
         nc.vector.memset(pages[1][:], 0.0)
+        pages.append(third_page)
         for g in range(HALVES):
             nc.vector.tensor_copy(
                 out=v_w[1][:, g * BANK : (g + 1) * BANK],
                 in_=tab_w[1][:].bitcast(U32).indirect(pick[:, g * LIST_COLS : (g + 1) * LIST_COLS]),
             )
 
-        def quantize_weight(raw, grouped_slot, codes_slot):
-            count, width = raw.shape[1], raw.shape[3]
-            scales = keep.tile([P, count * width], U8, name="scales", tag=f"scales_{codes_slot}", align_bytes=64)
-            grouped = keep.tile([P, count, width, PACK], BF16, name="grouped", tag=grouped_slot, align_bytes=64)
-            nc.scalar.copy(out=grouped[:], in_=raw.rearrange("p a i c -> p a c i"))
-            codes = keep.tile([P, count * width], U32, name="codes", tag=codes_slot, align_bytes=64)
-            nc.vector.quantize_mx(
-                out=codes[:].bitcast(FP8X4), scales=scales[:], in_=grouped[:].rearrange("p a c i -> p (a c i)")
-            )
-            return codes[:], scales[:]
+        def group_rest():
+            grouped = keep.tile([P, 2, PASSES, P, PACK], BF16, name="rest_grouped", tag="diff2", align_bytes=64)
+            for a in range(PASSES):
+                nc.scalar.copy(out=grouped[:, :, a], in_=win_rest[:, a].rearrange("p i (m c) -> p m c i", m=2))
+            return grouped[:].rearrange("p m a c i -> p (m a c i)")
 
-        def quantize_win(m):
-            if m < 2:
-                return first_codes[:, m], first_scales[:, m]
-            return quantize_weight(win_rest[:, :, :, (m - 2) * P : (m - 1) * P], f"second{m - 1}", f"first{m - 2}")
+        def group_wfree():
+            grouped = keep.tile([P, N, PACK], BF16, name="wfree_grouped", align_bytes=64)
+            nc.scalar.copy(out=grouped[:], in_=wfree_raw[:].rearrange("p i c -> p c i"))
+            return grouped[:].rearrange("p c i -> p (c i)")
+
+        def quantize_weight(grouped, codes_slot):
+            scales = keep.tile([P, BANK], U8, name="scales", tag=f"scales_{codes_slot}", align_bytes=64)
+            codes = keep.tile([P, BANK], U32, name="codes", tag=codes_slot, align_bytes=64)
+            nc.vector.quantize_mx(out=codes[:].bitcast(FP8X4), scales=scales[:], in_=grouped)
+            return codes[:], scales[:]
 
         def flows(m, g, win_w, win_s):
             cols = slice(g * BANK, (g + 1) * BANK)
             scale_cols = slice(g * BANK // 4, (g + 1) * BANK // 4)
-            outflow = psum.tile([P, BANK], F32, name="outflow", tag=f"bank{HALVES + g}")
-            inflow = psum.tile([P, BANK], F32, name="inflow", tag=f"bank{g}")
+            outflow = psum.tile([P, BANK], F32, name="outflow", tag=f"bank{2 * (m % 2)}")
+            inflow = psum.tile([P, BANK], F32, name="inflow", tag=f"bank{2 * (m % 2) + 1}")
+            first = (m % 2) * PASSES * P
             for a in range(PASSES):
                 nc.tensor.matmul_mx(
                     out=outflow[:],
@@ -160,30 +162,46 @@ def tile_list_junction_flow_forecast_kernel(
             for a in range(PASSES):
                 nc.tensor.matmul_mx(
                     out=inflow[:],
-                    lhsT=win_w[:, a * P : (a + 1) * P].bitcast(FP8X4),
-                    lhsT_scale=win_s[:, a * P : (a + 1) * P],
+                    lhsT=win_w[:, first + a * P : first + (a + 1) * P].bitcast(FP8X4),
+                    lhsT_scale=win_s[:, first + a * P : first + (a + 1) * P],
                     rhs=v_w[a][:, cols].bitcast(FP8X4),
                     rhs_scale=v_s[:, a, scale_cols].bitcast(U8),
                     start=(a == 0),
                     stop=(a == PASSES - 1),
                 )
-            out_relu = keep.tile([P, BANK], F32, name="out_relu", tag=f"out_relu{g}")
-            nc.scalar.activation(out=out_relu[:], in_=outflow[:], func=ACT.Relu)
-            return inflow, out_relu
+            return inflow, outflow
 
-        def net_inflow(m, g, inflow, out_relu):
-            h = keep.tile([P, BANK], F32, name="h", tag=f"{('first', 'second')[g]}{m}", align_bytes=64)
+        def relu(name, m, bank):
+            tile = keep.tile([P, BANK], F32, name=name, tag=f"{name}{m % 2}")
+            nc.scalar.activation(out=tile[:], in_=bank[:], func=ACT.Relu)
+            return tile
+
+        def weighted_on_vector(m, g, inflow, outflow, diff_slot):
+            out_relu = relu("out_relu", m, outflow)
+            diff = keep.tile([P, BANK], F32, name="diff", tag=diff_slot, align_bytes=64)
             nc.vector.scalar_tensor_tensor(
-                out=h[:], in0=inflow[:], scalar=0.0, in1=out_relu[:], op0=ALU.max, op1=ALU.subtract
+                out=diff[:], in0=inflow[:], scalar=0.0, in1=out_relu[:], op0=ALU.max, op1=ALU.subtract
             )
+            h = ring4.tile([P, BANK], F32, name="h")
+            nc.vector.tensor_tensor(out=h[:], in0=diff[:], in1=wgs_sb[:, g * BANK : (g + 1) * BANK], op=ALU.mult)
+            return h
+
+        def relus(m, inflow, outflow):
+            return relu("out_relu", m, outflow), relu("in_relu", m, inflow)
+
+        def weighted_on_gpsimd(g, out_relu, in_relu, diff_slot):
+            diff = keep.tile([P, BANK], F32, name="diff", tag=diff_slot, align_bytes=64)
+            nc.gpsimd.tensor_tensor(out=diff[:], in0=in_relu[:], in1=out_relu[:], op=ALU.subtract)
+            h = ring4.tile([P, BANK], F32, name="h")
+            nc.gpsimd.tensor_tensor(out=h[:], in0=diff[:], in1=wgs_sb[:, g * BANK : (g + 1) * BANK], op=ALU.mult)
             return h
 
         def scatter(m, g, h):
-            window = pages[m % 2][:].indirect(place[:, g * LIST_COLS : (g + 1) * LIST_COLS])
-            nc.vector.tensor_tensor(out=window, in0=h[:], in1=wgs_sb[:, g * BANK : (g + 1) * BANK], op=ALU.mult)
+            window = pages[m % 3][:].indirect(place[:, g * LIST_COLS : (g + 1) * LIST_COLS])
+            nc.vector.tensor_copy(out=window, in_=h[:])
 
         def warm_up(wfree_w, wfree_s):
-            bank = psum.tile([P, BANK], F32, name="warm_bank", tag="bank1")
+            bank = psum.tile([P, BANK], F32, name="warm_bank", tag="bank4")
             for n in range(WARM_PASSES):
                 cols = slice(n % OUT_TILES * P, (n % OUT_TILES + 1) * P)
                 nc.tensor.matmul_mx(
@@ -210,7 +228,7 @@ def tile_list_junction_flow_forecast_kernel(
         def turn_old(m):
             banks = []
             for c in range(CHUNKS):
-                bank = psum.tile([P, BLOCKS, P], F32, name="z_bank", tag=f"bank{4 + c}")
+                bank = psum.tile([P, BLOCKS, P], F32, name="z_bank", tag=f"bank{(0 if m == last else 4) + c}")
                 turn(bank, old_sb[m], c, True)
                 banks.append(bank)
             return banks
@@ -223,12 +241,12 @@ def tile_list_junction_flow_forecast_kernel(
 
         def add_page(m, banks):
             for c in range(CHUNKS):
-                turn(banks[c], pages[m % 2], c, False)
+                turn(banks[c], pages[m % 3], c, False)
                 dst = z_t[c][:].rearrange("t q (u m j e) -> t q u m j e", u=2, m=ROW_TILES, e=2)[:, :, :, m, :, :]
                 src = banks[c][:].rearrange("t q (j u e) -> t q u j e", u=2, e=2)
                 copy_out(m == last and c % 2 == 0, dst, src)
 
-        bank_pairs = ((0, 2), (3, 1), (4, 5), (6, 7))
+        bank_pairs = ((4, 5), (6, 7), (0, 1), (2, 3))
 
         def turn_back_and_quantize(c):
             pairs = z_t[c][:].rearrange("t q r -> t (q r)").bitcast(F32)
@@ -280,23 +298,34 @@ def tile_list_junction_flow_forecast_kernel(
                     nc.vector.tensor_tensor(out=result[:, cols], in0=jam[:, cols], in1=free_sb[:, cols], op=ALU.max)
                     nc.sync.dma_start(out=rows[:, cols], in_=result[:, cols])
 
-        codes = quantize_win(0)
-        banks = None
-        for m in range(ROW_TILES):
-            sums = [flows(m, g, *codes) for g in range(HALVES)]
-            if m > 0:
-                banks = turn_old(m - 1)
-            if m < last:
-                codes = quantize_win(m + 1)
-            h = [net_inflow(m, g, *sums[g]) for g in range(HALVES)]
-            if m > 0:
-                add_page(m - 1, banks)
-            scatter(m, 0, h[0])
-            if m == last:
-                banks = turn_old(last)
-                codes = quantize_weight(wfree_raw[:].rearrange("p i (a c) -> p a i c", a=1), "wfree", f"first{m}")
-                warm_up(*codes)
-            scatter(m, 1, h[1])
+        first = (first_codes[:].rearrange("p m c -> p (m c)"), first_scales[:].rearrange("p m c -> p (m c)"))
+        sums = [flows(m, 0, *first) for m in range(2)]
+        h00 = weighted_on_vector(0, 0, *sums[0], "diff0")
+        h10 = weighted_on_gpsimd(0, *relus(1, *sums[1]), "diff0")
+        scatter(0, 0, h00)
+        h01 = weighted_on_gpsimd(1, *relus(0, *flows(0, 1, *first)), "diff1")
+        scatter(1, 0, h10)
+        grouped = group_rest()
+        r11 = relus(1, *flows(1, 1, *first))
+        rest = quantize_weight(grouped, "diff1")
+        scatter(0, 1, h01)
+        h11 = weighted_on_gpsimd(1, *r11, "diff2")
+        h20 = weighted_on_gpsimd(0, *relus(2, *flows(2, 0, *rest)), "diff0")
+        h30 = weighted_on_gpsimd(0, *relus(3, *flows(3, 0, *rest)), "diff2")
+        grouped = group_wfree()
+        scatter(1, 1, h11)
+        scatter(2, 0, h20)
+        h21 = weighted_on_gpsimd(1, *relus(2, *flows(2, 1, *rest)), "diff0")
+        add_page(0, turn_old(0))
+        scatter(3, 0, h30)
+        h31 = weighted_on_gpsimd(1, *relus(3, *flows(3, 1, *rest)), "diff2")
+        add_page(1, turn_old(1))
+        scatter(2, 1, h21)
+        codes = quantize_weight(grouped, "diff2")
+        scatter(3, 1, h31)
+        banks = turn_old(last)
+        add_page(2, turn_old(2))
+        warm_up(*codes)
         add_page(last, banks)
         quantized = [turn_back_and_quantize(c) for c in range(CHUNKS - 1)]
         forecast(0, *codes, *quantized[0])

@@ -327,8 +327,6 @@ def tile_list_junction_flow_forecast_kernel(
         add_page(2, turn_old(2))
         warm_up(*codes)
         add_page(last, banks)
-        quantized = [turn_back_and_quantize(c) for c in range(CHUNKS - 1)]
-        forecast(0, *codes, *quantized[0])
-        quantized.append(turn_back_and_quantize(CHUNKS - 1))
-        for c in range(1, CHUNKS):
+        quantized = [turn_back_and_quantize(c) for c in range(CHUNKS)]
+        for c in range(CHUNKS):
             forecast(c, *codes, *quantized[c])

@@ -147,18 +147,8 @@ def tile_list_junction_flow_forecast_kernel(
             cols = slice(g * BANK, (g + 1) * BANK)
             scale_cols = slice(g * BANK // 4, (g + 1) * BANK // 4)
             outflow = psum.tile([P, BANK], F32, name="outflow", tag=f"bank{2 * (m % 2)}")
-            inflow = psum.tile([P, BANK], F32, name="inflow", tag=f"bank{2 * (m % 2) + 1}")
+            inflow = psum.tile([P, BANK], F32, name="inflow", tag=f"bank{1 if (m, g) == (1, 0) else 2 * (m % 2) + 1}")
             first = (m % 2) * PASSES * P
-            for a in range(PASSES):
-                nc.tensor.matmul_mx(
-                    out=outflow[:],
-                    lhsT=wout_w[:, a, m * P // 2 : (m + 1) * P // 2].bitcast(U8).bitcast(FP4X4),
-                    lhsT_scale=wout_s[:, a, m * P // 4 : (m + 1) * P // 4].bitcast(U8),
-                    rhs=v_w[a][:, cols].bitcast(FP8X4),
-                    rhs_scale=v_s[:, a, scale_cols].bitcast(U8),
-                    start=(a == 0),
-                    stop=(a == PASSES - 1),
-                )
             for a in range(PASSES):
                 nc.tensor.matmul_mx(
                     out=inflow[:],
@@ -169,29 +159,44 @@ def tile_list_junction_flow_forecast_kernel(
                     start=(a == 0),
                     stop=(a == PASSES - 1),
                 )
+            for a in range(PASSES):
+                nc.tensor.matmul_mx(
+                    out=outflow[:],
+                    lhsT=wout_w[:, a, m * P // 2 : (m + 1) * P // 2].bitcast(U8).bitcast(FP4X4),
+                    lhsT_scale=wout_s[:, a, m * P // 4 : (m + 1) * P // 4].bitcast(U8),
+                    rhs=v_w[a][:, cols].bitcast(FP8X4),
+                    rhs_scale=v_s[:, a, scale_cols].bitcast(U8),
+                    start=(a == 0),
+                    stop=(a == PASSES - 1),
+                )
             return inflow, outflow
 
         def relu(name, m, bank):
-            tile = keep.tile([P, BANK], F32, name=name, tag=f"{name}{m % 2}")
+            tile = keep.tile([P, BANK], F32, name=name, tag=f"{name}{m % 2}", align_bytes=64)
             nc.scalar.activation(out=tile[:], in_=bank[:], func=ACT.Relu)
             return tile
 
         def weighted_on_vector(m, g, inflow, outflow, diff_slot):
-            out_relu = relu("out_relu", m, outflow)
+            in_relu = relu("in_relu", m, inflow)
             diff = keep.tile([P, BANK], F32, name="diff", tag=diff_slot, align_bytes=64)
             nc.vector.scalar_tensor_tensor(
-                out=diff[:], in0=inflow[:], scalar=0.0, in1=out_relu[:], op0=ALU.max, op1=ALU.subtract
+                out=diff[:], in0=outflow[:], scalar=0.0, in1=in_relu[:], op0=ALU.max, op1=ALU.subtract
             )
             h = ring4.tile([P, BANK], F32, name="h")
-            nc.vector.tensor_tensor(out=h[:], in0=diff[:], in1=wgs_sb[:, g * BANK : (g + 1) * BANK], op=ALU.mult)
+            nc.vector.scalar_tensor_tensor(
+                out=h[:], in0=diff[:], scalar=-1.0, in1=wgs_sb[:, g * BANK : (g + 1) * BANK], op0=ALU.mult, op1=ALU.mult
+            )
             return h
 
         def relus(m, inflow, outflow):
             return relu("out_relu", m, outflow), relu("in_relu", m, inflow)
 
-        def weighted_on_gpsimd(g, out_relu, in_relu, diff_slot):
+        def subtract(out_relu, in_relu, diff_slot):
             diff = keep.tile([P, BANK], F32, name="diff", tag=diff_slot, align_bytes=64)
             nc.gpsimd.tensor_tensor(out=diff[:], in0=in_relu[:], in1=out_relu[:], op=ALU.subtract)
+            return diff
+
+        def weigh(g, diff):
             h = ring4.tile([P, BANK], F32, name="h")
             nc.gpsimd.tensor_tensor(out=h[:], in0=diff[:], in1=wgs_sb[:, g * BANK : (g + 1) * BANK], op=ALU.mult)
             return h
@@ -199,6 +204,10 @@ def tile_list_junction_flow_forecast_kernel(
         def scatter(m, g, h):
             window = pages[m % 3][:].indirect(place[:, g * LIST_COLS : (g + 1) * LIST_COLS])
             nc.vector.tensor_copy(out=window, in_=h[:])
+
+        def weigh_and_scatter(m, g, diff):
+            window = pages[m % 3][:].indirect(place[:, g * LIST_COLS : (g + 1) * LIST_COLS])
+            nc.vector.tensor_tensor(out=window, in0=diff[:], in1=wgs_sb[:, g * BANK : (g + 1) * BANK], op=ALU.mult)
 
         def warm_up(wfree_w, wfree_s):
             bank = psum.tile([P, BANK], F32, name="warm_bank", tag="bank4")
@@ -299,30 +308,32 @@ def tile_list_junction_flow_forecast_kernel(
                     nc.sync.dma_start(out=rows[:, cols], in_=result[:, cols])
 
         first = (first_codes[:].rearrange("p m c -> p (m c)"), first_scales[:].rearrange("p m c -> p (m c)"))
-        sums = [flows(m, 0, *first) for m in range(2)]
+        sums = [flows(0, 0, *first)]
         h00 = weighted_on_vector(0, 0, *sums[0], "diff0")
-        h10 = weighted_on_gpsimd(0, *relus(1, *sums[1]), "diff0")
+        h10 = weigh(0, subtract(*relus(1, *flows(1, 0, *first)), "diff0"))
         scatter(0, 0, h00)
-        h01 = weighted_on_gpsimd(1, *relus(0, *flows(0, 1, *first)), "diff1")
+        h01 = weigh(1, subtract(*relus(0, *flows(0, 1, *first)), "diff1"))
         scatter(1, 0, h10)
         grouped = group_rest()
         r11 = relus(1, *flows(1, 1, *first))
         rest = quantize_weight(grouped, "diff1")
         scatter(0, 1, h01)
-        h11 = weighted_on_gpsimd(1, *r11, "diff2")
-        h20 = weighted_on_gpsimd(0, *relus(2, *flows(2, 0, *rest)), "diff0")
-        h30 = weighted_on_gpsimd(0, *relus(3, *flows(3, 0, *rest)), "diff2")
+        h11 = weigh(1, subtract(*r11, "diff2"))
+        d20 = subtract(*relus(2, *flows(2, 0, *rest)), "diff0")
+        d30 = subtract(*relus(3, *flows(3, 0, *rest)), "diff2")
+        h20 = weigh(0, d20)
         grouped = group_wfree()
         scatter(1, 1, h11)
         scatter(2, 0, h20)
-        h21 = weighted_on_gpsimd(1, *relus(2, *flows(2, 1, *rest)), "diff0")
+        h30 = weigh(0, d30)
+        d21 = subtract(*relus(2, *flows(2, 1, *rest)), "diff0")
         add_page(0, turn_old(0))
         scatter(3, 0, h30)
-        h31 = weighted_on_gpsimd(1, *relus(3, *flows(3, 1, *rest)), "diff2")
+        d31 = subtract(*relus(3, *flows(3, 1, *rest)), "diff2")
         add_page(1, turn_old(1))
-        scatter(2, 1, h21)
-        codes = quantize_weight(grouped, "diff2")
-        scatter(3, 1, h31)
+        weigh_and_scatter(2, 1, d21)
+        codes = quantize_weight(grouped, "in_relu1")
+        weigh_and_scatter(3, 1, d31)
         banks = turn_old(last)
         add_page(2, turn_old(2))
         warm_up(*codes)

@@ -19,17 +19,18 @@ ACT = mybir.ActivationFunctionType
 
 P = 128
 PACK = 4
-K_PASS = P * PACK
-PASSES = K // K_PASS
+PASSES = K // (P * PACK)
 BANK = 512
 HALVES = S // BANK
 LIST_COLS = BANK // 16
 ROW_TILES = H // P
+PAIR = 2
+PAGES = 3
 CHUNKS = T2 // BANK
 BLOCKS = BANK // P
 OUT_TILES = N // P
 STEPS = OUT_TILES * CHUNKS
-WARM_PASSES = 4
+WARM_EARLY, WARM_LATE = 4, 2
 
 
 def tile_list_junction_flow_forecast_kernel(
@@ -58,8 +59,8 @@ def tile_list_junction_flow_forecast_kernel(
         wout_s = keep.tile([P, PASSES, H // 4], I32, name="wout_s", align_bytes=64)
         wjam_w = keep.tile([P, 1, N // 2], I32, name="wjam_w", align_bytes=64)
         wjam_s = keep.tile([P, 1, N // 4], I32, name="wjam_s", align_bytes=64)
-        win_first = [keep.tile([P, PACK, 2 * P], F32, name=f"win_first{a}") for a in range(PASSES)]
-        win_rest = keep.tile([P, PASSES, PACK, 2 * P], F32, name="win_rest")
+        win_first = [keep.tile([P, PACK, PAIR * P], F32, name=f"win_first{a}") for a in range(PASSES)]
+        win_rest = keep.tile([P, PASSES, PACK, PAIR * P], F32, name="win_rest")
         wgs_sb = keep.tile([P, S], F32, name="wgs_sb")
         old_sb = [keep.tile([P, T2], F32, name=f"old{m}") for m in range(ROW_TILES)]
         wfree_raw = keep.tile([P, PACK, N], F32, name="wfree_raw")
@@ -68,12 +69,12 @@ def tile_list_junction_flow_forecast_kernel(
         picked_s = keep.tile([P, S], U8, name="picked_s")
         v_s = keep.tile([P, PASSES, S // 4], I32, name="v_s", align_bytes=64)
 
-        pages = [keep.tile([P, T2], F32, name="page0")]
+        page0 = keep.tile([P, T2], F32, name="page0")
         for plane in (wout_s, tab_s, v_s, wjam_s):
             nc.vector.memset(plane[:], 0)
-        nc.vector.memset(pages[0][:], 0.0)
-        third_page = keep.tile([P, T2], F32, name="page2")
-        nc.vector.memset(third_page[:], 0.0)
+        nc.vector.memset(page0[:], 0.0)
+        page2 = keep.tile([P, T2], F32, name="page2")
+        nc.vector.memset(page2[:], 0.0)
         load_scale_rows(nc.scalar, wout_s, wout_scales)
         make_identity(nc, ident[:])
 
@@ -81,7 +82,7 @@ def tile_list_junction_flow_forecast_kernel(
         win_rows = win.rearrange("(a p i) c -> a p i c", a=PASSES, i=PACK)
         nc.sync.dma_start(pick[:], offs)
         for a in range(PASSES):
-            nc.sync.dma_start(out=win_first[a][:], in_=win_rows[a, :, :, 0 : 2 * P])
+            nc.sync.dma_start(out=win_first[a][:], in_=win_rows[a, :, :, 0 : PAIR * P])
         nc.sync.dma_start(out=tab_s[0:P:4, :], in_=tab_scales.bitcast(I32).rearrange("a q w -> (a q) w"))
         for a in range(PASSES):
             nc.sync.dma_start(out=tab_w[a][:], in_=words[a])
@@ -94,42 +95,42 @@ def tile_list_junction_flow_forecast_kernel(
         nc.sync.dma_start(out=wgs_sb[:], in_=wgs)
         nc.sync.dma_start(place[:], offs2)
         for a in range(PASSES):
-            nc.sync.dma_start(out=win_rest[:, a], in_=win_rows[a, :, :, 2 * P : H])
-        for m in range(ROW_TILES):
+            nc.sync.dma_start(out=win_rest[:, a], in_=win_rows[a, :, :, PAIR * P : H])
+        nc.sync.dma_start(out=old_sb[0][:], in_=old[0:P, :])
+        nc.sync.dma_start(out=wfree_raw[:], in_=wfree.rearrange("(p i) n -> p i n", i=PACK))
+        for m in range(1, ROW_TILES):
             nc.sync.dma_start(out=old_sb[m][:], in_=old[m * P : (m + 1) * P, :])
-            if m == 0:
-                nc.sync.dma_start(out=wfree_raw[:], in_=wfree.rearrange("(p i) n -> p i n", i=PACK))
         nc.sync.dma_start(out=wjam_w[:], in_=wjam_words.bitcast(I32).rearrange("a p w -> p a w"))
         load_scale_rows(nc.sync, wjam_s, wjam_scales)
 
         z_t = [keep.tile([P, BLOCKS, H], BF16, name=f"z_t{c}") for c in range(CHUNKS)]
 
         nc.vector.tensor_copy(out=v_w[0][:], in_=tab_w[0][:].bitcast(U32).indirect(pick[:]))
-        first_codes = keep.tile([P, 2, PASSES * P], U32, name="first_codes", align_bytes=64)
-        first_scales = keep.tile([P, 2, PASSES * P], U8, name="first_scales", align_bytes=64)
-        first_grouped = keep.tile([P, 2, PASSES, P, PACK], BF16, name="first_grouped", align_bytes=64)
+        first_codes = keep.tile([P, PAIR * PASSES * P], U32, name="first_codes", align_bytes=64)
+        first_scales = keep.tile([P, PAIR * PASSES * P], U8, name="first_scales", align_bytes=64)
+        first_grouped = keep.tile([P, PAIR, PASSES, P, PACK], BF16, name="first_grouped", align_bytes=64)
         for a in range(PASSES):
             nc.vector.tensor_copy(
-                out=first_grouped[:, :, a], in_=win_first[a][:].rearrange("p i (m c) -> p m c i", m=2)
+                out=first_grouped[:, :, a], in_=win_first[a][:].rearrange("p i (m c) -> p m c i", m=PAIR)
             )
         nc.vector.quantize_mx(
-            out=first_codes[:].rearrange("p m c -> p (m c)").bitcast(FP8X4),
-            scales=first_scales[:].rearrange("p m c -> p (m c)"),
+            out=first_codes[:].bitcast(FP8X4),
+            scales=first_scales[:],
             in_=first_grouped[:].rearrange("p m a c i -> p (m a c i)"),
         )
-        pages.append(keep.tile([P, T2], F32, name="page1", tag="page1"))
-        nc.vector.memset(pages[1][:], 0.0)
-        pages.append(third_page)
+        page1 = keep.tile([P, T2], F32, name="page1", tag="page1")
+        nc.vector.memset(page1[:], 0.0)
+        pages = (page0, page1, page2)
         for g in range(HALVES):
             nc.vector.tensor_copy(
                 out=v_w[1][:, g * BANK : (g + 1) * BANK],
                 in_=tab_w[1][:].bitcast(U32).indirect(pick[:, g * LIST_COLS : (g + 1) * LIST_COLS]),
             )
 
-        def group_rest():
-            grouped = keep.tile([P, 2, PASSES, P, PACK], BF16, name="rest_grouped", tag="diff2", align_bytes=64)
+        def group_rest(slot):
+            grouped = keep.tile([P, PAIR, PASSES, P, PACK], BF16, name="rest_grouped", tag=slot, align_bytes=64)
             for a in range(PASSES):
-                nc.scalar.copy(out=grouped[:, :, a], in_=win_rest[:, a].rearrange("p i (m c) -> p m c i", m=2))
+                nc.scalar.copy(out=grouped[:, :, a], in_=win_rest[:, a].rearrange("p i (m c) -> p m c i", m=PAIR))
             return grouped[:].rearrange("p m a c i -> p (m a c i)")
 
         def group_wfree():
@@ -137,23 +138,23 @@ def tile_list_junction_flow_forecast_kernel(
             nc.scalar.copy(out=grouped[:], in_=wfree_raw[:].rearrange("p i c -> p c i"))
             return grouped[:].rearrange("p c i -> p (c i)")
 
-        def quantize_weight(grouped, codes_slot):
-            scales = keep.tile([P, BANK], U8, name="scales", tag=f"scales_{codes_slot}", align_bytes=64)
-            codes = keep.tile([P, BANK], U32, name="codes", tag=codes_slot, align_bytes=64)
+        def quantize_weight(grouped, slot):
+            scales = keep.tile([P, BANK], U8, name="scales", tag=f"scales_{slot}", align_bytes=64)
+            codes = keep.tile([P, BANK], U32, name="codes", tag=slot, align_bytes=64)
             nc.vector.quantize_mx(out=codes[:].bitcast(FP8X4), scales=scales[:], in_=grouped)
             return codes[:], scales[:]
 
-        def flows(m, g, win_w, win_s):
+        def flows(m, g, win_w, win_s, inflow_bank):
             cols = slice(g * BANK, (g + 1) * BANK)
             scale_cols = slice(g * BANK // 4, (g + 1) * BANK // 4)
-            outflow = psum.tile([P, BANK], F32, name="outflow", tag=f"bank{2 * (m % 2)}")
-            inflow = psum.tile([P, BANK], F32, name="inflow", tag=f"bank{1 if (m, g) == (1, 0) else 2 * (m % 2) + 1}")
-            first = (m % 2) * PASSES * P
+            outflow = psum.tile([P, BANK], F32, name="outflow", tag=f"bank{2 * (m % PAIR)}")
+            inflow = psum.tile([P, BANK], F32, name="inflow", tag=f"bank{inflow_bank}")
             for a in range(PASSES):
+                weight_cols = slice((m % PAIR * PASSES + a) * P, (m % PAIR * PASSES + a + 1) * P)
                 nc.tensor.matmul_mx(
                     out=inflow[:],
-                    lhsT=win_w[:, first + a * P : first + (a + 1) * P].bitcast(FP8X4),
-                    lhsT_scale=win_s[:, first + a * P : first + (a + 1) * P],
+                    lhsT=win_w[:, weight_cols].bitcast(FP8X4),
+                    lhsT_scale=win_s[:, weight_cols],
                     rhs=v_w[a][:, cols].bitcast(FP8X4),
                     rhs_scale=v_s[:, a, scale_cols].bitcast(U8),
                     start=(a == 0),
@@ -172,51 +173,53 @@ def tile_list_junction_flow_forecast_kernel(
             return inflow, outflow
 
         def relu(name, m, bank):
-            tile = keep.tile([P, BANK], F32, name=name, tag=f"{name}{m % 2}", align_bytes=64)
+            tile = keep.tile([P, BANK], F32, name=name, tag=f"{name}{m % PAIR}", align_bytes=64)
             nc.scalar.activation(out=tile[:], in_=bank[:], func=ACT.Relu)
             return tile
 
-        def weighted_on_vector(m, g, inflow, outflow, diff_slot):
-            in_relu = relu("in_relu", m, inflow)
-            diff = keep.tile([P, BANK], F32, name="diff", tag=diff_slot, align_bytes=64)
-            nc.vector.scalar_tensor_tensor(
-                out=diff[:], in0=outflow[:], scalar=0.0, in1=in_relu[:], op0=ALU.max, op1=ALU.subtract
-            )
-            h = ring4.tile([P, BANK], F32, name="h")
-            nc.vector.scalar_tensor_tensor(
-                out=h[:], in0=diff[:], scalar=-1.0, in1=wgs_sb[:, g * BANK : (g + 1) * BANK], op0=ALU.mult, op1=ALU.mult
-            )
-            return h
-
-        def relus(m, inflow, outflow):
+        def relus(m, g, win_w, win_s, inflow_bank):
+            inflow, outflow = flows(m, g, win_w, win_s, inflow_bank)
             return relu("out_relu", m, outflow), relu("in_relu", m, inflow)
 
-        def subtract(out_relu, in_relu, diff_slot):
-            diff = keep.tile([P, BANK], F32, name="diff", tag=diff_slot, align_bytes=64)
-            nc.gpsimd.tensor_tensor(out=diff[:], in0=in_relu[:], in1=out_relu[:], op=ALU.subtract)
-            return diff
+        def first_weighted(win_w, win_s, slot):
+            inflow, outflow = flows(0, 0, win_w, win_s, 1)
+            in_relu = relu("in_relu", 0, inflow)
+            minus_h = keep.tile([P, BANK], F32, name="minus_h", tag=slot, align_bytes=64)
+            nc.vector.scalar_tensor_tensor(
+                out=minus_h[:], in0=outflow[:], scalar=0.0, in1=in_relu[:], op0=ALU.max, op1=ALU.subtract
+            )
+            weighted = ring4.tile([P, BANK], F32, name="weighted")
+            nc.vector.scalar_tensor_tensor(
+                out=weighted[:], in0=minus_h[:], scalar=-1.0, in1=wgs_sb[:, 0:BANK], op0=ALU.mult, op1=ALU.mult
+            )
+            return weighted
 
-        def weigh(g, diff):
-            h = ring4.tile([P, BANK], F32, name="h")
-            nc.gpsimd.tensor_tensor(out=h[:], in0=diff[:], in1=wgs_sb[:, g * BANK : (g + 1) * BANK], op=ALU.mult)
+        def subtract(out_relu, in_relu, slot):
+            h = keep.tile([P, BANK], F32, name="h", tag=slot, align_bytes=64)
+            nc.gpsimd.tensor_tensor(out=h[:], in0=in_relu[:], in1=out_relu[:], op=ALU.subtract)
             return h
 
-        def scatter(m, g, h):
-            window = pages[m % 3][:].indirect(place[:, g * LIST_COLS : (g + 1) * LIST_COLS])
-            nc.vector.tensor_copy(out=window, in_=h[:])
+        def weigh(g, h):
+            weighted = ring4.tile([P, BANK], F32, name="weighted")
+            nc.gpsimd.tensor_tensor(out=weighted[:], in0=h[:], in1=wgs_sb[:, g * BANK : (g + 1) * BANK], op=ALU.mult)
+            return weighted
 
-        def weigh_and_scatter(m, g, diff):
-            window = pages[m % 3][:].indirect(place[:, g * LIST_COLS : (g + 1) * LIST_COLS])
-            nc.vector.tensor_tensor(out=window, in0=diff[:], in1=wgs_sb[:, g * BANK : (g + 1) * BANK], op=ALU.mult)
+        def window(m, g):
+            return pages[m % PAGES][:].indirect(place[:, g * LIST_COLS : (g + 1) * LIST_COLS])
 
-        def warm_up(wfree_w, wfree_s):
-            bank = psum.tile([P, BANK], F32, name="warm_bank", tag="bank4")
-            for n in range(WARM_PASSES):
-                cols = slice(n % OUT_TILES * P, (n % OUT_TILES + 1) * P)
+        def scatter(m, g, weighted):
+            nc.vector.tensor_copy(out=window(m, g), in_=weighted[:])
+
+        def weigh_and_scatter(m, g, h):
+            nc.vector.tensor_tensor(out=window(m, g), in0=h[:], in1=wgs_sb[:, g * BANK : (g + 1) * BANK], op=ALU.mult)
+
+        def warm_up(passes, slot, win_w, win_s):
+            bank = psum.tile([P, BANK], F32, name="warm_bank", tag=slot)
+            for n in range(passes):
                 nc.tensor.matmul_mx(
                     out=bank[:],
-                    lhsT=wfree_w[:, cols].bitcast(FP8X4),
-                    lhsT_scale=wfree_s[:, cols],
+                    lhsT=win_w[:, n * P : (n + 1) * P].bitcast(FP8X4),
+                    lhsT_scale=win_s[:, n * P : (n + 1) * P],
                     rhs=v_w[0][:, 0:BANK].bitcast(FP8X4),
                     rhs_scale=v_s[:, 0, 0 : BANK // 4].bitcast(U8),
                     start=True,
@@ -250,7 +253,7 @@ def tile_list_junction_flow_forecast_kernel(
 
         def add_page(m, banks):
             for c in range(CHUNKS):
-                turn(banks[c], pages[m % 3], c, False)
+                turn(banks[c], pages[m % PAGES], c, False)
                 dst = z_t[c][:].rearrange("t q (u m j e) -> t q u m j e", u=2, m=ROW_TILES, e=2)[:, :, :, m, :, :]
                 src = banks[c][:].rearrange("t q (j u e) -> t q u j e", u=2, e=2)
                 copy_out(m == last and c % 2 == 0, dst, src)
@@ -265,8 +268,8 @@ def tile_list_junction_flow_forecast_kernel(
                 bank = psum.tile([P, 2, 2, P], F32, name="pair_bank", tag=f"bank{bank_pairs[c][b]}")
                 for q in range(2):
                     for u in range(2):
-                        word = ((2 * b + q) * 2 + u) * P
-                        nc.tensor.transpose(bank[:, q, u, :], pairs[:, word : word + P], ident[:])
+                        start = ((2 * b + q) * 2 + u) * P
+                        nc.tensor.transpose(bank[:, q, u, :], pairs[:, start : start + P], ident[:])
                 dst = grouped_pairs[:, b * BANK : (b + 1) * BANK].rearrange("p (q t u) -> p q t u", q=2, u=2)
                 src = bank[:].rearrange("p q u t -> p q t u")
                 copy_out(c < 2 and b == c, dst, src)
@@ -307,37 +310,38 @@ def tile_list_junction_flow_forecast_kernel(
                     nc.vector.tensor_tensor(out=result[:, cols], in0=jam[:, cols], in1=free_sb[:, cols], op=ALU.max)
                     nc.sync.dma_start(out=rows[:, cols], in_=result[:, cols])
 
-        first = (first_codes[:].rearrange("p m c -> p (m c)"), first_scales[:].rearrange("p m c -> p (m c)"))
-        sums = [flows(0, 0, *first)]
-        h00 = weighted_on_vector(0, 0, *sums[0], "diff0")
-        h10 = weigh(0, subtract(*relus(1, *flows(1, 0, *first)), "diff0"))
-        scatter(0, 0, h00)
-        h01 = weigh(1, subtract(*relus(0, *flows(0, 1, *first)), "diff1"))
-        scatter(1, 0, h10)
-        grouped = group_rest()
-        r11 = relus(1, *flows(1, 1, *first))
-        rest = quantize_weight(grouped, "diff1")
-        scatter(0, 1, h01)
-        h11 = weigh(1, subtract(*r11, "diff2"))
-        d20 = subtract(*relus(2, *flows(2, 0, *rest)), "diff0")
-        d30 = subtract(*relus(3, *flows(3, 0, *rest)), "diff2")
-        h20 = weigh(0, d20)
-        grouped = group_wfree()
-        scatter(1, 1, h11)
-        scatter(2, 0, h20)
-        h30 = weigh(0, d30)
-        d21 = subtract(*relus(2, *flows(2, 1, *rest)), "diff0")
+        first = (first_codes[:], first_scales[:])
+        weighted00 = first_weighted(*first, "h_a")
+        weighted10 = weigh(0, subtract(*relus(1, 0, *first, 1), "h_a"))
+        scatter(0, 0, weighted00)
+        weighted01 = weigh(1, subtract(*relus(0, 1, *first, 1), "h_b"))
+        scatter(1, 0, weighted10)
+        rest_grouped = group_rest("h_c")
+        relus11 = relus(1, 1, *first, 3)
+        rest = quantize_weight(rest_grouped, "h_b")
+        scatter(0, 1, weighted01)
+        weighted11 = weigh(1, subtract(*relus11, "h_c"))
+        h20 = subtract(*relus(2, 0, *rest, 1), "h_a")
+        h30 = subtract(*relus(3, 0, *rest, 3), "h_c")
+        weighted20 = weigh(0, h20)
+        wfree_grouped = group_wfree()
+        scatter(1, 1, weighted11)
+        scatter(2, 0, weighted20)
+        weighted30 = weigh(0, h30)
+        h21 = subtract(*relus(2, 1, *rest, 1), "h_a")
         add_page(0, turn_old(0))
-        scatter(3, 0, h30)
-        d31 = subtract(*relus(3, *flows(3, 1, *rest)), "diff2")
+        scatter(3, 0, weighted30)
+        h31 = subtract(*relus(3, 1, *rest, 3), "h_c")
         add_page(1, turn_old(1))
-        weigh_and_scatter(2, 1, d21)
-        codes = quantize_weight(grouped, "in_relu1")
-        weigh_and_scatter(3, 1, d31)
-        banks = turn_old(last)
+        last_banks = turn_old(last)
+        warm_up(WARM_EARLY, "bank7", *rest)
+        weigh_and_scatter(2, 1, h21)
+        weigh_and_scatter(3, 1, h31)
+        wfree_codes = quantize_weight(wfree_grouped, "in_relu1")
         add_page(2, turn_old(2))
-        warm_up(*codes)
-        add_page(last, banks)
+        warm_up(WARM_LATE, "bank4", *rest)
+        add_page(last, last_banks)
+
         quantized = [turn_back_and_quantize(c) for c in range(CHUNKS)]
         for c in range(CHUNKS):
-            forecast(c, *codes, *quantized[c])
+            forecast(c, *wfree_codes, *quantized[c])

@@ -21,8 +21,8 @@ P = 128
 PACK = 4
 PASSES = K // (P * PACK)
 BANK = 512
-HALVES = S // BANK
-LIST_COLS = BANK // 16
+QUARTER = BANK // 2
+HALF_0, HALF_1, QUARTER_0, QUARTER_1 = (0, BANK), (BANK, BANK), (0, QUARTER), (QUARTER, QUARTER)
 ROW_TILES = H // P
 PAIR = 2
 PAGES = 3
@@ -41,7 +41,6 @@ def tile_list_junction_flow_forecast_kernel(
         lists = ctx.enter_context(tc.tile_pool(name="lists", bufs=1))
         keep = ctx.enter_context(tc.tile_pool(name="keep", bufs=1))
         ring4 = ctx.enter_context(tc.tile_pool(name="ring4", bufs=4))
-        ring8 = ctx.enter_context(tc.tile_pool(name="ring8", bufs=8))
         psum = ctx.enter_context(tc.psum_pool(name="psum", bufs=1))
 
         def load_scale_rows(queue, plane, dram):
@@ -54,13 +53,13 @@ def tile_list_junction_flow_forecast_kernel(
         place = lists.tile([P, S // 16], U16, name="place")
 
         tab_s = keep.tile([P, T // 4], I32, name="tab_s")
-        tab_w = [keep.tile([P, T], I32, name=f"tab_w{a}", tag=("page1", "tab_w1")[a]) for a in range(PASSES)]
+        tab_w = [keep.tile([P, T], I32, name=f"tab_w{a}", tag=f"tab_w{a}") for a in range(PASSES)]
         wout_w = keep.tile([P, PASSES, H // 2], I32, name="wout_w", align_bytes=64)
         wout_s = keep.tile([P, PASSES, H // 4], I32, name="wout_s", align_bytes=64)
         wjam_w = keep.tile([P, 1, N // 2], I32, name="wjam_w", align_bytes=64)
         wjam_s = keep.tile([P, 1, N // 4], I32, name="wjam_s", align_bytes=64)
         win_first = [keep.tile([P, PACK, PAIR * P], F32, name=f"win_first{a}") for a in range(PASSES)]
-        win_rest = keep.tile([P, PASSES, PACK, PAIR * P], F32, name="win_rest")
+        win_rest = keep.tile([P, PASSES, PACK, PAIR * P], F32, name="win_rest", align_bytes=64)
         wgs_sb = keep.tile([P, S], F32, name="wgs_sb")
         old_sb = [keep.tile([P, T2], F32, name=f"old{m}") for m in range(ROW_TILES)]
         wfree_raw = keep.tile([P, PACK, N], F32, name="wfree_raw")
@@ -69,63 +68,66 @@ def tile_list_junction_flow_forecast_kernel(
         picked_s = keep.tile([P, S], U8, name="picked_s")
         v_s = keep.tile([P, PASSES, S // 4], I32, name="v_s", align_bytes=64)
 
-        page0 = keep.tile([P, T2], F32, name="page0")
-        for plane in (wout_s, tab_s, v_s, wjam_s):
-            nc.vector.memset(plane[:], 0)
-        nc.vector.memset(page0[:], 0.0)
-        page2 = keep.tile([P, T2], F32, name="page2")
-        nc.vector.memset(page2[:], 0.0)
+
+        def entries(piece, per=1):
+            return slice(piece[0] // per, (piece[0] + piece[1]) // per)
+
+        for plane in (wout_s[:], tab_s[32:64], tab_s[64:P], v_s[:]):
+            nc.vector.memset(plane, 0)
         load_scale_rows(nc.scalar, wout_s, wout_scales)
         make_identity(nc, ident[:])
 
         words = tab_words.rearrange("a p t i -> a p (t i)").bitcast(I32)
         win_rows = win.rearrange("(a p i) c -> a p i c", a=PASSES, i=PACK)
         nc.sync.dma_start(pick[:], offs)
-        for a in range(PASSES):
-            nc.sync.dma_start(out=win_first[a][:], in_=win_rows[a, :, :, 0 : PAIR * P])
-        nc.sync.dma_start(out=tab_s[0:P:4, :], in_=tab_scales.bitcast(I32).rearrange("a q w -> (a q) w"))
-        for a in range(PASSES):
-            nc.sync.dma_start(out=tab_w[a][:], in_=words[a])
+        nc.sync.dma_start(out=tab_s[0:32, :], in_=tab_scales.bitcast(I32).rearrange("a q w -> (a q) w"))
         nc.vector.tensor_copy(out=picked_s[:], in_=tab_s[:].bitcast(U8).indirect(pick[:]))
         for a in range(PASSES):
-            for r in range(4):
-                row = 64 * a + 4 * r
-                nc.scalar.dma_start(out=v_s[r:P:32, a, :], in_=picked_s[:].bitcast(I32)[row : 64 * a + 64 : 16, :])
+            for half in range(2):
+                cols = slice(half * T // 2, (half + 1) * T // 2)
+                nc.sync.dma_start(out=tab_w[a][:, cols], in_=words[a][:, cols])
+                if a == PASSES - 1:
+                    for r in range(4):
+                        rows = picked_s[:].bitcast(I32)[16 * half + r : 16 * half + 16 : 4, :]
+                        nc.sync.dma_start(out=v_s[r:P:32, half, :], in_=rows)
+        nc.vector.tensor_copy(out=v_w[0][:], in_=tab_w[0][:].bitcast(U32).indirect(pick[:]))
+        nc.vector.memset(wjam_s[:], 0)
+        pages = [keep.tile([P, T2], F32, name="page", tag=slot) for slot in ("page0", "tab_s", "tab_w0")]
+        for page in pages:
+            nc.vector.memset(page[:], 0.0)
         nc.sync.dma_start(out=wout_w[:], in_=wout_words.bitcast(I32).rearrange("a p w -> p a w"))
+        for a in range(PASSES):
+            nc.sync.dma_start(out=win_first[a][:], in_=win_rows[a, :, :, 0 : PAIR * P])
         nc.sync.dma_start(out=wgs_sb[:], in_=wgs)
         nc.sync.dma_start(place[:], offs2)
         for a in range(PASSES):
             nc.sync.dma_start(out=win_rest[:, a], in_=win_rows[a, :, :, PAIR * P : H])
-        nc.sync.dma_start(out=old_sb[0][:], in_=old[0:P, :])
         nc.sync.dma_start(out=wfree_raw[:], in_=wfree.rearrange("(p i) n -> p i n", i=PACK))
-        for m in range(1, ROW_TILES):
+        for m in range(ROW_TILES):
             nc.sync.dma_start(out=old_sb[m][:], in_=old[m * P : (m + 1) * P, :])
         nc.sync.dma_start(out=wjam_w[:], in_=wjam_words.bitcast(I32).rearrange("a p w -> p a w"))
         load_scale_rows(nc.sync, wjam_s, wjam_scales)
 
         z_t = [keep.tile([P, BLOCKS, H], BF16, name=f"z_t{c}") for c in range(CHUNKS)]
 
-        nc.vector.tensor_copy(out=v_w[0][:], in_=tab_w[0][:].bitcast(U32).indirect(pick[:]))
-        first_codes = keep.tile([P, PAIR * PASSES * P], U32, name="first_codes", align_bytes=64)
-        first_scales = keep.tile([P, PAIR * PASSES * P], U8, name="first_scales", align_bytes=64)
-        first_grouped = keep.tile([P, PAIR, PASSES, P, PACK], BF16, name="first_grouped", align_bytes=64)
+        for half in (HALF_0, HALF_1):
+            nc.vector.tensor_copy(
+                out=v_w[1][:, entries(half)], in_=tab_w[1][:].bitcast(U32).indirect(pick[:, entries(half, 16)])
+            )
+        first = {}
         for a in range(PASSES):
-            nc.vector.tensor_copy(
-                out=first_grouped[:, :, a], in_=win_first[a][:].rearrange("p i (m c) -> p m c i", m=PAIR)
-            )
-        nc.vector.quantize_mx(
-            out=first_codes[:].bitcast(FP8X4),
-            scales=first_scales[:],
-            in_=first_grouped[:].rearrange("p m a c i -> p (m a c i)"),
-        )
-        page1 = keep.tile([P, T2], F32, name="page1", tag="page1")
-        nc.vector.memset(page1[:], 0.0)
-        pages = (page0, page1, page2)
-        for g in range(HALVES):
-            nc.vector.tensor_copy(
-                out=v_w[1][:, g * BANK : (g + 1) * BANK],
-                in_=tab_w[1][:].bitcast(U32).indirect(pick[:, g * LIST_COLS : (g + 1) * LIST_COLS]),
-            )
+            grouped = [keep.tile([P, P, PACK], BF16, name=f"first_grouped{a}{m}", align_bytes=64) for m in range(PAIR)]
+            for m in range(PAIR):
+                nc.vector.tensor_copy(
+                    out=grouped[m][:], in_=win_first[a][:, :, m * P : (m + 1) * P].rearrange("p i c -> p c i")
+                )
+            for m in range(PAIR):
+                codes = keep.tile([P, P], U32, name=f"first_codes{a}{m}", align_bytes=64)
+                scales = keep.tile([P, P], U8, name=f"first_scales{a}{m}", align_bytes=64)
+                nc.vector.quantize_mx(
+                    out=codes[:].bitcast(FP8X4), scales=scales[:], in_=grouped[m][:].rearrange("p c i -> p (c i)")
+                )
+                first[m, a] = (codes[:], scales[:])
 
         def group_rest(slot):
             grouped = keep.tile([P, PAIR, PASSES, P, PACK], BF16, name="rest_grouped", tag=slot, align_bytes=64)
@@ -144,74 +146,61 @@ def tile_list_junction_flow_forecast_kernel(
             nc.vector.quantize_mx(out=codes[:].bitcast(FP8X4), scales=scales[:], in_=grouped)
             return codes[:], scales[:]
 
-        def flows(m, g, win_w, win_s, inflow_bank):
-            cols = slice(g * BANK, (g + 1) * BANK)
-            scale_cols = slice(g * BANK // 4, (g + 1) * BANK // 4)
-            outflow = psum.tile([P, BANK], F32, name="outflow", tag=f"bank{2 * (m % PAIR)}")
-            inflow = psum.tile([P, BANK], F32, name="inflow", tag=f"bank{inflow_bank}")
+        def product(name, piece, bank, weights):
+            total = psum.tile([P, piece[1]], F32, name=name, tag=f"bank{bank}")
             for a in range(PASSES):
-                weight_cols = slice((m % PAIR * PASSES + a) * P, (m % PAIR * PASSES + a + 1) * P)
                 nc.tensor.matmul_mx(
-                    out=inflow[:],
-                    lhsT=win_w[:, weight_cols].bitcast(FP8X4),
-                    lhsT_scale=win_s[:, weight_cols],
-                    rhs=v_w[a][:, cols].bitcast(FP8X4),
-                    rhs_scale=v_s[:, a, scale_cols].bitcast(U8),
+                    out=total[:],
+                    lhsT=weights[a][0],
+                    lhsT_scale=weights[a][1],
+                    rhs=v_w[a][:, entries(piece)].bitcast(FP8X4),
+                    rhs_scale=v_s[:, a, entries(piece, 4)].bitcast(U8),
                     start=(a == 0),
                     stop=(a == PASSES - 1),
                 )
-            for a in range(PASSES):
-                nc.tensor.matmul_mx(
-                    out=outflow[:],
-                    lhsT=wout_w[:, a, m * P // 2 : (m + 1) * P // 2].bitcast(U8).bitcast(FP4X4),
-                    lhsT_scale=wout_s[:, a, m * P // 4 : (m + 1) * P // 4].bitcast(U8),
-                    rhs=v_w[a][:, cols].bitcast(FP8X4),
-                    rhs_scale=v_s[:, a, scale_cols].bitcast(U8),
-                    start=(a == 0),
-                    stop=(a == PASSES - 1),
-                )
-            return inflow, outflow
+            return total
 
-        def relu(name, m, bank):
-            tile = keep.tile([P, BANK], F32, name=name, tag=f"{name}{m % PAIR}", align_bytes=64)
+        def inflow(blocks, m, piece, bank):
+            return product("inflow", piece, bank, [(blocks[m, a][0].bitcast(FP8X4), blocks[m, a][1]) for a in range(PASSES)])
+
+        def outflow(m, piece, bank):
+            weights = [
+                (
+                    wout_w[:, a, m * P // 2 : (m + 1) * P // 2].bitcast(U8).bitcast(FP4X4),
+                    wout_s[:, a, m * P // 4 : (m + 1) * P // 4].bitcast(U8),
+                )
+                for a in range(PASSES)
+            ]
+            return product("outflow", piece, bank, weights)
+
+        def relu(bank, slot):
+            tile = keep.tile([P, BANK], F32, name="relu", tag=slot, align_bytes=64)
             nc.scalar.activation(out=tile[:], in_=bank[:], func=ACT.Relu)
             return tile
 
-        def relus(m, g, win_w, win_s, inflow_bank):
-            inflow, outflow = flows(m, g, win_w, win_s, inflow_bank)
-            return relu("out_relu", m, outflow), relu("in_relu", m, inflow)
-
-        def first_weighted(win_w, win_s, slot):
-            inflow, outflow = flows(0, 0, win_w, win_s, 1)
-            in_relu = relu("in_relu", 0, inflow)
-            minus_h = keep.tile([P, BANK], F32, name="minus_h", tag=slot, align_bytes=64)
-            nc.vector.scalar_tensor_tensor(
-                out=minus_h[:], in0=outflow[:], scalar=0.0, in1=in_relu[:], op0=ALU.max, op1=ALU.subtract
-            )
-            weighted = ring4.tile([P, BANK], F32, name="weighted")
-            nc.vector.scalar_tensor_tensor(
-                out=weighted[:], in0=minus_h[:], scalar=-1.0, in1=wgs_sb[:, 0:BANK], op0=ALU.mult, op1=ALU.mult
-            )
-            return weighted
-
-        def subtract(out_relu, in_relu, slot):
+        def subtract(in_relu, out_relu, slot):
             h = keep.tile([P, BANK], F32, name="h", tag=slot, align_bytes=64)
             nc.gpsimd.tensor_tensor(out=h[:], in0=in_relu[:], in1=out_relu[:], op=ALU.subtract)
             return h
 
-        def weigh(g, h):
-            weighted = ring4.tile([P, BANK], F32, name="weighted")
-            nc.gpsimd.tensor_tensor(out=weighted[:], in0=h[:], in1=wgs_sb[:, g * BANK : (g + 1) * BANK], op=ALU.mult)
+        def net_flow(blocks, m, half, slot, in_bank, out_bank):
+            out_relu = relu(outflow(m, half, out_bank), f"out_relu{m % PAIR}")
+            in_relu = relu(inflow(blocks, m, half, in_bank), f"in_relu{m % PAIR}")
+            return subtract(in_relu, out_relu, slot)
+
+        def weigh(half, h, slot):
+            weighted = keep.tile([P, BANK], F32, name="weighted", tag=slot, align_bytes=64)
+            nc.gpsimd.tensor_tensor(out=weighted[:], in0=h[:], in1=wgs_sb[:, entries(half)], op=ALU.mult)
             return weighted
 
-        def window(m, g):
-            return pages[m % PAGES][:].indirect(place[:, g * LIST_COLS : (g + 1) * LIST_COLS])
+        def window(m, half):
+            return pages[m % PAGES][:].indirect(place[:, entries(half, 16)])
 
-        def scatter(m, g, weighted):
-            nc.vector.tensor_copy(out=window(m, g), in_=weighted[:])
+        def scatter(m, half, weighted):
+            nc.vector.tensor_copy(out=window(m, half), in_=weighted[:])
 
-        def weigh_and_scatter(m, g, h):
-            nc.vector.tensor_tensor(out=window(m, g), in0=h[:], in1=wgs_sb[:, g * BANK : (g + 1) * BANK], op=ALU.mult)
+        def weigh_and_scatter(m, half, h):
+            nc.vector.tensor_tensor(out=window(m, half), in0=h[:], in1=wgs_sb[:, entries(half)], op=ALU.mult)
 
         def warm_up(passes, slot, win_w, win_s):
             bank = psum.tile([P, BANK], F32, name="warm_bank", tag=slot)
@@ -237,11 +226,11 @@ def tile_list_junction_flow_forecast_kernel(
                     is_transpose=True,
                 )
 
-        def turn_old(m):
+        def open_banks(m, source):
             banks = []
             for c in range(CHUNKS):
                 bank = psum.tile([P, BLOCKS, P], F32, name="z_bank", tag=f"bank{(0 if m == last else 4) + c}")
-                turn(bank, old_sb[m], c, True)
+                turn(bank, source, c, True)
                 banks.append(bank)
             return banks
 
@@ -251,9 +240,9 @@ def tile_list_junction_flow_forecast_kernel(
             else:
                 nc.scalar.copy(out=dst, in_=src)
 
-        def add_page(m, banks):
+        def close_banks(m, banks, source):
             for c in range(CHUNKS):
-                turn(banks[c], pages[m % PAGES], c, False)
+                turn(banks[c], source, c, False)
                 dst = z_t[c][:].rearrange("t q (u m j e) -> t q u m j e", u=2, m=ROW_TILES, e=2)[:, :, :, m, :, :]
                 src = banks[c][:].rearrange("t q (j u e) -> t q u j e", u=2, e=2)
                 copy_out(m == last and c % 2 == 0, dst, src)
@@ -278,70 +267,106 @@ def tile_list_junction_flow_forecast_kernel(
             nc.vector.quantize_mx(out=z_w[:].bitcast(FP8X4), scales=z_s[:], in_=grouped[:])
             return z_w, z_s
 
-        def forecast(c, wfree_w, wfree_s, z_w, z_s):
-            for n in range(OUT_TILES):
-                free = psum.tile([P, BANK], F32, name="free", tag=f"bank{bank_pairs[n][0]}")
-                jam = psum.tile([P, BANK], F32, name="jam", tag=f"bank{bank_pairs[n][1]}")
-                nc.tensor.matmul_mx(
-                    out=free[:],
-                    lhsT=wfree_w[:, n * P : (n + 1) * P].bitcast(FP8X4),
-                    lhsT_scale=wfree_s[:, n * P : (n + 1) * P],
-                    rhs=z_w[:].bitcast(FP8X4),
-                    rhs_scale=z_s[:],
-                    start=True,
-                    stop=True,
-                )
-                nc.tensor.matmul_mx(
-                    out=jam[:],
-                    lhsT=wjam_w[:, 0, n * P // 2 : (n + 1) * P // 2].bitcast(U8).bitcast(FP4X4),
-                    lhsT_scale=wjam_s[:, 0, n * P // 4 : (n + 1) * P // 4].bitcast(U8),
-                    rhs=z_w[:].bitcast(FP8X4),
-                    rhs_scale=z_s[:],
-                    start=True,
-                    stop=True,
-                )
-                free_sb = ring4.tile([P, BANK], F32, name="free_sb")
-                result = ring8.tile([P, BANK], F32, name="result")
-                rows = out[n * P : (n + 1) * P, c * BANK : (c + 1) * BANK]
-                piece = BANK // 2 if c * OUT_TILES + n == STEPS - 1 else BANK
-                for start in range(0, BANK, piece):
-                    cols = slice(start, start + piece)
-                    nc.scalar.copy(out=free_sb[:, cols], in_=free[:, cols])
-                    nc.vector.tensor_tensor(out=result[:, cols], in0=jam[:, cols], in1=free_sb[:, cols], op=ALU.max)
-                    nc.sync.dma_start(out=rows[:, cols], in_=result[:, cols])
+        def forecast(step, n, c, wfree_w, wfree_s, z_w, z_s, result, piece):
+            free = psum.tile([P, BANK], F32, name="free", tag=f"bank{bank_pairs[step % 4][0]}")
+            jam = psum.tile([P, BANK], F32, name="jam", tag=f"bank{bank_pairs[step % 4][1]}")
+            nc.tensor.matmul_mx(
+                out=free[:],
+                lhsT=wfree_w[:, n * P : (n + 1) * P].bitcast(FP8X4),
+                lhsT_scale=wfree_s[:, n * P : (n + 1) * P],
+                rhs=z_w[:].bitcast(FP8X4),
+                rhs_scale=z_s[:],
+                start=True,
+                stop=True,
+            )
+            nc.tensor.matmul_mx(
+                out=jam[:],
+                lhsT=wjam_w[:, 0, n * P // 2 : (n + 1) * P // 2].bitcast(U8).bitcast(FP4X4),
+                lhsT_scale=wjam_s[:, 0, n * P // 4 : (n + 1) * P // 4].bitcast(U8),
+                rhs=z_w[:].bitcast(FP8X4),
+                rhs_scale=z_s[:],
+                start=True,
+                stop=True,
+            )
+            free_sb = ring4.tile([P, BANK], F32, name="free_sb")
+            for start in range(0, BANK, piece):
+                cols = slice(start, start + piece)
+                nc.scalar.copy(out=free_sb[:, cols], in_=free[:, cols])
+                nc.vector.tensor_tensor(out=result[:, cols], in0=jam[:, cols], in1=free_sb[:, cols], op=ALU.max)
+                if piece < BANK:
+                    nc.sync.dma_start(
+                        out=out[n * P : (n + 1) * P, c * BANK + start : c * BANK + start + piece], in_=result[:, cols]
+                    )
 
-        first = (first_codes[:], first_scales[:])
-        weighted00 = first_weighted(*first, "h_a")
-        weighted10 = weigh(0, subtract(*relus(1, 0, *first, 1), "h_a"))
-        scatter(0, 0, weighted00)
-        weighted01 = weigh(1, subtract(*relus(0, 1, *first, 1), "h_b"))
-        scatter(1, 0, weighted10)
+        out_relu = {}
+        for m in range(PAIR):
+            out_relu[m, HALF_0] = relu(outflow(m, HALF_0, 2 * m), f"early_out{m}")
+        h00 = keep.tile([P, BANK], F32, name="h00", tag="h_a", align_bytes=64)
+        weighted00 = keep.tile([P, BANK], F32, name="weighted00", tag="weighted0", align_bytes=64)
+        for quarter, bank in ((QUARTER_0, 1), (QUARTER_1, 3)):
+            nc.vector.scalar_tensor_tensor(
+                out=h00[:, entries(quarter)],
+                in0=inflow(first, 0, quarter, bank)[:],
+                scalar=0.0,
+                in1=out_relu[0, HALF_0][:, entries(quarter)],
+                op0=ALU.max,
+                op1=ALU.subtract,
+            )
+        for quarter in (QUARTER_0, QUARTER_1):
+            cols = entries(quarter)
+            nc.vector.tensor_tensor(out=weighted00[:, cols], in0=h00[:, cols], in1=wgs_sb[:, cols], op=ALU.mult)
+        h10 = subtract(relu(inflow(first, 1, HALF_0, 5), "in_relu1"), out_relu[1, HALF_0], "h_a")
+        weighted10 = weigh(HALF_0, h10, "weighted1")
+        scatter(0, HALF_0, weighted00)
+        h01 = net_flow(first, 0, HALF_1, "h_b", 3, 1)
+        h11 = net_flow(first, 1, HALF_1, "h_d", 1, 5)
         rest_grouped = group_rest("h_c")
-        relus11 = relus(1, 1, *first, 3)
-        rest = quantize_weight(rest_grouped, "h_b")
-        scatter(0, 1, weighted01)
-        weighted11 = weigh(1, subtract(*relus11, "h_c"))
-        h20 = subtract(*relus(2, 0, *rest, 1), "h_a")
-        h30 = subtract(*relus(3, 0, *rest, 3), "h_c")
-        weighted20 = weigh(0, h20)
+        weighted01 = weigh(HALF_1, h01, "win_rest")
+        scatter(1, HALF_0, weighted10)
+        rest_codes = quantize_weight(rest_grouped, "h_b")
+        rest = {}
+        for m in range(PAIR, ROW_TILES):
+            for a in range(PASSES):
+                cols = slice(((m - PAIR) * PASSES + a) * P, ((m - PAIR) * PASSES + a + 1) * P)
+                rest[m, a] = (rest_codes[0][:, cols], rest_codes[1][:, cols])
+        scatter(0, HALF_1, weighted01)
+        weighted11 = weigh(HALF_1, h11, "h_c")
         wfree_grouped = group_wfree()
-        scatter(1, 1, weighted11)
-        scatter(2, 0, weighted20)
-        weighted30 = weigh(0, h30)
-        h21 = subtract(*relus(2, 1, *rest, 1), "h_a")
-        add_page(0, turn_old(0))
-        scatter(3, 0, weighted30)
-        h31 = subtract(*relus(3, 1, *rest, 3), "h_c")
-        add_page(1, turn_old(1))
-        last_banks = turn_old(last)
-        warm_up(WARM_EARLY, "bank7", *rest)
-        weigh_and_scatter(2, 1, h21)
-        weigh_and_scatter(3, 1, h31)
-        wfree_codes = quantize_weight(wfree_grouped, "in_relu1")
-        add_page(2, turn_old(2))
-        warm_up(WARM_LATE, "bank4", *rest)
-        add_page(last, last_banks)
+        weighted20 = weigh(HALF_0, net_flow(rest, 2, HALF_0, "h_a", 0, 3), "weighted0")
+        h30 = net_flow(rest, 3, HALF_0, "h_a", 2, 1)
+        scatter(1, HALF_1, weighted11)
+        scatter(2, HALF_0, weighted20)
+        weighted30 = weigh(HALF_0, h30, "win_rest")
+        h21 = net_flow(rest, 2, HALF_1, "h_a", 0, 3)
+        close_banks(0, open_banks(0, pages[0]), old_sb[0])
+        scatter(3, HALF_0, weighted30)
+        h31 = net_flow(rest, 3, HALF_1, "h_d", 2, 1)
+        close_banks(1, open_banks(1, old_sb[1]), pages[1])
+        last_banks = open_banks(last, old_sb[last])
+        warm_up(WARM_EARLY, "bank7", *rest_codes)
+        weigh_and_scatter(2, HALF_1, h21)
+        weigh_and_scatter(3, HALF_1, h31)
+        wfree_codes = quantize_weight(wfree_grouped, "h_d")
+        close_banks(2, open_banks(2, old_sb[2]), pages[2])
+        warm_up(WARM_LATE, "bank4", *rest_codes)
+        close_banks(last, last_banks, pages[0])
 
         quantized = [turn_back_and_quantize(c) for c in range(CHUNKS)]
-        for c in range(CHUNKS):
-            forecast(c, *wfree_codes, *quantized[c])
+        result_slots = ("tab_w1", "win_first0", "win_first1", "wfree_raw", "old0", "old1", "old2", "old3")
+        step = 0
+        for first_chunk in range(0, CHUNKS, 2):
+            for n in range(OUT_TILES):
+                result = keep.tile([P, 2, BANK], F32, name="result", tag=result_slots[step // 2])
+                alone = step == 0 or step == STEPS - 2
+                for j in range(2):
+                    c = first_chunk + j
+                    piece = BANK // 2 if step == STEPS - 1 else BANK
+                    forecast(step, n, c, *wfree_codes, *quantized[c], result[:, j], piece)
+                    if alone and piece == BANK:
+                        nc.sync.dma_start(out=out[n * P : (n + 1) * P, c * BANK : (c + 1) * BANK], in_=result[:, j])
+                    step = step + 1
+                if not alone:
+                    nc.sync.dma_start(
+                        out=out[n * P : (n + 1) * P, first_chunk * BANK : (first_chunk + 2) * BANK],
+                        in_=result[:].rearrange("p j c -> p (j c)"),
+                    )

@@ -54,23 +54,29 @@ def tile_list_junction_flow_forecast_kernel(
 
         tab_s = keep.tile([P, T // 4], I32, name="tab_s")
         tab_w = [keep.tile([P, T], I32, name=f"tab_w{a}", tag=f"tab_w{a}") for a in range(PASSES)]
-        wout_w = keep.tile([P, PASSES, H // 2], I32, name="wout_w", align_bytes=64)
-        wout_s = keep.tile([P, PASSES, H // 4], I32, name="wout_s", align_bytes=64)
-        wjam_w = keep.tile([P, 1, N // 2], I32, name="wjam_w", align_bytes=64)
-        wjam_s = keep.tile([P, 1, N // 4], I32, name="wjam_s", align_bytes=64)
+        wout_w = keep.tile([P, PASSES, H // 2], I32, name="wout_w", align_bytes=256)
+        wout_s = keep.tile([P, PASSES, H // 4], I32, name="wout_s", align_bytes=256)
+        wjam_w = keep.tile([P, 1, N // 2], I32, name="wjam_w", align_bytes=256)
+        wjam_s = keep.tile([P, 1, N // 4], I32, name="wjam_s", align_bytes=256)
         win_first = [keep.tile([P, PACK, PAIR * P], F32, name=f"win_first{a}") for a in range(PASSES)]
-        win_rest = keep.tile([P, PASSES, PACK, PAIR * P], F32, name="win_rest", align_bytes=64)
+        win_rest = keep.tile([P, PASSES, PACK, PAIR * P], F32, name="win_rest", align_bytes=256)
         wgs_sb = keep.tile([P, S], F32, name="wgs_sb")
         old_sb = [keep.tile([P, T2], F32, name=f"old{m}") for m in range(ROW_TILES)]
         wfree_raw = keep.tile([P, PACK, N], F32, name="wfree_raw")
         ident = keep.tile([P, P], F32, name="ident")
-        v_w = [keep.tile([P, S], U32, name=f"v_w{a}", align_bytes=64) for a in range(PASSES)]
+        v_w = [keep.tile([P, S], U32, name=f"v_w{a}", align_bytes=256) for a in range(PASSES)]
         picked_s = keep.tile([P, S], U8, name="picked_s")
-        v_s = keep.tile([P, PASSES, S // 4], I32, name="v_s", align_bytes=64)
+        v_s = keep.tile([P, PASSES, S // 4], I32, name="v_s", align_bytes=256)
 
 
         def entries(piece, per=1):
             return slice(piece[0] // per, (piece[0] + piece[1]) // per)
+
+        def copy_out(on_vector, dst, src):
+            if on_vector:
+                nc.vector.tensor_copy(out=dst, in_=src)
+            else:
+                nc.scalar.copy(out=dst, in_=src)
 
         for plane in (wout_s[:], tab_s[32:64], tab_s[64:P], v_s[:]):
             nc.vector.memset(plane, 0)
@@ -116,33 +122,41 @@ def tile_list_junction_flow_forecast_kernel(
             )
         first = {}
         for a in range(PASSES):
-            grouped = [keep.tile([P, P, PACK], BF16, name=f"first_grouped{a}{m}", align_bytes=64) for m in range(PAIR)]
+            grouped = [keep.tile([P, P, PACK], BF16, name=f"first_grouped{a}{m}", align_bytes=256) for m in range(PAIR)]
             for m in range(PAIR):
-                nc.vector.tensor_copy(
-                    out=grouped[m][:], in_=win_first[a][:, :, m * P : (m + 1) * P].rearrange("p i c -> p c i")
+                copy_out(
+                    a > 0,
+                    grouped[m][:].rearrange("p (c n) i -> p c i n", n=PACK),
+                    win_first[a][:, :, m * P : (m + 1) * P].rearrange("p i (c n) -> p c i n", n=PACK),
                 )
             for m in range(PAIR):
-                codes = keep.tile([P, P], U32, name=f"first_codes{a}{m}", align_bytes=64)
-                scales = keep.tile([P, P], U8, name=f"first_scales{a}{m}", align_bytes=64)
+                codes = keep.tile([P, P], U32, name=f"first_codes{a}{m}", align_bytes=256)
+                scales = keep.tile([P, P], U8, name=f"first_scales{a}{m}", align_bytes=256)
                 nc.vector.quantize_mx(
                     out=codes[:].bitcast(FP8X4), scales=scales[:], in_=grouped[m][:].rearrange("p c i -> p (c i)")
                 )
                 first[m, a] = (codes[:], scales[:])
 
         def group_rest(slot):
-            grouped = keep.tile([P, PAIR, PASSES, P, PACK], BF16, name="rest_grouped", tag=slot, align_bytes=64)
+            grouped = keep.tile([P, PAIR, PASSES, P, PACK], BF16, name="rest_grouped", tag=slot, align_bytes=256)
             for a in range(PASSES):
-                nc.scalar.copy(out=grouped[:, :, a], in_=win_rest[:, a].rearrange("p i (m c) -> p m c i", m=PAIR))
+                nc.scalar.copy(
+                    out=grouped[:, :, a].rearrange("p m (c n) i -> p m c i n", n=PACK),
+                    in_=win_rest[:, a].rearrange("p i (m c n) -> p m c i n", m=PAIR, n=PACK),
+                )
             return grouped[:].rearrange("p m a c i -> p (m a c i)")
 
         def group_wfree():
-            grouped = keep.tile([P, N, PACK], BF16, name="wfree_grouped", align_bytes=64)
-            nc.scalar.copy(out=grouped[:], in_=wfree_raw[:].rearrange("p i c -> p c i"))
+            grouped = keep.tile([P, N, PACK], BF16, name="wfree_grouped", align_bytes=256)
+            nc.scalar.copy(
+                out=grouped[:].rearrange("p (c n) i -> p c i n", n=PACK),
+                in_=wfree_raw[:].rearrange("p i (c n) -> p c i n", n=PACK),
+            )
             return grouped[:].rearrange("p c i -> p (c i)")
 
         def quantize_weight(grouped, slot):
-            scales = keep.tile([P, BANK], U8, name="scales", tag=f"scales_{slot}", align_bytes=64)
-            codes = keep.tile([P, BANK], U32, name="codes", tag=slot, align_bytes=64)
+            scales = keep.tile([P, BANK], U8, name="scales", tag=f"scales_{slot}", align_bytes=256)
+            codes = keep.tile([P, BANK], U32, name="codes", tag=slot, align_bytes=256)
             nc.vector.quantize_mx(out=codes[:].bitcast(FP8X4), scales=scales[:], in_=grouped)
             return codes[:], scales[:]
 
@@ -174,22 +188,25 @@ def tile_list_junction_flow_forecast_kernel(
             return product("outflow", piece, bank, weights)
 
         def relu(bank, slot):
-            tile = keep.tile([P, BANK], F32, name="relu", tag=slot, align_bytes=64)
+            tile = keep.tile([P, BANK], F32, name="relu", tag=slot, align_bytes=256)
             nc.scalar.activation(out=tile[:], in_=bank[:], func=ACT.Relu)
             return tile
 
         def subtract(in_relu, out_relu, slot):
-            h = keep.tile([P, BANK], F32, name="h", tag=slot, align_bytes=64)
+            h = keep.tile([P, BANK], F32, name="h", tag=slot, align_bytes=256)
             nc.gpsimd.tensor_tensor(out=h[:], in0=in_relu[:], in1=out_relu[:], op=ALU.subtract)
             return h
 
-        def net_flow(blocks, m, half, slot, in_bank, out_bank):
+        def relus(blocks, m, half, in_bank, out_bank):
             out_relu = relu(outflow(m, half, out_bank), f"out_relu{m % PAIR}")
             in_relu = relu(inflow(blocks, m, half, in_bank), f"in_relu{m % PAIR}")
-            return subtract(in_relu, out_relu, slot)
+            return in_relu, out_relu
+
+        def net_flow(blocks, m, half, slot, in_bank, out_bank):
+            return subtract(*relus(blocks, m, half, in_bank, out_bank), slot)
 
         def weigh(half, h, slot):
-            weighted = keep.tile([P, BANK], F32, name="weighted", tag=slot, align_bytes=64)
+            weighted = keep.tile([P, BANK], F32, name="weighted", tag=slot, align_bytes=256)
             nc.gpsimd.tensor_tensor(out=weighted[:], in0=h[:], in1=wgs_sb[:, entries(half)], op=ALU.mult)
             return weighted
 
@@ -234,12 +251,6 @@ def tile_list_junction_flow_forecast_kernel(
                 banks.append(bank)
             return banks
 
-        def copy_out(on_vector, dst, src):
-            if on_vector:
-                nc.vector.tensor_copy(out=dst, in_=src)
-            else:
-                nc.scalar.copy(out=dst, in_=src)
-
         def close_banks(m, banks, source):
             for c in range(CHUNKS):
                 turn(banks[c], source, c, False)
@@ -251,7 +262,7 @@ def tile_list_junction_flow_forecast_kernel(
 
         def turn_back_and_quantize(c):
             pairs = z_t[c][:].rearrange("t q r -> t (q r)").bitcast(F32)
-            grouped = ring4.tile([P, BANK * PACK], BF16, name="z_grouped", align_bytes=64)
+            grouped = ring4.tile([P, BANK * PACK], BF16, name="z_grouped", align_bytes=256)
             grouped_pairs = grouped[:].bitcast(F32)
             for b in range(2):
                 bank = psum.tile([P, 2, 2, P], F32, name="pair_bank", tag=f"bank{bank_pairs[c][b]}")
@@ -262,8 +273,8 @@ def tile_list_junction_flow_forecast_kernel(
                 dst = grouped_pairs[:, b * BANK : (b + 1) * BANK].rearrange("p (q t u) -> p q t u", q=2, u=2)
                 src = bank[:].rearrange("p q u t -> p q t u")
                 copy_out(c < 2 and b == c, dst, src)
-            z_w = ring4.tile([P, BANK], U32, name="z_w", align_bytes=64)
-            z_s = ring4.tile([P, BANK], U8, name="z_s", align_bytes=64)
+            z_w = ring4.tile([P, BANK], U32, name="z_w", align_bytes=256)
+            z_s = ring4.tile([P, BANK], U8, name="z_s", align_bytes=256)
             nc.vector.quantize_mx(out=z_w[:].bitcast(FP8X4), scales=z_s[:], in_=grouped[:])
             return z_w, z_s
 
@@ -301,8 +312,8 @@ def tile_list_junction_flow_forecast_kernel(
         out_relu = {}
         for m in range(PAIR):
             out_relu[m, HALF_0] = relu(outflow(m, HALF_0, 2 * m), f"early_out{m}")
-        h00 = keep.tile([P, BANK], F32, name="h00", tag="h_a", align_bytes=64)
-        weighted00 = keep.tile([P, BANK], F32, name="weighted00", tag="weighted0", align_bytes=64)
+        h00 = keep.tile([P, BANK], F32, name="h00", tag="h_a", align_bytes=256)
+        weighted00 = keep.tile([P, BANK], F32, name="weighted00", tag="weighted0", align_bytes=256)
         for quarter, bank in ((QUARTER_0, 1), (QUARTER_1, 3)):
             nc.vector.scalar_tensor_tensor(
                 out=h00[:, entries(quarter)],
@@ -319,8 +330,8 @@ def tile_list_junction_flow_forecast_kernel(
         weighted10 = weigh(HALF_0, h10, "weighted1")
         scatter(0, HALF_0, weighted00)
         h01 = net_flow(first, 0, HALF_1, "h_b", 3, 1)
-        h11 = net_flow(first, 1, HALF_1, "h_d", 1, 5)
         rest_grouped = group_rest("h_c")
+        relus11 = relus(first, 1, HALF_1, 1, 5)
         weighted01 = weigh(HALF_1, h01, "win_rest")
         scatter(1, HALF_0, weighted10)
         rest_codes = quantize_weight(rest_grouped, "h_b")
@@ -330,7 +341,7 @@ def tile_list_junction_flow_forecast_kernel(
                 cols = slice(((m - PAIR) * PASSES + a) * P, ((m - PAIR) * PASSES + a + 1) * P)
                 rest[m, a] = (rest_codes[0][:, cols], rest_codes[1][:, cols])
         scatter(0, HALF_1, weighted01)
-        weighted11 = weigh(HALF_1, h11, "h_c")
+        weighted11 = weigh(HALF_1, subtract(*relus11, "h_c"), "h_d")
         wfree_grouped = group_wfree()
         weighted20 = weigh(HALF_0, net_flow(rest, 2, HALF_0, "h_a", 0, 3), "weighted0")
         h30 = net_flow(rest, 3, HALF_0, "h_a", 2, 1)
@@ -340,13 +351,13 @@ def tile_list_junction_flow_forecast_kernel(
         h21 = net_flow(rest, 2, HALF_1, "h_a", 0, 3)
         close_banks(0, open_banks(0, pages[0]), old_sb[0])
         scatter(3, HALF_0, weighted30)
-        h31 = net_flow(rest, 3, HALF_1, "h_d", 2, 1)
+        h31 = net_flow(rest, 3, HALF_1, "h_c", 2, 1)
         close_banks(1, open_banks(1, old_sb[1]), pages[1])
         last_banks = open_banks(last, old_sb[last])
         warm_up(WARM_EARLY, "bank7", *rest_codes)
         weigh_and_scatter(2, HALF_1, h21)
         weigh_and_scatter(3, HALF_1, h31)
-        wfree_codes = quantize_weight(wfree_grouped, "h_d")
+        wfree_codes = quantize_weight(wfree_grouped, "h_c")
         close_banks(2, open_banks(2, old_sb[2]), pages[2])
         warm_up(WARM_LATE, "bank4", *rest_codes)
         close_banks(last, last_banks, pages[0])

@@ -58,7 +58,7 @@ def tile_list_junction_flow_forecast_kernel(
         wout_s = keep.tile([P, PASSES, H // 4], I32, name="wout_s", align_bytes=256)
         wjam_w = keep.tile([P, 1, N // 2], I32, name="wjam_w", align_bytes=256)
         wjam_s = keep.tile([P, 1, N // 4], I32, name="wjam_s", align_bytes=256)
-        win_first = [keep.tile([P, PACK, PAIR * P], F32, name=f"win_first{a}") for a in range(PASSES)]
+        win_first = [keep.tile([P, PACK, PAIR * P], F32, name=f"win_first{a}", align_bytes=256) for a in range(PASSES)]
         win_rest = keep.tile([P, PASSES, PACK, PAIR * P], F32, name="win_rest", align_bytes=256)
         wgs_sb = keep.tile([P, S], F32, name="wgs_sb")
         old_sb = [keep.tile([P, T2], F32, name=f"old{m}") for m in range(ROW_TILES)]
@@ -86,12 +86,16 @@ def tile_list_junction_flow_forecast_kernel(
         words = tab_words.rearrange("a p t i -> a p (t i)").bitcast(I32)
         win_rows = win.rearrange("(a p i) c -> a p i c", a=PASSES, i=PACK)
         nc.sync.dma_start(pick[:], offs)
+        nc.sync.dma_start(place[:], offs2)
         nc.sync.dma_start(out=tab_s[0:32, :], in_=tab_scales.bitcast(I32).rearrange("a q w -> (a q) w"))
         nc.vector.tensor_copy(out=picked_s[:], in_=tab_s[:].bitcast(U8).indirect(pick[:]))
         for a in range(PASSES):
             for half in range(2):
                 cols = slice(half * T // 2, (half + 1) * T // 2)
-                nc.sync.dma_start(out=tab_w[a][:, cols], in_=words[a][:, cols])
+                if a == PASSES - 1:
+                    nc.sync.dma_start(out=tab_w[a][:, cols], in_=words[a][:, cols])
+                elif half == 0:
+                    nc.sync.dma_start(out=tab_w[a][:], in_=words[a])
                 if a == PASSES - 1:
                     for r in range(4):
                         rows = picked_s[:].bitcast(I32)[16 * half + r : 16 * half + 16 : 4, :]
@@ -104,10 +108,10 @@ def tile_list_junction_flow_forecast_kernel(
         nc.sync.dma_start(out=wout_w[:], in_=wout_words.bitcast(I32).rearrange("a p w -> p a w"))
         for a in range(PASSES):
             nc.sync.dma_start(out=win_first[a][:], in_=win_rows[a, :, :, 0 : PAIR * P])
-        nc.sync.dma_start(out=wgs_sb[:], in_=wgs)
-        nc.sync.dma_start(place[:], offs2)
+        nc.sync.dma_start(out=wgs_sb[:, 0:BANK], in_=wgs[:, 0:BANK])
         for a in range(PASSES):
             nc.sync.dma_start(out=win_rest[:, a], in_=win_rows[a, :, :, PAIR * P : H])
+        nc.sync.dma_start(out=wgs_sb[:, BANK:S], in_=wgs[:, BANK:S])
         nc.sync.dma_start(out=wfree_raw[:], in_=wfree.rearrange("(p i) n -> p i n", i=PACK))
         for m in range(ROW_TILES):
             nc.sync.dma_start(out=old_sb[m][:], in_=old[m * P : (m + 1) * P, :])
@@ -125,7 +129,7 @@ def tile_list_junction_flow_forecast_kernel(
             grouped = [keep.tile([P, P, PACK], BF16, name=f"first_grouped{a}{m}", align_bytes=256) for m in range(PAIR)]
             for m in range(PAIR):
                 copy_out(
-                    a > 0,
+                    a > 0 and m == 0,
                     grouped[m][:].rearrange("p (c n) i -> p c i n", n=PACK),
                     win_first[a][:, :, m * P : (m + 1) * P].rearrange("p i (c n) -> p c i n", n=PACK),
                 )
@@ -311,7 +315,7 @@ def tile_list_junction_flow_forecast_kernel(
 
         out_relu = {}
         for m in range(PAIR):
-            out_relu[m, HALF_0] = relu(outflow(m, HALF_0, 2 * m), f"early_out{m}")
+            out_relu[m, HALF_0] = relu(outflow(m, HALF_0, 2 * m), f"win_first{m}")
         h00 = keep.tile([P, BANK], F32, name="h00", tag="h_a", align_bytes=256)
         weighted00 = keep.tile([P, BANK], F32, name="weighted00", tag="weighted0", align_bytes=256)
         for quarter, bank in ((QUARTER_0, 1), (QUARTER_1, 3)):
@@ -363,15 +367,15 @@ def tile_list_junction_flow_forecast_kernel(
         close_banks(last, last_banks, pages[0])
 
         quantized = [turn_back_and_quantize(c) for c in range(CHUNKS)]
-        result_slots = ("tab_w1", "win_first0", "win_first1", "wfree_raw", "old0", "old1", "old2", "old3")
+        result_slots = ("tab_w1", "picked_s", "spare_result", "wfree_raw", "old0", "old1", "old2", "old3")
         step = 0
         for first_chunk in range(0, CHUNKS, 2):
             for n in range(OUT_TILES):
                 result = keep.tile([P, 2, BANK], F32, name="result", tag=result_slots[step // 2])
-                alone = step == 0 or step == STEPS - 2
+                alone = step == 0
                 for j in range(2):
                     c = first_chunk + j
-                    piece = BANK // 2 if step == STEPS - 1 else BANK
+                    piece = BANK
                     forecast(step, n, c, *wfree_codes, *quantized[c], result[:, j], piece)
                     if alone and piece == BANK:
                         nc.sync.dma_start(out=out[n * P : (n + 1) * P, c * BANK : (c + 1) * BANK], in_=result[:, j])

@@ -66,6 +66,8 @@ def tile_list_junction_flow_forecast_kernel(
         ident = keep.tile([P, P], F32, name="ident")
         v_w = [keep.tile([P, S], U32, name=f"v_w{a}", align_bytes=256) for a in range(PASSES)]
         picked_s = keep.tile([P, S], U8, name="picked_s")
+        paired_s = keep.tile([64, PASSES, S // 4], I32, name="paired_s")
+        wout_rows_s = keep.tile([4, PASSES * 4, H // 4], I32, name="wout_rows_s")
         v_s = keep.tile([P, PASSES, S // 4], I32, name="v_s", align_bytes=256)
 
 
@@ -78,28 +80,25 @@ def tile_list_junction_flow_forecast_kernel(
             else:
                 nc.scalar.copy(out=dst, in_=src)
 
-        for plane in (wout_s[:], tab_s[32:64], tab_s[64:P], v_s[:]):
+        for plane in (tab_s[:], wout_s[:], v_s[:]):
             nc.vector.memset(plane, 0)
-        load_scale_rows(nc.scalar, wout_s, wout_scales)
         make_identity(nc, ident[:])
 
         words = tab_words.rearrange("a p t i -> a p (t i)").bitcast(I32)
         win_rows = win.rearrange("(a p i) c -> a p i c", a=PASSES, i=PACK)
         nc.sync.dma_start(pick[:], offs)
-        nc.sync.dma_start(place[:], offs2)
-        nc.sync.dma_start(out=tab_s[0:32, :], in_=tab_scales.bitcast(I32).rearrange("a q w -> (a q) w"))
+        nc.sync.dma_start(out=wout_rows_s[:], in_=wout_scales.bitcast(I32).rearrange("a (q r) w -> r (a q) w", r=4))
+        nc.sync.dma_start(out=tab_s[0:P:4, :], in_=tab_scales.bitcast(I32).rearrange("a j w -> (a j) w"))
         nc.vector.tensor_copy(out=picked_s[:], in_=tab_s[:].bitcast(U8).indirect(pick[:]))
         for a in range(PASSES):
-            for half in range(2):
-                cols = slice(half * T // 2, (half + 1) * T // 2)
-                if a == PASSES - 1:
-                    nc.sync.dma_start(out=tab_w[a][:, cols], in_=words[a][:, cols])
-                elif half == 0:
-                    nc.sync.dma_start(out=tab_w[a][:], in_=words[a])
-                if a == PASSES - 1:
-                    for r in range(4):
-                        rows = picked_s[:].bitcast(I32)[16 * half + r : 16 * half + 16 : 4, :]
-                        nc.sync.dma_start(out=v_s[r:P:32, half, :], in_=rows)
+            nc.vector.tensor_copy(out=paired_s[:, a, :], in_=picked_s[:].bitcast(I32)[64 * a : 64 * a + 64, :])
+        for q in range(4):
+            nc.vector.tensor_copy(out=wout_s[32 * q : 32 * q + 4], in_=wout_rows_s[:, q : PASSES * 4 : 4, :])
+        nc.sync.dma_start(out=tab_w[0][:], in_=words[0])
+        nc.sync.dma_start(out=tab_w[1][:, 0 : T // 2], in_=words[1][:, 0 : T // 2])
+        for r in range(4):
+            nc.sync.dma_start(out=v_s[r:P:32], in_=paired_s[4 * r : 64 : 16])
+        nc.sync.dma_start(out=tab_w[1][:, T // 2 : T], in_=words[1][:, T // 2 : T])
         nc.vector.tensor_copy(out=v_w[0][:], in_=tab_w[0][:].bitcast(U32).indirect(pick[:]))
         nc.vector.memset(wjam_s[:], 0)
         pages = [keep.tile([P, T2], F32, name="page", tag=slot) for slot in ("page0", "tab_s", "tab_w0")]
@@ -109,6 +108,7 @@ def tile_list_junction_flow_forecast_kernel(
         for a in range(PASSES):
             nc.sync.dma_start(out=win_first[a][:], in_=win_rows[a, :, :, 0 : PAIR * P])
         nc.sync.dma_start(out=wgs_sb[:, 0:BANK], in_=wgs[:, 0:BANK])
+        nc.sync.dma_start(place[:], offs2)
         for a in range(PASSES):
             nc.sync.dma_start(out=win_rest[:, a], in_=win_rows[a, :, :, PAIR * P : H])
         nc.sync.dma_start(out=wgs_sb[:, BANK:S], in_=wgs[:, BANK:S])

@@ -30,6 +30,7 @@ CHUNKS = T2 // BANK
 BLOCKS = BANK // P
 OUT_TILES = N // P
 STEPS = OUT_TILES * CHUNKS
+WORDS_CUT = 5 * T // 8
 WARM_EARLY, WARM_LATE = 4, 2
 
 
@@ -54,7 +55,7 @@ def tile_list_junction_flow_forecast_kernel(
 
         tab_s = keep.tile([P, T // 4], I32, name="tab_s")
         tab_w = [keep.tile([P, T], I32, name=f"tab_w{a}", tag=f"tab_w{a}") for a in range(PASSES)]
-        wout_w = keep.tile([P, PASSES, H // 2], I32, name="wout_w", align_bytes=256)
+        wout_w = [keep.tile([P, PASSES, H // 4], I32, name=f"wout_w{pair}", align_bytes=256) for pair in range(2)]
         wout_s = keep.tile([P, PASSES, H // 4], I32, name="wout_s", align_bytes=256)
         wjam_w = keep.tile([P, 1, N // 2], I32, name="wjam_w", align_bytes=256)
         wjam_s = keep.tile([P, 1, N // 4], I32, name="wjam_s", align_bytes=256)
@@ -86,6 +87,7 @@ def tile_list_junction_flow_forecast_kernel(
 
         words = tab_words.rearrange("a p t i -> a p (t i)").bitcast(I32)
         win_rows = win.rearrange("(a p i) c -> a p i c", a=PASSES, i=PACK)
+        nc.sync.dma_start(out=tab_w[0][:, 0 : T // 4], in_=words[0][:, 0 : T // 4])
         nc.sync.dma_start(pick[:], offs)
         nc.sync.dma_start(out=wout_rows_s[:], in_=wout_scales.bitcast(I32).rearrange("a (q r) w -> r (a q) w", r=4))
         nc.sync.dma_start(out=tab_s[0:P:4, :], in_=tab_scales.bitcast(I32).rearrange("a j w -> (a j) w"))
@@ -94,17 +96,18 @@ def tile_list_junction_flow_forecast_kernel(
             nc.vector.tensor_copy(out=paired_s[:, a, :], in_=picked_s[:].bitcast(I32)[64 * a : 64 * a + 64, :])
         for q in range(4):
             nc.vector.tensor_copy(out=wout_s[32 * q : 32 * q + 4], in_=wout_rows_s[:, q : PASSES * 4 : 4, :])
-        nc.sync.dma_start(out=tab_w[0][:], in_=words[0])
-        nc.sync.dma_start(out=tab_w[1][:, 0 : T // 2], in_=words[1][:, 0 : T // 2])
+        nc.sync.dma_start(out=tab_w[0][:, T // 4 : T], in_=words[0][:, T // 4 : T])
+        nc.sync.dma_start(out=tab_w[1][:, 0:WORDS_CUT], in_=words[1][:, 0:WORDS_CUT])
         for r in range(4):
             nc.sync.dma_start(out=v_s[r:P:32], in_=paired_s[4 * r : 64 : 16])
-        nc.sync.dma_start(out=tab_w[1][:, T // 2 : T], in_=words[1][:, T // 2 : T])
+        nc.sync.dma_start(out=tab_w[1][:, WORDS_CUT:T], in_=words[1][:, WORDS_CUT:T])
         nc.vector.tensor_copy(out=v_w[0][:], in_=tab_w[0][:].bitcast(U32).indirect(pick[:]))
         nc.vector.memset(wjam_s[:], 0)
         pages = [keep.tile([P, T2], F32, name="page", tag=slot) for slot in ("page0", "tab_s", "tab_w0")]
         for page in pages:
             nc.vector.memset(page[:], 0.0)
-        nc.sync.dma_start(out=wout_w[:], in_=wout_words.bitcast(I32).rearrange("a p w -> p a w"))
+        wout_rows = wout_words.bitcast(I32).rearrange("a p w -> p a w")
+        nc.sync.dma_start(out=wout_w[0][:], in_=wout_rows[:, :, 0 : H // 4])
         for a in range(PASSES):
             nc.sync.dma_start(out=win_first[a][:], in_=win_rows[a, :, :, 0 : PAIR * P])
         nc.sync.dma_start(out=wgs_sb[:, 0:BANK], in_=wgs[:, 0:BANK])
@@ -112,6 +115,7 @@ def tile_list_junction_flow_forecast_kernel(
         for a in range(PASSES):
             nc.sync.dma_start(out=win_rest[:, a], in_=win_rows[a, :, :, PAIR * P : H])
         nc.sync.dma_start(out=wgs_sb[:, BANK:S], in_=wgs[:, BANK:S])
+        nc.sync.dma_start(out=wout_w[1][:], in_=wout_rows[:, :, H // 4 : H // 2])
         nc.sync.dma_start(out=wfree_raw[:], in_=wfree.rearrange("(p i) n -> p i n", i=PACK))
         for m in range(ROW_TILES):
             nc.sync.dma_start(out=old_sb[m][:], in_=old[m * P : (m + 1) * P, :])
@@ -184,7 +188,7 @@ def tile_list_junction_flow_forecast_kernel(
         def outflow(m, piece, bank):
             weights = [
                 (
-                    wout_w[:, a, m * P // 2 : (m + 1) * P // 2].bitcast(U8).bitcast(FP4X4),
+                    wout_w[m // PAIR][:, a, m % PAIR * P // 2 : (m % PAIR + 1) * P // 2].bitcast(U8).bitcast(FP4X4),
                     wout_s[:, a, m * P // 4 : (m + 1) * P // 4].bitcast(U8),
                 )
                 for a in range(PASSES)

@@ -68,7 +68,6 @@ def tile_list_junction_flow_forecast_kernel(
         v_w = [keep.tile([P, S], U32, name=f"v_w{a}", align_bytes=256) for a in range(PASSES)]
         picked_s = keep.tile([P, S], U8, name="picked_s")
         paired_s = keep.tile([64, PASSES, S // 4], I32, name="paired_s")
-        wout_rows_s = keep.tile([4, PASSES * 4, H // 4], I32, name="wout_rows_s")
         v_s = keep.tile([P, PASSES, S // 4], I32, name="v_s", align_bytes=256)
 
 
@@ -89,13 +88,11 @@ def tile_list_junction_flow_forecast_kernel(
         win_rows = win.rearrange("(a p i) c -> a p i c", a=PASSES, i=PACK)
         nc.sync.dma_start(out=tab_w[0][:, 0 : T // 4], in_=words[0][:, 0 : T // 4])
         nc.sync.dma_start(pick[:], offs)
-        nc.sync.dma_start(out=wout_rows_s[:], in_=wout_scales.bitcast(I32).rearrange("a (q r) w -> r (a q) w", r=4))
         nc.sync.dma_start(out=tab_s[0:P:4, :], in_=tab_scales.bitcast(I32).rearrange("a j w -> (a j) w"))
         nc.vector.tensor_copy(out=picked_s[:], in_=tab_s[:].bitcast(U8).indirect(pick[:]))
         for a in range(PASSES):
             nc.vector.tensor_copy(out=paired_s[:, a, :], in_=picked_s[:].bitcast(I32)[64 * a : 64 * a + 64, :])
-        for q in range(4):
-            nc.vector.tensor_copy(out=wout_s[32 * q : 32 * q + 4], in_=wout_rows_s[:, q : PASSES * 4 : 4, :])
+        load_scale_rows(nc.sync, wout_s, wout_scales)
         nc.sync.dma_start(out=tab_w[0][:, T // 4 : T], in_=words[0][:, T // 4 : T])
         nc.sync.dma_start(out=tab_w[1][:, 0:WORDS_CUT], in_=words[1][:, 0:WORDS_CUT])
         for r in range(4):
@@ -103,7 +100,7 @@ def tile_list_junction_flow_forecast_kernel(
         nc.sync.dma_start(out=tab_w[1][:, WORDS_CUT:T], in_=words[1][:, WORDS_CUT:T])
         nc.vector.tensor_copy(out=v_w[0][:], in_=tab_w[0][:].bitcast(U32).indirect(pick[:]))
         nc.vector.memset(wjam_s[:], 0)
-        pages = [keep.tile([P, T2], F32, name="page", tag=slot) for slot in ("page0", "tab_s", "tab_w0")]
+        pages = [keep.tile([P, T2], F32, name="page", tag=slot) for slot in ("page0", "page1", "tab_s")]
         for page in pages:
             nc.vector.memset(page[:], 0.0)
         wout_rows = wout_words.bitcast(I32).rearrange("a p w -> p a w")

@@ -31,7 +31,7 @@ BLOCKS = BANK // P
 OUT_TILES = N // P
 STEPS = OUT_TILES * CHUNKS
 WORDS_CUT = 5 * T // 8
-WARM_EARLY, WARM_LATE = 4, 2
+WARM_EARLY = 3
 
 
 def tile_list_junction_flow_forecast_kernel(
@@ -237,12 +237,12 @@ def tile_list_junction_flow_forecast_kernel(
                     stop=True,
                 )
 
-        def turn(bank, source, c, opens):
+        def turn(bank, source, c, opens, identity):
             for q in range(BLOCKS):
                 nc.tensor.matmul(
                     bank[:, q, :],
                     source[:, c * BANK + q * P : c * BANK + (q + 1) * P],
-                    ident[:],
+                    identity[:],
                     start=(opens and q == 0),
                     stop=(not opens and q == BLOCKS - 1),
                     is_transpose=True,
@@ -252,13 +252,13 @@ def tile_list_junction_flow_forecast_kernel(
             banks = []
             for c in range(CHUNKS):
                 bank = psum.tile([P, BLOCKS, P], F32, name="z_bank", tag=f"bank{(0 if m == last else 4) + c}")
-                turn(bank, source, c, True)
+                turn(bank, source, c, True, ident)
                 banks.append(bank)
             return banks
 
-        def close_banks(m, banks, source):
+        def close_banks(m, banks, source, identity=ident):
             for c in range(CHUNKS):
-                turn(banks[c], source, c, False)
+                turn(banks[c], source, c, False, identity)
                 dst = z_t[c][:].rearrange("t q (u m j e) -> t q u m j e", u=2, m=ROW_TILES, e=2)[:, :, :, m, :, :]
                 src = banks[c][:].rearrange("t q (j u e) -> t q u j e", u=2, e=2)
                 copy_out(m == last and c % 2 == 0, dst, src)
@@ -364,8 +364,11 @@ def tile_list_junction_flow_forecast_kernel(
         weigh_and_scatter(3, HALF_1, h31)
         wfree_codes = quantize_weight(wfree_grouped, "h_c")
         close_banks(2, open_banks(2, old_sb[2]), pages[2])
-        warm_up(WARM_LATE, "bank4", *rest_codes)
-        close_banks(last, last_banks, pages[0])
+        for c in range(1, CHUNKS):
+            warm_up(1, f"bank{4 + c}", *rest_codes)
+        last_ident = keep.tile([P, P], F32, name="last_ident", tag="tab_s")
+        nc.scalar.copy(out=last_ident[:], in_=ident[:])
+        close_banks(last, last_banks, pages[0], last_ident)
 
         quantized = [turn_back_and_quantize(c) for c in range(CHUNKS)]
         result_slots = ("tab_w1", "picked_s", "spare_result", "wfree_raw", "old0", "old1", "old2", "old3")

@@ -256,12 +256,15 @@ def tile_list_junction_flow_forecast_kernel(
                 banks.append(bank)
             return banks
 
+        def round_out(m, banks, c):
+            dst = z_t[c][:].rearrange("t q (u m j e) -> t q u m j e", u=2, m=ROW_TILES, e=2)[:, :, :, m, :, :]
+            src = banks[c][:].rearrange("t q (j u e) -> t q u j e", u=2, e=2)
+            copy_out(m == last and c % 2 == 0, dst, src)
+
         def close_banks(m, banks, source, identity=ident):
             for c in range(CHUNKS):
                 turn(banks[c], source, c, False, identity)
-                dst = z_t[c][:].rearrange("t q (u m j e) -> t q u m j e", u=2, m=ROW_TILES, e=2)[:, :, :, m, :, :]
-                src = banks[c][:].rearrange("t q (j u e) -> t q u j e", u=2, e=2)
-                copy_out(m == last and c % 2 == 0, dst, src)
+                round_out(m, banks, c)
 
         bank_pairs = ((4, 5), (6, 7), (0, 1), (2, 3))
 
@@ -363,11 +366,15 @@ def tile_list_junction_flow_forecast_kernel(
         weigh_and_scatter(2, HALF_1, h21)
         weigh_and_scatter(3, HALF_1, h31)
         wfree_codes = quantize_weight(wfree_grouped, "h_c")
-        close_banks(2, open_banks(2, old_sb[2]), pages[2])
-        for c in range(1, CHUNKS):
+        banks2 = open_banks(2, old_sb[2])
+        for c in range(CHUNKS):
+            turn(banks2[c], pages[2], c, False, ident)
+        for c in range(CHUNKS - 1):
+            round_out(2, banks2, c)
             warm_up(1, f"bank{4 + c}", *rest_codes)
         last_ident = keep.tile([P, P], F32, name="last_ident", tag="tab_s")
         nc.scalar.copy(out=last_ident[:], in_=ident[:])
+        round_out(2, banks2, CHUNKS - 1)
         close_banks(last, last_banks, pages[0], last_ident)
 
         quantized = [turn_back_and_quantize(c) for c in range(CHUNKS)]

from contextlib import ExitStack

import concourse.mybir as mybir
from concourse.masks import make_identity

K, T, S, H, T2, N = 1024, 4096, 1024, 512, 2048, 512
FLOPS = 2 * (2 * K * H * S + 2 * H * N * T2)

F32 = mybir.dt.float32
BF16 = mybir.dt.bfloat16
I32 = mybir.dt.int32
U32 = mybir.dt.uint32
U16 = mybir.dt.uint16
U8 = mybir.dt.uint8
FP8X4 = mybir.dt.float8_e4m3fn_x4
FP4X4 = mybir.dt.float4_e2m1fn_x4
ALU = mybir.AluOpType
ACT = mybir.ActivationFunctionType

P = 128
PACK = 4
PASSES = K // (P * PACK)
BANK = 512
QUARTER = BANK // 2
HALF_0, HALF_1, QUARTER_0, QUARTER_1 = (0, BANK), (BANK, BANK), (0, QUARTER), (QUARTER, QUARTER)
ROW_TILES = H // P
PAIR = 2
PAGES = 3
CHUNKS = T2 // BANK
BLOCKS = BANK // P
OUT_TILES = N // P
STEPS = OUT_TILES * CHUNKS
WORDS_CUT = 5 * T // 8
WARM_EARLY = 3


def tile_list_junction_flow_forecast_kernel(
    tc, tab_words, tab_scales, offs, offs2, win, wout_words, wout_scales, wgs, old, wfree, wjam_words, wjam_scales, out
):
    nc = tc.nc
    with ExitStack() as ctx:
        lists = ctx.enter_context(tc.tile_pool(name="lists", bufs=1))
        keep = ctx.enter_context(tc.tile_pool(name="keep", bufs=1))
        ring4 = ctx.enter_context(tc.tile_pool(name="ring4", bufs=4))
        psum = ctx.enter_context(tc.psum_pool(name="psum", bufs=1))

        def load_scale_rows(queue, plane, dram):
            rows = dram.bitcast(I32).rearrange("a (q r) w -> r q a w", r=4)
            for r in range(4):
                queue.dma_start(out=plane[r:P:32, :, :], in_=rows[r])

        last = ROW_TILES - 1
        pick = lists.tile([P, S // 16], U16, name="pick")
        place = lists.tile([P, S // 16], U16, name="place")

        tab_s = keep.tile([P, T // 4], I32, name="tab_s")
        tab_w = [keep.tile([P, T], I32, name=f"tab_w{a}", tag=f"tab_w{a}") for a in range(PASSES)]
        wout_w = [keep.tile([P, PASSES, H // 4], I32, name=f"wout_w{pair}", align_bytes=256) for pair in range(2)]
        wout_s = keep.tile([P, PASSES, H // 4], I32, name="wout_s", align_bytes=256)
        wjam_w = keep.tile([P, 1, N // 2], I32, name="wjam_w", align_bytes=256)
        wjam_s = keep.tile([P, 1, N // 4], I32, name="wjam_s", align_bytes=256)
        win_first = [keep.tile([P, PACK, PAIR * P], F32, name=f"win_first{a}", align_bytes=256) for a in range(PASSES)]
        win_rest = keep.tile([P, PASSES, PACK, PAIR * P], F32, name="win_rest", align_bytes=256)
        wgs_sb = keep.tile([P, S], F32, name="wgs_sb")
        old_sb = [keep.tile([P, T2], F32, name=f"old{m}") for m in range(ROW_TILES)]
        wfree_raw = keep.tile([P, PACK, N], F32, name="wfree_raw")
        ident = keep.tile([P, P], F32, name="ident")
        v_w = [keep.tile([P, S], U32, name=f"v_w{a}", align_bytes=256) for a in range(PASSES)]
        picked_s = keep.tile([P, S], U8, name="picked_s")
        paired_s = keep.tile([64, PASSES, S // 4], I32, name="paired_s")
        v_s = keep.tile([P, PASSES, S // 4], I32, name="v_s", align_bytes=256)


        def entries(piece, per=1):
            return slice(piece[0] // per, (piece[0] + piece[1]) // per)

        def copy_out(on_vector, dst, src):
            if on_vector:
                nc.vector.tensor_copy(out=dst, in_=src)
            else:
                nc.scalar.copy(out=dst, in_=src)

        for plane in (tab_s[:], wout_s[:], v_s[:]):
            nc.vector.memset(plane, 0)
        make_identity(nc, ident[:])

        words = tab_words.rearrange("a p t i -> a p (t i)").bitcast(I32)
        win_rows = win.rearrange("(a p i) c -> a p i c", a=PASSES, i=PACK)
        nc.sync.dma_start(out=tab_w[0][:, 0 : T // 4], in_=words[0][:, 0 : T // 4])
        nc.sync.dma_start(pick[:], offs)
        nc.sync.dma_start(out=tab_s[0:P:4, :], in_=tab_scales.bitcast(I32).rearrange("a j w -> (a j) w"))
        nc.vector.tensor_copy(out=picked_s[:], in_=tab_s[:].bitcast(U8).indirect(pick[:]))
        for a in range(PASSES):
            nc.vector.tensor_copy(out=paired_s[:, a, :], in_=picked_s[:].bitcast(I32)[64 * a : 64 * a + 64, :])
        load_scale_rows(nc.sync, wout_s, wout_scales)
        nc.sync.dma_start(out=tab_w[0][:, T // 4 : T], in_=words[0][:, T // 4 : T])
        nc.sync.dma_start(out=tab_w[1][:, 0:WORDS_CUT], in_=words[1][:, 0:WORDS_CUT])
        for r in range(4):
            nc.sync.dma_start(out=v_s[r:P:32], in_=paired_s[4 * r : 64 : 16])
        nc.sync.dma_start(out=tab_w[1][:, WORDS_CUT:T], in_=words[1][:, WORDS_CUT:T])
        nc.vector.tensor_copy(out=v_w[0][:], in_=tab_w[0][:].bitcast(U32).indirect(pick[:]))
        nc.vector.memset(wjam_s[:], 0)
        pages = [keep.tile([P, T2], F32, name="page", tag=slot) for slot in ("page0", "page1", "tab_s")]
        for page in pages:
            nc.vector.memset(page[:], 0.0)
        wout_rows = wout_words.bitcast(I32).rearrange("a p w -> p a w")
        nc.sync.dma_start(out=wout_w[0][:], in_=wout_rows[:, :, 0 : H // 4])
        for a in range(PASSES):
            nc.sync.dma_start(out=win_first[a][:], in_=win_rows[a, :, :, 0 : PAIR * P])
        nc.sync.dma_start(out=wgs_sb[:, 0:BANK], in_=wgs[:, 0:BANK])
        nc.sync.dma_start(place[:], offs2)
        for a in range(PASSES):
            nc.sync.dma_start(out=win_rest[:, a], in_=win_rows[a, :, :, PAIR * P : H])
        nc.sync.dma_start(out=wgs_sb[:, BANK:S], in_=wgs[:, BANK:S])
        nc.sync.dma_start(out=wout_w[1][:], in_=wout_rows[:, :, H // 4 : H // 2])
        nc.sync.dma_start(out=wfree_raw[:], in_=wfree.rearrange("(p i) n -> p i n", i=PACK))
        for m in range(ROW_TILES):
            nc.sync.dma_start(out=old_sb[m][:], in_=old[m * P : (m + 1) * P, :])
        nc.sync.dma_start(out=wjam_w[:], in_=wjam_words.bitcast(I32).rearrange("a p w -> p a w"))
        load_scale_rows(nc.sync, wjam_s, wjam_scales)

        z_t = [keep.tile([P, BLOCKS, H], BF16, name=f"z_t{c}") for c in range(CHUNKS)]

        for half in (HALF_0, HALF_1):
            nc.vector.tensor_copy(
                out=v_w[1][:, entries(half)], in_=tab_w[1][:].bitcast(U32).indirect(pick[:, entries(half, 16)])
            )
        first = {}
        for a in range(PASSES):
            grouped = [keep.tile([P, P, PACK], BF16, name=f"first_grouped{a}{m}", align_bytes=256) for m in range(PAIR)]
            for m in range(PAIR):
                copy_out(
                    a > 0 and m == 0,
                    grouped[m][:].rearrange("p (c n) i -> p c i n", n=PACK),
                    win_first[a][:, :, m * P : (m + 1) * P].rearrange("p i (c n) -> p c i n", n=PACK),
                )
            for m in range(PAIR):
                codes = keep.tile([P, P], U32, name=f"first_codes{a}{m}", align_bytes=256)
                scales = keep.tile([P, P], U8, name=f"first_scales{a}{m}", align_bytes=256)
                nc.vector.quantize_mx(
                    out=codes[:].bitcast(FP8X4), scales=scales[:], in_=grouped[m][:].rearrange("p c i -> p (c i)")
                )
                first[m, a] = (codes[:], scales[:])

        def group_rest(slot):
            grouped = keep.tile([P, PAIR, PASSES, P, PACK], BF16, name="rest_grouped", tag=slot, align_bytes=256)
            for a in range(PASSES):
                nc.scalar.copy(
                    out=grouped[:, :, a].rearrange("p m (c n) i -> p m c i n", n=PACK),
                    in_=win_rest[:, a].rearrange("p i (m c n) -> p m c i n", m=PAIR, n=PACK),
                )
            return grouped[:].rearrange("p m a c i -> p (m a c i)")

        def group_wfree():
            grouped = keep.tile([P, N, PACK], BF16, name="wfree_grouped", align_bytes=256)
            nc.scalar.copy(
                out=grouped[:].rearrange("p (c n) i -> p c i n", n=PACK),
                in_=wfree_raw[:].rearrange("p i (c n) -> p c i n", n=PACK),
            )
            return grouped[:].rearrange("p c i -> p (c i)")

        def quantize_weight(grouped, slot):
            scales = keep.tile([P, BANK], U8, name="scales", tag=f"scales_{slot}", align_bytes=256)
            codes = keep.tile([P, BANK], U32, name="codes", tag=slot, align_bytes=256)
            nc.vector.quantize_mx(out=codes[:].bitcast(FP8X4), scales=scales[:], in_=grouped)
            return codes[:], scales[:]

        def product(name, piece, bank, weights):
            total = psum.tile([P, piece[1]], F32, name=name, tag=f"bank{bank}")
            for a in range(PASSES):
                nc.tensor.matmul_mx(
                    out=total[:],
                    lhsT=weights[a][0],
                    lhsT_scale=weights[a][1],
                    rhs=v_w[a][:, entries(piece)].bitcast(FP8X4),
                    rhs_scale=v_s[:, a, entries(piece, 4)].bitcast(U8),
                    start=(a == 0),
                    stop=(a == PASSES - 1),
                )
            return total

        def inflow(blocks, m, piece, bank):
            return product("inflow", piece, bank, [(blocks[m, a][0].bitcast(FP8X4), blocks[m, a][1]) for a in range(PASSES)])

        def outflow(m, piece, bank):
            weights = [
                (
                    wout_w[m // PAIR][:, a, m % PAIR * P // 2 : (m % PAIR + 1) * P // 2].bitcast(U8).bitcast(FP4X4),
                    wout_s[:, a, m * P // 4 : (m + 1) * P // 4].bitcast(U8),
                )
                for a in range(PASSES)
            ]
            return product("outflow", piece, bank, weights)

        def relu(bank, slot):
            tile = keep.tile([P, BANK], F32, name="relu", tag=slot, align_bytes=256)
            nc.scalar.activation(out=tile[:], in_=bank[:], func=ACT.Relu)
            return tile

        def subtract(in_relu, out_relu, slot):
            h = keep.tile([P, BANK], F32, name="h", tag=slot, align_bytes=256)
            nc.gpsimd.tensor_tensor(out=h[:], in0=in_relu[:], in1=out_relu[:], op=ALU.subtract)
            return h

        def relus(blocks, m, half, in_bank, out_bank):
            out_relu = relu(outflow(m, half, out_bank), f"out_relu{m % PAIR}")
            in_relu = relu(inflow(blocks, m, half, in_bank), f"in_relu{m % PAIR}")
            return in_relu, out_relu

        def net_flow(blocks, m, half, slot, in_bank, out_bank):
            return subtract(*relus(blocks, m, half, in_bank, out_bank), slot)

        def weigh(half, h, slot):
            weighted = keep.tile([P, BANK], F32, name="weighted", tag=slot, align_bytes=256)
            nc.gpsimd.tensor_tensor(out=weighted[:], in0=h[:], in1=wgs_sb[:, entries(half)], op=ALU.mult)
            return weighted

        def window(m, half):
            return pages[m % PAGES][:].indirect(place[:, entries(half, 16)])

        def scatter(m, half, weighted):
            nc.vector.tensor_copy(out=window(m, half), in_=weighted[:])

        def weigh_and_scatter(m, half, h):
            nc.vector.tensor_tensor(out=window(m, half), in0=h[:], in1=wgs_sb[:, entries(half)], op=ALU.mult)

        def warm_up(passes, slot, win_w, win_s):
            bank = psum.tile([P, BANK], F32, name="warm_bank", tag=slot)
            for n in range(passes):
                nc.tensor.matmul_mx(
                    out=bank[:],
                    lhsT=win_w[:, n * P : (n + 1) * P].bitcast(FP8X4),
                    lhsT_scale=win_s[:, n * P : (n + 1) * P],
                    rhs=v_w[0][:, 0:BANK].bitcast(FP8X4),
                    rhs_scale=v_s[:, 0, 0 : BANK // 4].bitcast(U8),
                    start=True,
                    stop=True,
                )

        def turn(bank, source, c, opens, identity):
            for q in range(BLOCKS):
                nc.tensor.matmul(
                    bank[:, q, :],
                    source[:, c * BANK + q * P : c * BANK + (q + 1) * P],
                    identity[:],
                    start=(opens and q == 0),
                    stop=(not opens and q == BLOCKS - 1),
                    is_transpose=True,
                )

        def open_banks(m, source):
            banks = []
            for c in range(CHUNKS):
                bank = psum.tile([P, BLOCKS, P], F32, name="z_bank", tag=f"bank{(0 if m == last else 4) + c}")
                turn(bank, source, c, True, ident)
                banks.append(bank)
            return banks

        def round_out(m, banks, c):
            dst = z_t[c][:].rearrange("t q (u m j e) -> t q u m j e", u=2, m=ROW_TILES, e=2)[:, :, :, m, :, :]
            src = banks[c][:].rearrange("t q (j u e) -> t q u j e", u=2, e=2)
            copy_out(m == last and c % 2 == 0, dst, src)

        def close_banks(m, banks, source, identity=ident):
            for c in range(CHUNKS):
                turn(banks[c], source, c, False, identity)
                round_out(m, banks, c)

        bank_pairs = ((4, 5), (6, 7), (0, 1), (2, 3))

        def turn_back_and_quantize(c):
            pairs = z_t[c][:].rearrange("t q r -> t (q r)").bitcast(F32)
            grouped = ring4.tile([P, BANK * PACK], BF16, name="z_grouped", align_bytes=256)
            grouped_pairs = grouped[:].bitcast(F32)
            for b in range(2):
                bank = psum.tile([P, 2, 2, P], F32, name="pair_bank", tag=f"bank{bank_pairs[c][b]}")
                for q in range(2):
                    for u in range(2):
                        start = ((2 * b + q) * 2 + u) * P
                        nc.tensor.transpose(bank[:, q, u, :], pairs[:, start : start + P], ident[:])
                dst = grouped_pairs[:, b * BANK : (b + 1) * BANK].rearrange("p (q t u) -> p q t u", q=2, u=2)
                src = bank[:].rearrange("p q u t -> p q t u")
                copy_out(c < 2 and b == c, dst, src)
            z_w = ring4.tile([P, BANK], U32, name="z_w", align_bytes=256)
            z_s = ring4.tile([P, BANK], U8, name="z_s", align_bytes=256)
            nc.vector.quantize_mx(out=z_w[:].bitcast(FP8X4), scales=z_s[:], in_=grouped[:])
            return z_w, z_s

        def forecast(step, n, c, wfree_w, wfree_s, z_w, z_s, result, piece):
            free = psum.tile([P, BANK], F32, name="free", tag=f"bank{bank_pairs[step % 4][0]}")
            jam = psum.tile([P, BANK], F32, name="jam", tag=f"bank{bank_pairs[step % 4][1]}")
            nc.tensor.matmul_mx(
                out=free[:],
                lhsT=wfree_w[:, n * P : (n + 1) * P].bitcast(FP8X4),
                lhsT_scale=wfree_s[:, n * P : (n + 1) * P],
                rhs=z_w[:].bitcast(FP8X4),
                rhs_scale=z_s[:],
                start=True,
                stop=True,
            )
            nc.tensor.matmul_mx(
                out=jam[:],
                lhsT=wjam_w[:, 0, n * P // 2 : (n + 1) * P // 2].bitcast(U8).bitcast(FP4X4),
                lhsT_scale=wjam_s[:, 0, n * P // 4 : (n + 1) * P // 4].bitcast(U8),
                rhs=z_w[:].bitcast(FP8X4),
                rhs_scale=z_s[:],
                start=True,
                stop=True,
            )
            free_sb = ring4.tile([P, BANK], F32, name="free_sb")
            for start in range(0, BANK, piece):
                cols = slice(start, start + piece)
                nc.scalar.copy(out=free_sb[:, cols], in_=free[:, cols])
                nc.vector.tensor_tensor(out=result[:, cols], in0=jam[:, cols], in1=free_sb[:, cols], op=ALU.max)
                if piece < BANK:
                    nc.sync.dma_start(
                        out=out[n * P : (n + 1) * P, c * BANK + start : c * BANK + start + piece], in_=result[:, cols]
                    )

        out_relu = {}
        for m in range(PAIR):
            out_relu[m, HALF_0] = relu(outflow(m, HALF_0, 2 * m), f"win_first{m}")
        h00 = keep.tile([P, BANK], F32, name="h00", tag="h_a", align_bytes=256)
        weighted00 = keep.tile([P, BANK], F32, name="weighted00", tag="weighted0", align_bytes=256)
        for quarter, bank in ((QUARTER_0, 1), (QUARTER_1, 3)):
            nc.vector.scalar_tensor_tensor(
                out=h00[:, entries(quarter)],
                in0=inflow(first, 0, quarter, bank)[:],
                scalar=0.0,
                in1=out_relu[0, HALF_0][:, entries(quarter)],
                op0=ALU.max,
                op1=ALU.subtract,
            )
        for quarter in (QUARTER_0, QUARTER_1):
            cols = entries(quarter)
            nc.vector.tensor_tensor(out=weighted00[:, cols], in0=h00[:, cols], in1=wgs_sb[:, cols], op=ALU.mult)
        h10 = subtract(relu(inflow(first, 1, HALF_0, 5), "in_relu1"), out_relu[1, HALF_0], "h_a")
        weighted10 = weigh(HALF_0, h10, "weighted1")
        scatter(0, HALF_0, weighted00)
        h01 = net_flow(first, 0, HALF_1, "h_b", 3, 1)
        rest_grouped = group_rest("h_c")
        relus11 = relus(first, 1, HALF_1, 1, 5)
        weighted01 = weigh(HALF_1, h01, "win_rest")
        scatter(1, HALF_0, weighted10)
        rest_codes = quantize_weight(rest_grouped, "h_b")
        rest = {}
        for m in range(PAIR, ROW_TILES):
            for a in range(PASSES):
                cols = slice(((m - PAIR) * PASSES + a) * P, ((m - PAIR) * PASSES + a + 1) * P)
                rest[m, a] = (rest_codes[0][:, cols], rest_codes[1][:, cols])
        scatter(0, HALF_1, weighted01)
        weighted11 = weigh(HALF_1, subtract(*relus11, "h_c"), "h_d")
        wfree_grouped = group_wfree()
        weighted20 = weigh(HALF_0, net_flow(rest, 2, HALF_0, "h_a", 0, 3), "weighted0")
        h30 = net_flow(rest, 3, HALF_0, "h_a", 2, 1)
        scatter(1, HALF_1, weighted11)
        scatter(2, HALF_0, weighted20)
        weighted30 = weigh(HALF_0, h30, "win_rest")
        h21 = net_flow(rest, 2, HALF_1, "h_a", 0, 3)
        close_banks(0, open_banks(0, pages[0]), old_sb[0])
        scatter(3, HALF_0, weighted30)
        h31 = net_flow(rest, 3, HALF_1, "h_c", 2, 1)
        close_banks(1, open_banks(1, old_sb[1]), pages[1])
        last_banks = open_banks(last, old_sb[last])
        warm_up(WARM_EARLY, "bank7", *rest_codes)
        weigh_and_scatter(2, HALF_1, h21)
        weigh_and_scatter(3, HALF_1, h31)
        wfree_codes = quantize_weight(wfree_grouped, "h_c")
        banks2 = open_banks(2, old_sb[2])
        for c in range(CHUNKS):
            turn(banks2[c], pages[2], c, False, ident)
        for c in range(CHUNKS - 1):
            round_out(2, banks2, c)
            warm_up(1, f"bank{4 + c}", *rest_codes)
        last_ident = keep.tile([P, P], F32, name="last_ident", tag="tab_s")
        nc.scalar.copy(out=last_ident[:], in_=ident[:])
        round_out(2, banks2, CHUNKS - 1)
        close_banks(last, last_banks, pages[0], last_ident)

        quantized = [turn_back_and_quantize(c) for c in range(CHUNKS)]
        result_slots = ("tab_w1", "picked_s", "spare_result", "wfree_raw", "old0", "old1", "old2", "old3")
        step = 0
        for first_chunk in range(0, CHUNKS, 2):
            for n in range(OUT_TILES):
                result = keep.tile([P, 2, BANK], F32, name="result", tag=result_slots[step // 2])
                alone = step == 0
                for j in range(2):
                    c = first_chunk + j
                    piece = BANK
                    forecast(step, n, c, *wfree_codes, *quantized[c], result[:, j], piece)
                    if alone and piece == BANK:
                        nc.sync.dma_start(out=out[n * P : (n + 1) * P, c * BANK : (c + 1) * BANK], in_=result[:, j])
                    step = step + 1
                if not alone:
                    nc.sync.dma_start(
                        out=out[n * P : (n + 1) * P, first_chunk * BANK : (first_chunk + 2) * BANK],
                        in_=result[:].rearrange("p j c -> p (j c)"),
                    )
